import numpy as np
import ml_dtypes


def mxq(x, axis, fmt="e4m3"):
    dtype, down = {"e4m3": (ml_dtypes.float8_e4m3fn, 7), "e5m2": (ml_dtypes.float8_e5m2, 14)}[fmt]
    v = np.moveaxis(np.asarray(x, np.float32).astype(ml_dtypes.bfloat16).astype(np.float64), axis, -1)
    blocks = v.reshape(v.shape[:-1] + (-1, 32))
    amax = np.abs(blocks).max(-1, keepdims=True)
    byte = np.maximum(np.where(amax > 0, np.frexp(amax)[1] - 1 + 127, 0) - down, 1)
    scale = np.exp2(byte - 127.0)
    codes = (blocks / scale).astype(np.float32).astype(dtype).astype(np.float64)
    return np.moveaxis((codes * scale).reshape(v.shape), -1, axis)


WIDE = False


def mx_kscale(k):
    if not WIDE:
        return np.ones(k)
    levels = np.array([10, -10, 5, -5, 0])
    if k % 512:
        return np.exp2(np.random.permutation(np.resize(levels, k // 32))).repeat(32)
    a = np.empty((k // 512, 16))
    for p in range(k // 512):
        a[p, :8] = np.random.permutation(np.resize(levels, 8))
        for g in range(8):
            far = levels[np.abs(levels - a[p, g]) >= 10]
            a[p, g + 8] = far[np.random.randint(len(far))]
    return np.exp2(a.ravel()).repeat(32)


def f64(x):
    return np.asarray(x).astype(np.float64)


def striped(idx):
    return np.tile(idx.reshape(-1, 16).T, (8, 1)).astype(np.uint16)


def unstriped(offs):
    return offs[:16].T.reshape(-1).astype(np.int64)


E2M1 = np.array([0.0, 0.5, 1.0, 1.5, 2.0, 3.0, 4.0, 6.0, -0.0, -0.5, -1.0, -1.5, -2.0, -3.0, -4.0, -6.0])


def pack_weight(w, fmt):
    k, n = w.shape
    w = f64(np.asarray(w, np.float32).astype(ml_dtypes.bfloat16)).reshape(k // 32, 32, n)
    amax = np.abs(w).max(1)
    if fmt == "e4m3":
        byte = np.frexp(amax)[1] - 1 + 127 - 7
    else:
        mant, ex = np.frexp(amax / 6.0)
        byte = np.where(mant > 0.5, ex, ex - 1) + 127
    byte = np.clip(np.where(amax > 0, byte, 1), 1, 254)
    scaled = (w * np.exp2(127.0 - byte)[:, None, :]).reshape(k, n).astype(np.float32)
    by_word = np.ascontiguousarray(scaled.reshape(k // 512, 128, 4, n).transpose(0, 1, 3, 2))
    if fmt == "e4m3":
        words = by_word.astype(ml_dtypes.float8_e4m3fn).view(np.uint8)
    else:
        c = by_word.astype(ml_dtypes.float4_e2m1fn).view(np.uint8) & 0xF
        words = (c[..., 0::2] | (c[..., 1::2] << 4)).reshape(k // 512, 128, 2 * n)
    return np.ascontiguousarray(words), np.ascontiguousarray(byte.astype(np.uint8).reshape(k // 512, 16, n))


def unpack_weight(words, scales, fmt):
    g, _, n = scales.shape
    words = np.ascontiguousarray(words).reshape(g, 128, n, -1)
    if fmt == "e4m3":
        vals = words.view(ml_dtypes.float8_e4m3fn).astype(np.float64)
    else:
        nib = np.empty((g, 128, n, 4), np.uint8)
        nib[..., 0::2] = words & 0xF
        nib[..., 1::2] = words >> 4
        vals = E2M1[nib]
    vals = vals * np.repeat(np.exp2(scales.astype(np.float64) - 127.0), 8, axis=1)[..., None]
    return vals.transpose(0, 1, 3, 2).reshape(g * 512, n)


def gelu(v):
    return 0.5 * v * (1.0 + np.tanh(np.sqrt(2.0 / np.pi) * (v + 0.044715 * v**3)))


K, H, N, T, S, P = 1024, 1024, 512, 2048, 1024, 512

def setup_inputs():
    n = np.random.standard_normal
    s = mx_kscale(K)[:, None]
    u = mx_kscale(H)[:, None]
    tab_words, tab_scales = pack_weight(n((K, T)) * s, "e4m3")
    w1 = (2.0 * n((K, H)) / np.sqrt(K) / s).astype(np.float32)
    g = (np.exp(0.3 * n(H)) * u[:, 0]).astype(np.float32)
    w2_words, w2_scales = pack_weight(n((H, N)) / np.sqrt(H) / u, "e2m1")
    b2 = (0.3 * n(N)).astype(np.float32)
    offs = striped(np.random.permutation(T)[:S])
    pos1 = striped(np.random.permutation(S)[:P])
    pos2 = striped(np.random.permutation(S)[:P])
    return dict(tab_words=tab_words, tab_scales=tab_scales, w1=w1, g=g,
                w2_words=w2_words, w2_scales=w2_scales, b2=b2,
                offs=offs, pos1=pos1, pos2=pos2)

def reference(tab_words, tab_scales, w1, g, w2_words, w2_scales, b2, offs, pos1, pos2):
    v = unpack_weight(tab_words, tab_scales, "e4m3")[:, unstriped(offs)]
    w1q = mxq(f64(w1), 0, "e4m3")
    w2 = unpack_weight(w2_words, w2_scales, "e2m1")
    h = 1.0 / (1.0 + np.exp(-(w1q.T @ v)))
    a = h[:, unstriped(pos1)]
    b = h[:, unstriped(pos2)]
    z = f64(g)[:, None] * np.minimum(a, b)
    zq = mxq(z, 0, "e4m3")
    y = (w2.T @ zq) + f64(b2)[:, None]
    return np.exp(y)

@@ -1,0 +1,231 @@
+from contextlib import ExitStack
+
+import concourse.mybir as mybir
+
+K, H, N, T, S, J = 1024, 1024, 512, 2048, 1024, 512
+
+F32 = mybir.dt.float32
+BF16 = mybir.dt.bfloat16
+I32 = mybir.dt.int32
+U32 = mybir.dt.uint32
+U16 = mybir.dt.uint16
+U8 = mybir.dt.uint8
+FP8X4 = mybir.dt.float8_e4m3fn_x4
+FP4X4 = mybir.dt.float4_e2m1fn_x4
+ACT = mybir.ActivationFunctionType
+ALU = mybir.AluOpType
+
+P = 128
+PACK = 4
+PASS = P * PACK
+BANK = 512
+LIST_ROWS = 16
+CHUNKS = ((0, 256), (256, 128), (384, 128))
+N_MX = 128
+
+FLOPS = 2 * K * H * S + 2 * H * N * J
+
+
+def tile_list_join_sketch_cardinality_kernel(
+    tc, tab_words, tab_scales, w1, g, w2_words, w2_scales, b2, offs, pos1, pos2, out
+):
+    nc = tc.nc
+    with ExitStack() as ctx:
+        keep = ctx.enter_context(tc.tile_pool(name="keep", bufs=1))
+        psum = ctx.enter_context(tc.psum_pool(name="psum", bufs=1))
+
+        def tile(shape, dtype, name, tag=None):
+            return keep.tile(shape, dtype, name=name, tag=tag or name, align_bytes=64)
+
+        offs_sb = keep.tile([P, S // LIST_ROWS], U16, name="offs_sb")
+        pos_sb = [keep.tile([P, J // LIST_ROWS], U16, name="pos%d_sb" % side) for side in range(2)]
+        tab_w = [tile([P, T], I32, "tab_w%d" % a) for a in range(2)]
+        tab_s = tile([P, T // 4], I32, "tab_s")
+        w1_raw = {}
+        w2_w = tile([P, 2, 2 * N], U8, "w2_w")
+        w2_s = tile([P, 2, N], U8, "w2_s")
+        g_sb = tile([P, 2, PACK], F32, "g_sb")
+        b2_sb = tile([P, N // P], F32, "b2_sb")
+
+        nc.vector.memset(tab_s[:], 0)
+        nc.vector.memset(w2_s[:].bitcast(I32), 0)
+
+        def load_w1(b, a, c0, c1):
+            rows = w1[a * PASS : (a + 1) * PASS, b * PASS + c0 : b * PASS + c1]
+            w1_raw[b, a, c0] = tile([P, PACK, c1 - c0], F32, "w1_raw%d%d_%d" % (b, a, c0))
+            nc.sync.dma_start(out=w1_raw[b, a, c0][:], in_=rows.rearrange("(p j) c -> p j c", j=PACK))
+
+        nc.sync.dma_start(offs_sb[:], offs)
+        for q in range(4):
+            nc.scalar.dma_start(
+                out=tab_s[32 * q : 32 * q + 8, :], in_=tab_scales[:, 4 * q : 4 * q + 4, :].bitcast(I32)
+            )
+        nc.scalar.dma_start(out=g_sb[:], in_=g.rearrange("(b p t) -> p b t", b=2, t=PACK))
+        for a in range(2):
+            nc.sync.dma_start(out=tab_w[a][:], in_=tab_words[a].rearrange("p n t -> p (n t)").bitcast(I32))
+            load_w1(0, a, 0, PASS // 2)
+            load_w1(0, a, PASS // 2, PASS)
+        nc.sync.dma_start(pos_sb[0][:], pos1)
+        nc.sync.dma_start(pos_sb[1][:], pos2)
+        for a in range(2):
+            load_w1(1, a, 0, PASS)
+        nc.sync.dma_start(out=w2_w[:].bitcast(I32), in_=w2_words.rearrange("a p c -> p a c").bitcast(I32))
+        for q in range(4):
+            nc.sync.dma_start(
+                out=w2_s[32 * q : 32 * q + 4, :, :].bitcast(I32),
+                in_=w2_scales[:, 4 * q : 4 * q + 4, :].rearrange("a q c -> q a c").bitcast(I32),
+            )
+        with nc.allow_non_contiguous_dma(reason="one bias value a partition"):
+            nc.sync.dma_start(out=b2_sb[:], in_=b2.rearrange("(t p) -> p t", p=P))
+
+        g_width = [J, max(n for j0, n in CHUNKS)]
+        g_wide = {}
+
+        def spread_g(b, tag=None):
+            g_wide[b] = tile([P, PACK, g_width[b]], F32, "g_wide%d" % b, tag)
+            nc.scalar.activation(
+                g_wide[b][:], g_sb[:, b, :].unsqueeze(2).to_broadcast([P, PACK, g_width[b]]), ACT.Copy
+            )
+
+        v_w = [tile([P, S], U32, "v_w%d" % a) for a in range(2)]
+        v_s = tile([P, S], U8, "v_s")
+        nc.vector.tensor_copy(v_s[:], tab_s[:].bitcast(U8).indirect(offs_sb[:]))
+
+        def gather_words(a):
+            nc.vector.tensor_copy(v_w[a][:], tab_w[a][:].bitcast(U32).indirect(offs_sb[:]))
+
+        w1_bf, w1_w, w1_s = {}, {}, {}
+
+        def round_w1(copy, b, a, c0, c1, tag=None):
+            if c0 == 0:
+                w1_bf[b, a] = tile([P, PACK, P, PACK], BF16, "w1_bf%d%d" % (b, a), tag)
+            m = slice(c0 // PACK, c1 // PACK)
+            copy(
+                w1_bf[b, a][:, :, m, :].rearrange("p t m j -> p m t j"),
+                w1_raw[b, a, c0][:].rearrange("p j (m t) -> p m t j", t=PACK),
+            )
+
+        def quantize_w1(b, a, t0, t1):
+            width = (t1 - t0) * P
+            words = tile([P, width], U32, "w1_w%d%d%d" % (b, a, t0))
+            scales = tile([P, width], U8, "w1_s%d%d%d" % (b, a, t0))
+            nc.vector.quantize_mx(
+                out=words[:].bitcast(FP8X4),
+                scales=scales[:],
+                in_=w1_bf[b, a][:, t0:t1, :, :].rearrange("p t m j -> p (t m j)"),
+            )
+            for t in range(t0, t1):
+                cols = slice((t - t0) * P, (t - t0 + 1) * P)
+                w1_w[b, a, t], w1_s[b, a, t] = words[:, cols], scales[:, cols]
+
+        h = [[tile([P, S], F32, "h%d%d" % (b, t)) for t in range(PACK)] for b in range(2)]
+        acc = {}
+
+        def first_product(b, a, t):
+            for half in range(2):
+                if a == 0:
+                    acc[t, half] = psum.tile([P, BANK], F32, name="bank%d" % (2 * t + half))
+                cols = slice(half * BANK, (half + 1) * BANK)
+                nc.tensor.matmul_mx(
+                    out=acc[t, half][:],
+                    lhsT=w1_w[b, a, t].bitcast(FP8X4),
+                    lhsT_scale=w1_s[b, a, t],
+                    rhs=v_w[a][:, cols].bitcast(FP8X4),
+                    rhs_scale=v_s[4 * a : P, cols],
+                    start=(a == 0),
+                    stop=(a == 1),
+                )
+
+        def sigmoid(b, t):
+            for half in range(2):
+                nc.scalar.activation(h[b][t][:, half * BANK : (half + 1) * BANK], acc[t, half][:], ACT.Sigmoid)
+
+        z_w = [tile([P, J], U32, "z_w%d" % b) for b in range(2)]
+        z_s = [tile([P, J], U8, "z_s%d" % b) for b in range(2)]
+
+        def sides(b, j0, n):
+            return [tile([P, PACK, n], F32, "side%d_%d_%d" % (side, b, j0), "side%d_%d" % (side, b)) for side in range(2)]
+
+        def fetch(pair, b, t, j0, n):
+            for side in range(2):
+                entries = pos_sb[side][:, j0 // LIST_ROWS : (j0 + n) // LIST_ROWS]
+                nc.vector.tensor_tensor(
+                    pair[side][:, t, :], h[b][t][:].indirect(entries), g_wide[b][:, t, 0:n], ALU.mult
+                )
+
+        def overlap(pair, b, j0, n):
+            z_bf = tile([P, n, PACK], BF16, "z_bf%d_%d" % (b, j0))
+            left, right = (side[:].rearrange("p t (c i) -> p c t i", i=4) for side in pair)
+            nc.vector.tensor_tensor(z_bf[:].rearrange("p (c i) t -> p c t i", i=4), left, right, ALU.min)
+            return z_bf
+
+        def quantize_z(z_bf, b, j0, n):
+            nc.vector.quantize_mx(
+                out=z_w[b][:, j0 : j0 + n].bitcast(FP8X4),
+                scales=z_s[b][:, j0 : j0 + n],
+                in_=z_bf[:].rearrange("p j t -> p (j t)"),
+            )
+
+        def second_product(y, b, nt, j0, jj):
+            cols = slice(j0 + jj, j0 + jj + N_MX)
+            nc.tensor.matmul_mx(
+                out=y[:, jj : jj + N_MX],
+                lhsT=w2_w[:, b, 2 * nt * P : 2 * (nt + 1) * P].bitcast(FP4X4),
+                lhsT_scale=w2_s[:, b, nt * P : (nt + 1) * P],
+                rhs=z_w[b][:, cols].bitcast(FP8X4),
+                rhs_scale=z_s[b][:, cols],
+                start=(b == 0),
+                stop=(b == 1),
+            )
+
+        half = PASS // 2
+        spread_g(0)
+        gather_words(0)
+        round_w1(nc.scalar.copy, 0, 0, 0, half)
+        round_w1(nc.scalar.copy, 0, 0, half, PASS)
+        spread_g(1, "w1_raw00_%d" % half)
+        quantize_w1(0, 0, 0, PACK)
+        for t in range(PACK):
+            first_product(0, 0, t)
+        gather_words(1)
+        round_w1(nc.scalar.copy, 0, 1, 0, half)
+        round_w1(nc.vector.tensor_copy, 0, 1, half, PASS)
+        for t in range(PACK):
+            quantize_w1(0, 1, t, t + 1)
+            first_product(0, 1, t)
+
+        pair = sides(0, 0, J)
+        for t in range(PACK):
+            sigmoid(0, t)
+            fetch(pair, 0, t, 0, J)
+            if t >= 2:
+                a = t - 2
+                round_w1(nc.scalar.copy, 1, a, 0, PASS, "w1_w01%d" % t)
+                quantize_w1(1, a, 0, PACK)
+            if t == 2:
+                for tt in range(PACK - 1):
+                    first_product(1, 0, tt)
+        first_product(1, 0, PACK - 1)
+        for t in range(PACK):
+            first_product(1, 1, t)
+            sigmoid(1, t)
+        quantize_z(overlap(pair, 0, 0, J), 0, 0, J)
+
+        out_rows = out.rearrange("(t p) j -> p t j", p=P)
+        for c, (j0, n) in enumerate(CHUNKS):
+            pair = sides(1, j0, n)
+            y = [psum.tile([P, n], F32, name="bank%d" % (4 * (c % 2) + nt)) for nt in range(N // P)]
+            if n == N_MX:
+                for nt in range(N // P):
+                    second_product(y[nt], 0, nt, j0, 0)
+            for t in range(PACK):
+                fetch(pair, 1, t, j0, n)
+            quantize_z(overlap(pair, 1, j0, n), 1, j0, n)
+            res = tile([P, N // P, n], F32, "res%d" % c)
+            for nt in range(N // P):
+                for jj in range(0, n, N_MX):
+                    if n != N_MX:
+                        second_product(y[nt], 0, nt, j0, jj)
+                    second_product(y[nt], 1, nt, j0, jj)
+                nc.scalar.activation(res[:, nt, :], y[nt][:], ACT.Exp, bias=b2_sb[:, nt : nt + 1])
+            nc.sync.dma_start(out=out_rows[:, :, j0 : j0 + n], in_=res[:])

@@ -20,7 +20,7 @@ PACK = 4
 PASS = P * PACK
 BANK = 512
 LIST_ROWS = 16
-CHUNKS = ((0, 256), (256, 128), (384, 128))
+CHUNKS = ((0, 384), (384, 128))
 N_MX = 128
 
 FLOPS = 2 * K * H * S + 2 * H * N * J
@@ -47,13 +47,13 @@ def tile_list_join_sketch_cardinality_kernel(
         g_sb = tile([P, 2, PACK], F32, "g_sb")
         b2_sb = tile([P, N // P], F32, "b2_sb")
 
-        nc.vector.memset(tab_s[:], 0)
-        nc.vector.memset(w2_s[:].bitcast(I32), 0)
+        nc.gpsimd.memset(tab_s[:], 0)
+        nc.gpsimd.memset(w2_s[:].bitcast(I32), 0)
 
-        def load_w1(b, a, c0, c1):
-            rows = w1[a * PASS : (a + 1) * PASS, b * PASS + c0 : b * PASS + c1]
-            w1_raw[b, a, c0] = tile([P, PACK, c1 - c0], F32, "w1_raw%d%d_%d" % (b, a, c0))
-            nc.sync.dma_start(out=w1_raw[b, a, c0][:], in_=rows.rearrange("(p j) c -> p j c", j=PACK))
+        def load_w1(b, a):
+            rows = w1[a * PASS : (a + 1) * PASS, b * PASS : (b + 1) * PASS]
+            w1_raw[b, a] = tile([P, PACK, PASS], F32, "w1_raw%d%d" % (b, a))
+            nc.sync.dma_start(out=w1_raw[b, a][:], in_=rows.rearrange("(p j) c -> p j c", j=PACK))
 
         nc.sync.dma_start(offs_sb[:], offs)
         for q in range(4):
@@ -63,12 +63,11 @@ def tile_list_join_sketch_cardinality_kernel(
         nc.scalar.dma_start(out=g_sb[:], in_=g.rearrange("(b p t) -> p b t", b=2, t=PACK))
         for a in range(2):
             nc.sync.dma_start(out=tab_w[a][:], in_=tab_words[a].rearrange("p n t -> p (n t)").bitcast(I32))
-            load_w1(0, a, 0, PASS // 2)
-            load_w1(0, a, PASS // 2, PASS)
+            load_w1(0, a)
         nc.sync.dma_start(pos_sb[0][:], pos1)
         nc.sync.dma_start(pos_sb[1][:], pos2)
         for a in range(2):
-            load_w1(1, a, 0, PASS)
+            load_w1(1, a)
         nc.sync.dma_start(out=w2_w[:].bitcast(I32), in_=w2_words.rearrange("a p c -> p a c").bitcast(I32))
         for q in range(4):
             nc.sync.dma_start(
@@ -96,27 +95,26 @@ def tile_list_join_sketch_cardinality_kernel(
 
         w1_bf, w1_w, w1_s = {}, {}, {}
 
-        def round_w1(copy, b, a, c0, c1, tag=None):
-            if c0 == 0:
-                w1_bf[b, a] = tile([P, PACK, P, PACK], BF16, "w1_bf%d%d" % (b, a), tag)
-            m = slice(c0 // PACK, c1 // PACK)
+        def round_w1(copy, b, a, u, tag=None):
+            w1_bf[b, a, u] = tile([P, 2, P, PACK], BF16, "w1_bf%d%d%d" % (b, a, u), tag)
             copy(
-                w1_bf[b, a][:, :, m, :].rearrange("p t m j -> p m t j"),
-                w1_raw[b, a, c0][:].rearrange("p j (m t) -> p m t j", t=PACK),
+                w1_bf[b, a, u][:].rearrange("p e m j -> p m j e"),
+                w1_raw[b, a][:].rearrange("p j (m u e) -> p u m j e", u=2, e=2)[:, u],
             )
 
-        def quantize_w1(b, a, t0, t1):
-            width = (t1 - t0) * P
-            words = tile([P, width], U32, "w1_w%d%d%d" % (b, a, t0))
-            scales = tile([P, width], U8, "w1_s%d%d%d" % (b, a, t0))
-            nc.vector.quantize_mx(
-                out=words[:].bitcast(FP8X4),
-                scales=scales[:],
-                in_=w1_bf[b, a][:, t0:t1, :, :].rearrange("p t m j -> p (t m j)"),
-            )
-            for t in range(t0, t1):
-                cols = slice((t - t0) * P, (t - t0 + 1) * P)
-                w1_w[b, a, t], w1_s[b, a, t] = words[:, cols], scales[:, cols]
+        def quantize_w1(b, a, u, parts=((0, 2),)):
+            for e0, e1 in parts:
+                width = (e1 - e0) * P
+                words = tile([P, width], U32, "w1_w%d%d%d" % (b, a, 2 * u + e0))
+                scales = tile([P, width], U8, "w1_s%d%d%d" % (b, a, 2 * u + e0))
+                nc.vector.quantize_mx(
+                    out=words[:].bitcast(FP8X4),
+                    scales=scales[:],
+                    in_=w1_bf[b, a, u][:, e0:e1].rearrange("p e m j -> p (e m j)"),
+                )
+                for e in range(e0, e1):
+                    cols = slice((e - e0) * P, (e - e0 + 1) * P)
+                    w1_w[b, a, 2 * u + e], w1_s[b, a, 2 * u + e] = words[:, cols], scales[:, cols]
 
         h = [[tile([P, S], F32, "h%d%d" % (b, t)) for t in range(PACK)] for b in range(2)]
         acc = {}
@@ -146,25 +144,27 @@ def tile_list_join_sketch_cardinality_kernel(
         def sides(b, j0, n):
             return [tile([P, PACK, n], F32, "side%d_%d_%d" % (side, b, j0), "side%d_%d" % (side, b)) for side in range(2)]
 
-        def fetch(pair, b, t, j0, n):
+        def fetch(pair, b, t, j0, n, last_parts=None):
             for side in range(2):
-                entries = pos_sb[side][:, j0 // LIST_ROWS : (j0 + n) // LIST_ROWS]
+                for lo, hi in last_parts if last_parts and side == 1 else ((0, n),):
+                    entries = pos_sb[side][:, (j0 + lo) // LIST_ROWS : (j0 + hi) // LIST_ROWS]
+                    nc.vector.tensor_tensor(
+                        pair[side][:, t, lo:hi], h[b][t][:].indirect(entries), g_wide[b][:, t, lo:hi], ALU.mult
+                    )
+
+        def overlap(pair, b, j0, parts):
+            z_bf = tile([P, parts[-1][1], PACK], BF16, "z_bf%d_%d" % (b, j0))
+            for lo, hi in parts:
+                left, right = (side[:, :, lo:hi].rearrange("p t (c i) -> p c t i", i=2) for side in pair)
                 nc.vector.tensor_tensor(
-                    pair[side][:, t, :], h[b][t][:].indirect(entries), g_wide[b][:, t, 0:n], ALU.mult
+                    z_bf[:, lo:hi, :].rearrange("p (c i) t -> p c t i", i=2), left, right, ALU.min
                 )
-
-        def overlap(pair, b, j0, n):
-            z_bf = tile([P, n, PACK], BF16, "z_bf%d_%d" % (b, j0))
-            left, right = (side[:].rearrange("p t (c i) -> p c t i", i=4) for side in pair)
-            nc.vector.tensor_tensor(z_bf[:].rearrange("p (c i) t -> p c t i", i=4), left, right, ALU.min)
-            return z_bf
-
-        def quantize_z(z_bf, b, j0, n):
-            nc.vector.quantize_mx(
-                out=z_w[b][:, j0 : j0 + n].bitcast(FP8X4),
-                scales=z_s[b][:, j0 : j0 + n],
-                in_=z_bf[:].rearrange("p j t -> p (j t)"),
-            )
+            for lo, hi in parts:
+                nc.vector.quantize_mx(
+                    out=z_w[b][:, j0 + lo : j0 + hi].bitcast(FP8X4),
+                    scales=z_s[b][:, j0 + lo : j0 + hi],
+                    in_=z_bf[:, lo:hi, :].rearrange("p j t -> p (j t)"),
+                )
 
         def second_product(y, b, nt, j0, jj):
             cols = slice(j0 + jj, j0 + jj + N_MX)
@@ -178,20 +178,19 @@ def tile_list_join_sketch_cardinality_kernel(
                 stop=(b == 1),
             )
 
-        half = PASS // 2
         spread_g(0)
         gather_words(0)
-        round_w1(nc.scalar.copy, 0, 0, 0, half)
-        round_w1(nc.scalar.copy, 0, 0, half, PASS)
-        spread_g(1, "w1_raw00_%d" % half)
-        quantize_w1(0, 0, 0, PACK)
+        for u in range(2):
+            round_w1(nc.scalar.copy, 0, 0, u)
+            quantize_w1(0, 0, u)
+        spread_g(1, "w1_raw00")
         for t in range(PACK):
             first_product(0, 0, t)
         gather_words(1)
-        round_w1(nc.scalar.copy, 0, 1, 0, half)
-        round_w1(nc.vector.tensor_copy, 0, 1, half, PASS)
+        for u, copy in enumerate((nc.scalar.copy, nc.vector.tensor_copy)):
+            round_w1(copy, 0, 1, u)
+            quantize_w1(0, 1, u, ((0, 1), (1, 2)))
         for t in range(PACK):
-            quantize_w1(0, 1, t, t + 1)
             first_product(0, 1, t)
 
         pair = sides(0, 0, J)
@@ -200,8 +199,9 @@ def tile_list_join_sketch_cardinality_kernel(
             fetch(pair, 0, t, 0, J)
             if t >= 2:
                 a = t - 2
-                round_w1(nc.scalar.copy, 1, a, 0, PASS, "w1_w01%d" % t)
-                quantize_w1(1, a, 0, PACK)
+                for u, kind in enumerate("ws"):
+                    round_w1(nc.scalar.copy, 1, a, u, "w1_%s01%d" % (kind, t))
+                    quantize_w1(1, a, u)
             if t == 2:
                 for tt in range(PACK - 1):
                     first_product(1, 0, tt)
@@ -209,23 +209,25 @@ def tile_list_join_sketch_cardinality_kernel(
         for t in range(PACK):
             first_product(1, 1, t)
             sigmoid(1, t)
-        quantize_z(overlap(pair, 0, 0, J), 0, 0, J)
+        overlap(pair, 0, 0, ((0, J // 2), (J // 2, J)))
 
         out_rows = out.rearrange("(t p) j -> p t j", p=P)
         for c, (j0, n) in enumerate(CHUNKS):
+            parts = ((0, 256), (256, n)) if n > 256 else ((0, n),)
             pair = sides(1, j0, n)
-            y = [psum.tile([P, n], F32, name="bank%d" % (4 * (c % 2) + nt)) for nt in range(N // P)]
-            if n == N_MX:
-                for nt in range(N // P):
-                    second_product(y[nt], 0, nt, j0, 0)
+            y = [psum.tile([P, n], F32, name="bank%d" % (4 * c + nt)) for nt in range(N // P)]
+            for nt in range(N // P):
+                second_product(y[nt], 0, nt, j0, 0)
             for t in range(PACK):
-                fetch(pair, 1, t, j0, n)
-            quantize_z(overlap(pair, 1, j0, n), 1, j0, n)
+                fetch(pair, 1, t, j0, n, parts if t == PACK - 1 else None)
+            overlap(pair, 1, j0, parts)
             res = tile([P, N // P, n], F32, "res%d" % c)
             for nt in range(N // P):
                 for jj in range(0, n, N_MX):
-                    if n != N_MX:
+                    if jj > 0:
                         second_product(y[nt], 0, nt, j0, jj)
                     second_product(y[nt], 1, nt, j0, jj)
                 nc.scalar.activation(res[:, nt, :], y[nt][:], ACT.Exp, bias=b2_sb[:, nt : nt + 1])
-            nc.sync.dma_start(out=out_rows[:, :, j0 : j0 + n], in_=res[:])
+                if nt % 2 == 1:
+                    rows = slice(nt - 1, nt + 1)
+                    nc.sync.dma_start(out=out_rows[:, rows, j0 : j0 + n], in_=res[:, rows, :])

@@ -47,23 +47,27 @@ def tile_list_join_sketch_cardinality_kernel(
         g_sb = tile([P, 2, PACK], F32, "g_sb")
         b2_sb = tile([P, N // P], F32, "b2_sb")
 
-        nc.gpsimd.memset(tab_s[:], 0)
+        nc.vector.memset(tab_s[:], 0)
         nc.gpsimd.memset(w2_s[:].bitcast(I32), 0)
 
-        def load_w1(b, a):
-            rows = w1[a * PASS : (a + 1) * PASS, b * PASS : (b + 1) * PASS]
+        def load_w1(b, a, parts=1):
             w1_raw[b, a] = tile([P, PACK, PASS], F32, "w1_raw%d%d" % (b, a))
-            nc.sync.dma_start(out=w1_raw[b, a][:], in_=rows.rearrange("(p j) c -> p j c", j=PACK))
+            rows = w1[a * PASS : (a + 1) * PASS, b * PASS : (b + 1) * PASS].rearrange("(p j) c -> p j c", j=PACK)
+            for c0 in range(0, PASS, PASS // parts):
+                cols = slice(c0, c0 + PASS // parts)
+                nc.sync.dma_start(out=w1_raw[b, a][:, :, cols], in_=rows[:, :, cols])
 
         nc.sync.dma_start(offs_sb[:], offs)
         for q in range(4):
-            nc.scalar.dma_start(
+            nc.sync.dma_start(
                 out=tab_s[32 * q : 32 * q + 8, :], in_=tab_scales[:, 4 * q : 4 * q + 4, :].bitcast(I32)
             )
         nc.scalar.dma_start(out=g_sb[:], in_=g.rearrange("(b p t) -> p b t", b=2, t=PACK))
         for a in range(2):
-            nc.sync.dma_start(out=tab_w[a][:], in_=tab_words[a].rearrange("p n t -> p (n t)").bitcast(I32))
-            load_w1(0, a)
+            words = tab_words[a].rearrange("p n t -> p (n t)").bitcast(I32)
+            for cols in (slice(0, T // 2), slice(T // 2, T)) if a == 0 else (slice(0, T),):
+                nc.sync.dma_start(out=tab_w[a][:, cols], in_=words[:, cols])
+            load_w1(0, a, a + 1)
         nc.sync.dma_start(pos_sb[0][:], pos1)
         nc.sync.dma_start(pos_sb[1][:], pos2)
         for a in range(2):
@@ -95,17 +99,17 @@ def tile_list_join_sketch_cardinality_kernel(
 
         w1_bf, w1_w, w1_s = {}, {}, {}
 
-        def round_w1(copy, b, a, u, tag=None):
+        def round_w1(copy, b, a, u, tag=None, parts=1):
             w1_bf[b, a, u] = tile([P, 2, P, PACK], BF16, "w1_bf%d%d%d" % (b, a, u), tag)
-            copy(
-                w1_bf[b, a, u][:].rearrange("p e m j -> p m j e"),
-                w1_raw[b, a][:].rearrange("p j (m u e) -> p u m j e", u=2, e=2)[:, u],
-            )
+            dst = w1_bf[b, a, u][:].rearrange("p e m j -> p m j e")
+            src = w1_raw[b, a][:].rearrange("p j (m u e) -> p u m j e", u=2, e=2)[:, u]
+            for m0 in range(0, P, P // parts):
+                copy(dst[:, m0 : m0 + P // parts], src[:, m0 : m0 + P // parts])
 
-        def quantize_w1(b, a, u, parts=((0, 2),)):
+        def quantize_w1(b, a, u, parts=((0, 2),), tag=None):
             for e0, e1 in parts:
                 width = (e1 - e0) * P
-                words = tile([P, width], U32, "w1_w%d%d%d" % (b, a, 2 * u + e0))
+                words = tile([P, width], U32, "w1_w%d%d%d" % (b, a, 2 * u + e0), tag)
                 scales = tile([P, width], U8, "w1_s%d%d%d" % (b, a, 2 * u + e0))
                 nc.vector.quantize_mx(
                     out=words[:].bitcast(FP8X4),
@@ -174,23 +178,29 @@ def tile_list_join_sketch_cardinality_kernel(
                 lhsT_scale=w2_s[:, b, nt * P : (nt + 1) * P],
                 rhs=z_w[b][:, cols].bitcast(FP8X4),
                 rhs_scale=z_s[b][:, cols],
-                start=(b == 0),
-                stop=(b == 1),
+                start=(b == 0 and jj == 0),
+                stop=(b == 1 and jj + N_MX == y.shape[1]),
             )
 
+        singly = ((0, 1), (1, 2))
         spread_g(0)
+        spread_g(1)
         gather_words(0)
-        for u in range(2):
-            round_w1(nc.scalar.copy, 0, 0, u)
-            quantize_w1(0, 0, u)
-        spread_g(1, "w1_raw00")
-        for t in range(PACK):
+        round_w1(nc.scalar.copy, 0, 0, 0)
+        round_w1(nc.scalar.copy, 0, 0, 1)
+        quantize_w1(0, 0, 0)
+        for t in (0, 1):
             first_product(0, 0, t)
         gather_words(1)
-        for u, copy in enumerate((nc.scalar.copy, nc.vector.tensor_copy)):
-            round_w1(copy, 0, 1, u)
-            quantize_w1(0, 1, u, ((0, 1), (1, 2)))
-        for t in range(PACK):
+        round_w1(nc.scalar.copy, 0, 1, 0, parts=2)
+        quantize_w1(0, 1, 0, singly)
+        for t in (0, 1):
+            first_product(0, 1, t)
+        round_w1(nc.vector.tensor_copy, 0, 1, 1, "w1_bf010")
+        quantize_w1(0, 0, 1, tag="w1_raw01")
+        quantize_w1(0, 1, 1, singly)
+        for t in (2, 3):
+            first_product(0, 0, t)
             first_product(0, 1, t)
 
         pair = sides(0, 0, J)
@@ -217,17 +227,14 @@ def tile_list_join_sketch_cardinality_kernel(
             pair = sides(1, j0, n)
             y = [psum.tile([P, n], F32, name="bank%d" % (4 * c + nt)) for nt in range(N // P)]
             for nt in range(N // P):
-                second_product(y[nt], 0, nt, j0, 0)
+                for jj in range(0, n, N_MX):
+                    second_product(y[nt], 0, nt, j0, jj)
             for t in range(PACK):
                 fetch(pair, 1, t, j0, n, parts if t == PACK - 1 else None)
             overlap(pair, 1, j0, parts)
             res = tile([P, N // P, n], F32, "res%d" % c)
             for nt in range(N // P):
                 for jj in range(0, n, N_MX):
-                    if jj > 0:
-                        second_product(y[nt], 0, nt, j0, jj)
                     second_product(y[nt], 1, nt, j0, jj)
                 nc.scalar.activation(res[:, nt, :], y[nt][:], ACT.Exp, bias=b2_sb[:, nt : nt + 1])
-                if nt % 2 == 1:
-                    rows = slice(nt - 1, nt + 1)
-                    nc.sync.dma_start(out=out_rows[:, rows, j0 : j0 + n], in_=res[:, rows, :])
+                nc.sync.dma_start(out=out_rows[:, nt, j0 : j0 + n], in_=res[:, nt, :])

@@ -99,12 +99,12 @@ def tile_list_join_sketch_cardinality_kernel(
 
         w1_bf, w1_w, w1_s = {}, {}, {}
 
-        def round_w1(copy, b, a, u, tag=None, parts=1):
-            w1_bf[b, a, u] = tile([P, 2, P, PACK], BF16, "w1_bf%d%d%d" % (b, a, u), tag)
+        def round_w1(copy, b, a, u, m0=0, m1=P, tag=None):
+            if m0 == 0:
+                w1_bf[b, a, u] = tile([P, 2, P, PACK], BF16, "w1_bf%d%d%d" % (b, a, u), tag)
             dst = w1_bf[b, a, u][:].rearrange("p e m j -> p m j e")
             src = w1_raw[b, a][:].rearrange("p j (m u e) -> p u m j e", u=2, e=2)[:, u]
-            for m0 in range(0, P, P // parts):
-                copy(dst[:, m0 : m0 + P // parts], src[:, m0 : m0 + P // parts])
+            copy(dst[:, m0:m1], src[:, m0:m1])
 
         def quantize_w1(b, a, u, parts=((0, 2),), tag=None):
             for e0, e1 in parts:
@@ -159,9 +159,9 @@ def tile_list_join_sketch_cardinality_kernel(
         def overlap(pair, b, j0, parts):
             z_bf = tile([P, parts[-1][1], PACK], BF16, "z_bf%d_%d" % (b, j0))
             for lo, hi in parts:
-                left, right = (side[:, :, lo:hi].rearrange("p t (c i) -> p c t i", i=2) for side in pair)
+                left, right = (side[:, :, lo:hi].rearrange("p t (c i) -> p c t i", i=4) for side in pair)
                 nc.vector.tensor_tensor(
-                    z_bf[:, lo:hi, :].rearrange("p (c i) t -> p c t i", i=2), left, right, ALU.min
+                    z_bf[:, lo:hi, :].rearrange("p (c i) t -> p c t i", i=4), left, right, ALU.min
                 )
             for lo, hi in parts:
                 nc.vector.quantize_mx(
@@ -192,12 +192,14 @@ def tile_list_join_sketch_cardinality_kernel(
         for t in (0, 1):
             first_product(0, 0, t)
         gather_words(1)
-        round_w1(nc.scalar.copy, 0, 1, 0, parts=2)
+        round_w1(nc.scalar.copy, 0, 1, 0, 0, P // 2)
+        round_w1(nc.scalar.copy, 0, 1, 1, 0, P // 2)
+        round_w1(nc.scalar.copy, 0, 1, 0, P // 2, P)
+        round_w1(nc.vector.tensor_copy, 0, 1, 1, P // 2, P)
         quantize_w1(0, 1, 0, singly)
         for t in (0, 1):
             first_product(0, 1, t)
-        round_w1(nc.vector.tensor_copy, 0, 1, 1, "w1_bf010")
-        quantize_w1(0, 0, 1, tag="w1_raw01")
+        quantize_w1(0, 0, 1, tag="w1_bf010")
         quantize_w1(0, 1, 1, singly)
         for t in (2, 3):
             first_product(0, 0, t)
@@ -210,7 +212,7 @@ def tile_list_join_sketch_cardinality_kernel(
             if t >= 2:
                 a = t - 2
                 for u, kind in enumerate("ws"):
-                    round_w1(nc.scalar.copy, 1, a, u, "w1_%s01%d" % (kind, t))
+                    round_w1(nc.scalar.copy, 1, a, u, tag="w1_%s01%d" % (kind, t))
                     quantize_w1(1, a, u)
             if t == 2:
                 for tt in range(PACK - 1):
@@ -223,7 +225,7 @@ def tile_list_join_sketch_cardinality_kernel(
 
         out_rows = out.rearrange("(t p) j -> p t j", p=P)
         for c, (j0, n) in enumerate(CHUNKS):
-            parts = ((0, 256), (256, n)) if n > 256 else ((0, n),)
+            parts = ((0, 256), (256, n)) if n > 256 else ((0, n // 2), (n // 2, n))
             pair = sides(1, j0, n)
             y = [psum.tile([P, n], F32, name="bank%d" % (4 * c + nt)) for nt in range(N // P)]
             for nt in range(N // P):

@@ -16,12 +16,15 @@ ACT = mybir.ActivationFunctionType
 ALU = mybir.AluOpType
 
 P = 128
+HALF = P // 2
 PACK = 4
 PASS = P * PACK
+QUARTER = PASS // 2
 BANK = 512
 LIST_ROWS = 16
 CHUNKS = ((0, 384), (384, 128))
 N_MX = 128
+EARLY = 768
 
 FLOPS = 2 * K * H * S + 2 * H * N * J
 
@@ -41,37 +44,37 @@ def tile_list_join_sketch_cardinality_kernel(
         pos_sb = [keep.tile([P, J // LIST_ROWS], U16, name="pos%d_sb" % side) for side in range(2)]
         tab_w = [tile([P, T], I32, "tab_w%d" % a) for a in range(2)]
         tab_s = tile([P, T // 4], I32, "tab_s")
-        w1_raw = {}
         w2_w = tile([P, 2, 2 * N], U8, "w2_w")
         w2_s = tile([P, 2, N], U8, "w2_s")
-        g_sb = tile([P, 2, PACK], F32, "g_sb")
+        g_low = tile([P, 2, 2], F32, "g_low")
+        g_high = tile([P, PACK], F32, "g_high")
         b2_sb = tile([P, N // P], F32, "b2_sb")
 
         nc.vector.memset(tab_s[:], 0)
         nc.gpsimd.memset(w2_s[:].bitcast(I32), 0)
 
-        def load_w1(b, a, parts=1):
-            w1_raw[b, a] = tile([P, PACK, PASS], F32, "w1_raw%d%d" % (b, a))
-            rows = w1[a * PASS : (a + 1) * PASS, b * PASS : (b + 1) * PASS].rearrange("(p j) c -> p j c", j=PACK)
-            for c0 in range(0, PASS, PASS // parts):
-                cols = slice(c0, c0 + PASS // parts)
-                nc.sync.dma_start(out=w1_raw[b, a][:, :, cols], in_=rows[:, :, cols])
+        def load_w1(a, c0, width):
+            raw = tile([P, PACK, width], F32, "w1_raw%d_%d" % (a, c0))
+            rows = w1[a * PASS : (a + 1) * PASS, c0 : c0 + width]
+            nc.sync.dma_start(out=raw[:], in_=rows.rearrange("(p j) c -> p j c", j=PACK))
+            return raw
 
         nc.sync.dma_start(offs_sb[:], offs)
+        nc.sync.dma_start(out=g_low[:], in_=g[0:PASS].rearrange("(u p e) -> p u e", u=2, e=2))
         for q in range(4):
             nc.sync.dma_start(
                 out=tab_s[32 * q : 32 * q + 8, :], in_=tab_scales[:, 4 * q : 4 * q + 4, :].bitcast(I32)
             )
-        nc.scalar.dma_start(out=g_sb[:], in_=g.rearrange("(b p t) -> p b t", b=2, t=PACK))
-        for a in range(2):
-            words = tab_words[a].rearrange("p n t -> p (n t)").bitcast(I32)
-            for cols in (slice(0, T // 2), slice(T // 2, T)) if a == 0 else (slice(0, T),):
-                nc.sync.dma_start(out=tab_w[a][:, cols], in_=words[:, cols])
-            load_w1(0, a, a + 1)
+        words = [tab_words[a].rearrange("p n t -> p (n t)").bitcast(I32) for a in range(2)]
+        nc.sync.dma_start(out=tab_w[0][:], in_=words[0])
+        low_raw = {(0, 0): load_w1(0, 0, QUARTER)}
+        nc.sync.dma_start(out=g_high[:], in_=g[PASS:H].rearrange("(p t) -> p t", t=PACK))
+        nc.sync.dma_start(out=tab_w[1][:], in_=words[1])
+        low_raw[0, 1] = load_w1(1, 0, QUARTER)
         nc.sync.dma_start(pos_sb[0][:], pos1)
         nc.sync.dma_start(pos_sb[1][:], pos2)
-        for a in range(2):
-            load_w1(1, a)
+        low_raw.update({(1, a): load_w1(a, QUARTER, QUARTER) for a in range(2)})
+        high_raw = [load_w1(a, PASS, PASS) for a in range(2)]
         nc.sync.dma_start(out=w2_w[:].bitcast(I32), in_=w2_words.rearrange("a p c -> p a c").bitcast(I32))
         for q in range(4):
             nc.sync.dma_start(
@@ -81,94 +84,105 @@ def tile_list_join_sketch_cardinality_kernel(
         with nc.allow_non_contiguous_dma(reason="one bias value a partition"):
             nc.sync.dma_start(out=b2_sb[:], in_=b2.rearrange("(t p) -> p t", p=P))
 
-        g_width = [J, max(n for j0, n in CHUNKS)]
+        warm = tile([P, 1], F32, "warm")
+        nc.scalar.activation(warm[:], g_low[:, 0, 0:1], ACT.Sigmoid)
+
+        widest = max(n for j0, n in CHUNKS)
         g_wide = {}
+        g_rows = [g_low[:].rearrange("p u e -> p (u e)"), g_high[:]]
 
-        def spread_g(b, tag=None):
-            g_wide[b] = tile([P, PACK, g_width[b]], F32, "g_wide%d" % b, tag)
-            nc.scalar.activation(
-                g_wide[b][:], g_sb[:, b, :].unsqueeze(2).to_broadcast([P, PACK, g_width[b]]), ACT.Copy
-            )
+        def spread_g(b, width, tag=None):
+            g_wide[b] = tile([P, PACK, width], F32, "g_wide%d" % b, tag)
+            nc.scalar.activation(g_wide[b][:], g_rows[b].unsqueeze(2).to_broadcast([P, PACK, width]), ACT.Copy)
 
-        v_w = [tile([P, S], U32, "v_w%d" % a) for a in range(2)]
+        v_w = {}
         v_s = tile([P, S], U8, "v_s")
         nc.vector.tensor_copy(v_s[:], tab_s[:].bitcast(U8).indirect(offs_sb[:]))
 
-        def gather_words(a):
-            nc.vector.tensor_copy(v_w[a][:], tab_w[a][:].bitcast(U32).indirect(offs_sb[:]))
+        def gather_words(a, lo, hi, tag=None):
+            picked = tile([P, hi - lo], U32, "v_w%d_%d" % (a, lo), tag)
+            entries = offs_sb[:, lo // LIST_ROWS : hi // LIST_ROWS]
+            nc.vector.tensor_copy(picked[:], tab_w[a][:].bitcast(U32).indirect(entries))
+            v_w.setdefault(a, []).append((lo, hi, picked))
 
-        w1_bf, w1_w, w1_s = {}, {}, {}
+        w1_w, w1_s = {}, {}
 
-        def round_w1(copy, b, a, u, m0=0, m1=P, tag=None):
-            if m0 == 0:
-                w1_bf[b, a, u] = tile([P, 2, P, PACK], BF16, "w1_bf%d%d%d" % (b, a, u), tag)
-            dst = w1_bf[b, a, u][:].rearrange("p e m j -> p m j e")
-            src = w1_raw[b, a][:].rearrange("p j (m u e) -> p u m j e", u=2, e=2)[:, u]
-            copy(dst[:, m0:m1], src[:, m0:m1])
+        def round_low(copy, rounded, u, a):
+            dst = rounded.rearrange("p (e m j) -> p m j e", e=2, j=PACK)
+            copy(dst, low_raw[u, a][:].rearrange("p j (m e) -> p m j e", e=2))
 
-        def quantize_w1(b, a, u, parts=((0, 2),), tag=None):
+        def prepare_plane(a, e):
+            rounded = tile([P, PASS], BF16, "w1_plane%d%d" % (a, e))
+            dst = rounded[:].rearrange("p (m i j) -> p m j i", i=2, j=PACK)
+            nc.scalar.copy(dst, low_raw[0, a][:].rearrange("p j (m i e) -> p e m j i", i=2, e=2)[:, e])
+            words = tile([P, P], U32, "w1_w0%d%d" % (a, e))
+            scales = tile([P, P], U8, "w1_s0%d%d" % (a, e))
+            nc.vector.quantize_mx(out=words[:].bitcast(FP8X4), scales=scales[:], in_=rounded[:])
+            w1_w[0, a, e], w1_s[0, a, e] = words[:], scales[:]
+
+        def round_high(rounded, u, a):
+            dst = rounded.rearrange("p (e m j) -> p m j e", e=2, j=PACK)
+            src = high_raw[a][:].rearrange("p j (m u e) -> p u m j e", u=2, e=2)[:, u]
+            nc.scalar.copy(dst, src)
+
+        def quantize_w1(rounded, b, u, a, parts=((0, 2),)):
             for e0, e1 in parts:
                 width = (e1 - e0) * P
-                words = tile([P, width], U32, "w1_w%d%d%d" % (b, a, 2 * u + e0), tag)
+                words = tile([P, width], U32, "w1_w%d%d%d" % (b, a, 2 * u + e0))
                 scales = tile([P, width], U8, "w1_s%d%d%d" % (b, a, 2 * u + e0))
                 nc.vector.quantize_mx(
-                    out=words[:].bitcast(FP8X4),
-                    scales=scales[:],
-                    in_=w1_bf[b, a, u][:, e0:e1].rearrange("p e m j -> p (e m j)"),
+                    out=words[:].bitcast(FP8X4), scales=scales[:], in_=rounded[:, e0 * PASS : e1 * PASS]
                 )
                 for e in range(e0, e1):
                     cols = slice((e - e0) * P, (e - e0 + 1) * P)
                     w1_w[b, a, 2 * u + e], w1_s[b, a, 2 * u + e] = words[:, cols], scales[:, cols]
 
-        h = [[tile([P, S], F32, "h%d%d" % (b, t)) for t in range(PACK)] for b in range(2)]
+        def rounded_tile(name, tag=None):
+            return tile([P, 2 * PASS], BF16, name, tag)[:]
+
+        h = {}
         acc = {}
+        banks = (((0, 1, 6), (2, 3), (4, 5), (6, 7)), ((0, 1), (2, 3), (4, 5), (6, 7)))
+
+        def spans(b, t):
+            edges = (0, BANK, EARLY, S) if len(banks[b][t]) == 3 else (0, BANK, S)
+            return list(zip(edges, edges[1:]))
 
         def first_product(b, a, t):
-            for half in range(2):
+            for (c0, c1), bank in zip(spans(b, t), banks[b][t]):
                 if a == 0:
-                    acc[t, half] = psum.tile([P, BANK], F32, name="bank%d" % (2 * t + half))
-                cols = slice(half * BANK, (half + 1) * BANK)
-                nc.tensor.matmul_mx(
-                    out=acc[t, half][:],
-                    lhsT=w1_w[b, a, t].bitcast(FP8X4),
-                    lhsT_scale=w1_s[b, a, t],
-                    rhs=v_w[a][:, cols].bitcast(FP8X4),
-                    rhs_scale=v_s[4 * a : P, cols],
-                    start=(a == 0),
-                    stop=(a == 1),
-                )
+                    acc[t, c0] = psum.tile([P, c1 - c0], F32, name="bank%d" % bank)
+                for lo, hi, picked in v_w[a]:
+                    first, last = max(lo, c0), min(hi, c1)
+                    if first < last:
+                        nc.tensor.matmul_mx(
+                            out=acc[t, c0][:, first - c0 : last - c0],
+                            lhsT=w1_w[b, a, t].bitcast(FP8X4),
+                            lhsT_scale=w1_s[b, a, t],
+                            rhs=picked[:, first - lo : last - lo].bitcast(FP8X4),
+                            rhs_scale=v_s[4 * a : P, first:last],
+                            start=(a == 0),
+                            stop=(a == 1 and last == c1),
+                        )
 
-        def sigmoid(b, t):
-            for half in range(2):
-                nc.scalar.activation(h[b][t][:, half * BANK : (half + 1) * BANK], acc[t, half][:], ACT.Sigmoid)
+        def sigmoid(b, t, tag=None):
+            h[b, t] = tile([P, S], F32, "h%d%d" % (b, t), tag)
+            for c0, c1 in spans(b, t):
+                nc.scalar.activation(h[b, t][:, c0:c1], acc[t, c0][:], ACT.Sigmoid)
+
+        def fetch(dst, side, b, t, j0, lo, hi):
+            entries = pos_sb[side][:, (j0 + lo) // LIST_ROWS : (j0 + hi) // LIST_ROWS]
+            nc.vector.tensor_tensor(dst, h[b, t][:].indirect(entries), g_wide[b][:, t, lo:hi], ALU.mult)
 
         z_w = [tile([P, J], U32, "z_w%d" % b) for b in range(2)]
         z_s = [tile([P, J], U8, "z_s%d" % b) for b in range(2)]
 
-        def sides(b, j0, n):
-            return [tile([P, PACK, n], F32, "side%d_%d_%d" % (side, b, j0), "side%d_%d" % (side, b)) for side in range(2)]
-
-        def fetch(pair, b, t, j0, n, last_parts=None):
-            for side in range(2):
-                for lo, hi in last_parts if last_parts and side == 1 else ((0, n),):
-                    entries = pos_sb[side][:, (j0 + lo) // LIST_ROWS : (j0 + hi) // LIST_ROWS]
-                    nc.vector.tensor_tensor(
-                        pair[side][:, t, lo:hi], h[b][t][:].indirect(entries), g_wide[b][:, t, lo:hi], ALU.mult
-                    )
-
-        def overlap(pair, b, j0, parts):
-            z_bf = tile([P, parts[-1][1], PACK], BF16, "z_bf%d_%d" % (b, j0))
-            for lo, hi in parts:
-                left, right = (side[:, :, lo:hi].rearrange("p t (c i) -> p c t i", i=4) for side in pair)
-                nc.vector.tensor_tensor(
-                    z_bf[:, lo:hi, :].rearrange("p (c i) t -> p c t i", i=4), left, right, ALU.min
-                )
-            for lo, hi in parts:
-                nc.vector.quantize_mx(
-                    out=z_w[b][:, j0 + lo : j0 + hi].bitcast(FP8X4),
-                    scales=z_s[b][:, j0 + lo : j0 + hi],
-                    in_=z_bf[:, lo:hi, :].rearrange("p j t -> p (j t)"),
-                )
+        def quantize_z(z_bf, b, j0, lo, hi):
+            nc.vector.quantize_mx(
+                out=z_w[b][:, j0 + lo : j0 + hi].bitcast(FP8X4),
+                scales=z_s[b][:, j0 + lo : j0 + hi],
+                in_=z_bf[:, lo:hi, :].rearrange("p j t -> p (j t)"),
+            )
 
         def second_product(y, b, nt, j0, jj):
             cols = slice(j0 + jj, j0 + jj + N_MX)
@@ -182,58 +196,113 @@ def tile_list_join_sketch_cardinality_kernel(
                 stop=(b == 1 and jj + N_MX == y.shape[1]),
             )
 
-        singly = ((0, 1), (1, 2))
-        spread_g(0)
-        spread_g(1)
-        gather_words(0)
-        round_w1(nc.scalar.copy, 0, 0, 0)
-        round_w1(nc.scalar.copy, 0, 0, 1)
-        quantize_w1(0, 0, 0)
-        for t in (0, 1):
-            first_product(0, 0, t)
-        gather_words(1)
-        round_w1(nc.scalar.copy, 0, 1, 0, 0, P // 2)
-        round_w1(nc.scalar.copy, 0, 1, 1, 0, P // 2)
-        round_w1(nc.scalar.copy, 0, 1, 0, P // 2, P)
-        round_w1(nc.vector.tensor_copy, 0, 1, 1, P // 2, P)
-        quantize_w1(0, 1, 0, singly)
-        for t in (0, 1):
-            first_product(0, 1, t)
-        quantize_w1(0, 0, 1, tag="w1_bf010")
-        quantize_w1(0, 1, 1, singly)
-        for t in (2, 3):
-            first_product(0, 0, t)
-            first_product(0, 1, t)
+        low_sides = {}
+        halves = tile([P, 2, 2 * J], BF16, "halves")
 
-        pair = sides(0, 0, J)
-        for t in range(PACK):
-            sigmoid(0, t)
-            fetch(pair, 0, t, 0, J)
-            if t >= 2:
-                a = t - 2
-                for u, kind in enumerate("ws"):
-                    round_w1(nc.scalar.copy, 1, a, u, tag="w1_%s01%d" % (kind, t))
-                    quantize_w1(1, a, u)
-            if t == 2:
-                for tt in range(PACK - 1):
-                    first_product(1, 0, tt)
-        first_product(1, 0, PACK - 1)
-        for t in range(PACK):
+        low_parts = ((0, J // 2), (J // 2, J))
+
+        def fetch_low(u, e, side, tag=None):
+            if e == 0:
+                low_sides[u, side] = tile([P, 2, J], F32, "low_side%d%d" % (u, side), tag)
+            for lo, hi in low_parts if e == 1 and side == 1 else ((0, J),):
+                fetch(low_sides[u, side][:, e, lo:hi], side, 0, 2 * u + e, 0, lo, hi)
+
+        def overlap_low(u):
+            pairs = tile([P, J, 2], BF16, "pairs%d" % u)
+            left, right = (low_sides[u, side][:].rearrange("p e j -> p j e") for side in range(2))
+            for lo, hi in low_parts:
+                nc.vector.tensor_tensor(pairs[:, lo:hi], left[:, lo:hi], right[:, lo:hi], ALU.min)
+            for x in range(2):
+                nc.sync.dma_start(
+                    out=halves[u * HALF : (u + 1) * HALF, x, :].bitcast(I32),
+                    in_=pairs[x:P:2].rearrange("p j e -> p (j e)").bitcast(I32),
+                )
+
+        spread_g(0, J)
+        gather_words(0, 0, S)
+        rounded = rounded_tile("w1_bf000")
+        round_low(nc.scalar.copy, rounded, 0, 0)
+        quantize_w1(rounded, 0, 0, 0)
+        for t in (0, 1):
+            first_product(0, 0, t)
+        spread_g(1, widest)
+        gather_words(1, 0, EARLY)
+        prepare_plane(1, 0)
+        gather_words(1, EARLY, S, "w1_plane10")
+        first_product(0, 1, 0)
+        prepare_plane(1, 1)
+        first_product(0, 1, 1)
+        rounded = rounded_tile("w1_bf010")
+        round_low(nc.vector.tensor_copy, rounded, 1, 0)
+        quantize_w1(rounded, 0, 1, 0)
+        sigmoid(0, 0)
+        fetch_low(0, 0, 0, "w1_raw0_256")
+        fetch_low(0, 0, 1)
+        rounded = rounded_tile("w1_bf011")
+        round_low(nc.scalar.copy, rounded, 1, 1)
+        quantize_w1(rounded, 0, 1, 1)
+        for a in range(2):
+            for t in (2, 3):
+                first_product(0, a, t)
+        sigmoid(0, 1, "w1_raw1_256")
+        fetch_low(0, 1, 0)
+        fetch_low(0, 1, 1)
+        overlap_low(0)
+
+        def prepare_high(u, a):
+            rounded = rounded_tile("w1_bf1%d%d" % (a, u))
+            round_high(rounded, u, a)
+            quantize_w1(rounded, 1, u, a)
+
+        prepare_high(0, 0)
+        sigmoid(0, 2)
+        fetch_low(1, 0, 0)
+        prepare_high(0, 1)
+        fetch_low(1, 0, 1, "w1_bf110")
+        for a in range(2):
+            for t in (0, 1):
+                first_product(1, a, t)
+        sigmoid(0, 3)
+        fetch_low(1, 1, 0)
+        fetch_low(1, 1, 1)
+        overlap_low(1)
+        prepare_high(1, 0)
+        prepare_high(1, 1)
+        sigmoid(1, 0, "w1_raw1_512")
+        sigmoid(1, 1)
+        high_sides = [tile([P, PACK * widest], F32, "high_side%d" % side) for side in range(2)]
+        for t in (2, 3):
+            first_product(1, 0, t)
             first_product(1, 1, t)
             sigmoid(1, t)
-        overlap(pair, 0, 0, ((0, J // 2), (J // 2, J)))
+
+        z_low = tile([P, J, PACK], BF16, "z_low", "w1_w112")
+        nc.scalar.copy(
+            z_low[:].rearrange("p j t -> p (j t)").bitcast(U32).rearrange("p (j x) -> p j x", x=2),
+            halves[:].bitcast(U32).rearrange("p x j -> p j x"),
+        )
+        quantize_z(z_low, 0, 0, 0, J)
 
         out_rows = out.rearrange("(t p) j -> p t j", p=P)
         for c, (j0, n) in enumerate(CHUNKS):
             parts = ((0, 256), (256, n)) if n > 256 else ((0, n // 2), (n // 2, n))
-            pair = sides(1, j0, n)
+            pair = [side[:, 0 : PACK * n].rearrange("p (t j) -> p t j", t=PACK) for side in high_sides]
             y = [psum.tile([P, n], F32, name="bank%d" % (4 * c + nt)) for nt in range(N // P)]
             for nt in range(N // P):
                 for jj in range(0, n, N_MX):
                     second_product(y[nt], 0, nt, j0, jj)
             for t in range(PACK):
-                fetch(pair, 1, t, j0, n, parts if t == PACK - 1 else None)
-            overlap(pair, 1, j0, parts)
+                for side in range(2):
+                    for lo, hi in parts if t == PACK - 1 and side == 1 else ((0, n),):
+                        fetch(pair[side][:, t, lo:hi], side, 1, t, j0, lo, hi)
+            z_bf = tile([P, n, PACK], BF16, "z_bf%d" % c)
+            for lo, hi in parts:
+                left, right = (side[:, :, lo:hi].rearrange("p t (c i) -> p c t i", i=4) for side in pair)
+                nc.vector.tensor_tensor(
+                    z_bf[:, lo:hi, :].rearrange("p (c i) t -> p c t i", i=4), left, right, ALU.min
+                )
+            for lo, hi in parts:
+                quantize_z(z_bf, 1, j0, lo, hi)
             res = tile([P, N // P, n], F32, "res%d" % c)
             for nt in range(N // P):
                 for jj in range(0, n, N_MX):

@@ -120,10 +120,11 @@ def tile_list_join_sketch_cardinality_kernel(
             nc.vector.quantize_mx(out=words[:].bitcast(FP8X4), scales=scales[:], in_=rounded[:])
             w1_w[0, a, e], w1_s[0, a, e] = words[:], scales[:]
 
-        def round_high(rounded, u, a):
-            dst = rounded.rearrange("p (e m j) -> p m j e", e=2, j=PACK)
-            src = high_raw[a][:].rearrange("p j (m u e) -> p u m j e", u=2, e=2)[:, u]
-            nc.scalar.copy(dst, src)
+        def prepare_high(a):
+            rounded = tile([P, PACK * PASS], BF16, "w1_bf1%d" % a)
+            dst = rounded[:].rearrange("p (t m j) -> p m j t", t=PACK, j=PACK)
+            nc.scalar.copy(dst, high_raw[a][:].rearrange("p j (m t) -> p m j t", t=PACK))
+            quantize_w1(rounded[:], 1, 0, a, ((0, PACK),))
 
         def quantize_w1(rounded, b, u, a, parts=((0, 2),)):
             for e0, e1 in parts:
@@ -197,6 +198,7 @@ def tile_list_join_sketch_cardinality_kernel(
             )
 
         low_sides = {}
+        planes = {}
         halves = tile([P, 2, 2 * J], BF16, "halves")
 
         low_parts = ((0, J // 2), (J // 2, J))
@@ -204,18 +206,28 @@ def tile_list_join_sketch_cardinality_kernel(
         def fetch_low(u, e, side, tag=None):
             if e == 0:
                 low_sides[u, side] = tile([P, 2, J], F32, "low_side%d%d" % (u, side), tag)
-            for lo, hi in low_parts if e == 1 and side == 1 else ((0, J),):
-                fetch(low_sides[u, side][:, e, lo:hi], side, 0, 2 * u + e, 0, lo, hi)
+            if side == 0:
+                nc.vector.tensor_copy(low_sides[u, 0][:, e, :], h[0, 2 * u + e][:].indirect(pos_sb[0][:]))
+                return
+            if e == 0:
+                planes[u] = tile([P, 2, J], BF16, "planes%d" % u)
+            for lo, hi in low_parts:
+                fetch(low_sides[u, 1][:, e, lo:hi], 1, 0, 2 * u + e, 0, lo, hi)
+            for lo, hi in low_parts:
+                nc.vector.scalar_tensor_tensor(
+                    out=planes[u][:, e, lo:hi],
+                    in0=low_sides[u, 0][:, e, lo:hi],
+                    scalar=g_low[:, u, e : e + 1],
+                    in1=low_sides[u, 1][:, e, lo:hi],
+                    op0=ALU.mult,
+                    op1=ALU.min,
+                )
 
         def overlap_low(u):
-            pairs = tile([P, J, 2], BF16, "pairs%d" % u)
-            left, right = (low_sides[u, side][:].rearrange("p e j -> p j e") for side in range(2))
-            for lo, hi in low_parts:
-                nc.vector.tensor_tensor(pairs[:, lo:hi], left[:, lo:hi], right[:, lo:hi], ALU.min)
             for x in range(2):
                 nc.sync.dma_start(
                     out=halves[u * HALF : (u + 1) * HALF, x, :].bitcast(I32),
-                    in_=pairs[x:P:2].rearrange("p j e -> p (j e)").bitcast(I32),
+                    in_=planes[u][x:P:2].rearrange("p e j -> p (e j)").bitcast(I32),
                 )
 
         spread_g(0, J)
@@ -236,8 +248,8 @@ def tile_list_join_sketch_cardinality_kernel(
         round_low(nc.vector.tensor_copy, rounded, 1, 0)
         quantize_w1(rounded, 0, 1, 0)
         sigmoid(0, 0)
-        fetch_low(0, 0, 0, "w1_raw0_256")
-        fetch_low(0, 0, 1)
+        fetch_low(0, 0, 0)
+        fetch_low(0, 0, 1, "w1_raw0_256")
         rounded = rounded_tile("w1_bf011")
         round_low(nc.scalar.copy, rounded, 1, 1)
         quantize_w1(rounded, 0, 1, 1)
@@ -249,38 +261,23 @@ def tile_list_join_sketch_cardinality_kernel(
         fetch_low(0, 1, 1)
         overlap_low(0)
 
-        def prepare_high(u, a):
-            rounded = rounded_tile("w1_bf1%d%d" % (a, u))
-            round_high(rounded, u, a)
-            quantize_w1(rounded, 1, u, a)
-
-        prepare_high(0, 0)
-        sigmoid(0, 2)
+        prepare_high(0)
+        sigmoid(0, 2, "w1_raw0_512")
         fetch_low(1, 0, 0)
-        prepare_high(0, 1)
-        fetch_low(1, 0, 1, "w1_bf110")
-        for a in range(2):
-            for t in (0, 1):
-                first_product(1, a, t)
-        sigmoid(0, 3)
+        fetch_low(1, 0, 1)
+        prepare_high(1)
+        sigmoid(0, 3, "w1_raw1_512")
         fetch_low(1, 1, 0)
         fetch_low(1, 1, 1)
         overlap_low(1)
-        prepare_high(1, 0)
-        prepare_high(1, 1)
-        sigmoid(1, 0, "w1_raw1_512")
-        sigmoid(1, 1)
         high_sides = [tile([P, PACK * widest], F32, "high_side%d" % side) for side in range(2)]
-        for t in (2, 3):
+        for t in range(PACK):
             first_product(1, 0, t)
             first_product(1, 1, t)
             sigmoid(1, t)
 
-        z_low = tile([P, J, PACK], BF16, "z_low", "w1_w112")
-        nc.scalar.copy(
-            z_low[:].rearrange("p j t -> p (j t)").bitcast(U32).rearrange("p (j x) -> p j x", x=2),
-            halves[:].bitcast(U32).rearrange("p x j -> p j x"),
-        )
+        z_low = tile([P, J, PACK], BF16, "z_low", "w1_w110")
+        nc.scalar.copy(z_low[:], halves[:].rearrange("p x (e j) -> p j (x e)", e=2))
         quantize_z(z_low, 0, 0, 0, J)
 
         out_rows = out.rearrange("(t p) j -> p t j", p=P)
@@ -293,9 +290,9 @@ def tile_list_join_sketch_cardinality_kernel(
                     second_product(y[nt], 0, nt, j0, jj)
             for t in range(PACK):
                 for side in range(2):
-                    for lo, hi in parts if t == PACK - 1 and side == 1 else ((0, n),):
+                    for lo, hi in parts if c == 1 and t == PACK - 1 and side == 1 else ((0, n),):
                         fetch(pair[side][:, t, lo:hi], side, 1, t, j0, lo, hi)
-            z_bf = tile([P, n, PACK], BF16, "z_bf%d" % c)
+            z_bf = tile([P, n, PACK], BF16, "z_bf%d" % c, "halves" if c == 0 else None)
             for lo, hi in parts:
                 left, right = (side[:, :, lo:hi].rearrange("p t (c i) -> p c t i", i=4) for side in pair)
                 nc.vector.tensor_tensor(

@@ -204,21 +204,20 @@ def tile_list_join_sketch_cardinality_kernel(
         low_parts = ((0, J // 2), (J // 2, J))
 
         def fetch_low(u, e, side, tag=None):
-            if e == 0:
-                low_sides[u, side] = tile([P, 2, J], F32, "low_side%d%d" % (u, side), tag)
             if side == 0:
-                nc.vector.tensor_copy(low_sides[u, 0][:, e, :], h[0, 2 * u + e][:].indirect(pos_sb[0][:]))
+                low_sides[u, e] = tile([P, 2, J], F32, "low_sides%d%d" % (u, e), tag)
+                nc.vector.tensor_copy(low_sides[u, e][:, 0, :], h[0, 2 * u + e][:].indirect(pos_sb[0][:]))
                 return
             if e == 0:
                 planes[u] = tile([P, 2, J], BF16, "planes%d" % u)
             for lo, hi in low_parts:
-                fetch(low_sides[u, 1][:, e, lo:hi], 1, 0, 2 * u + e, 0, lo, hi)
+                fetch(low_sides[u, e][:, 1, lo:hi], 1, 0, 2 * u + e, 0, lo, hi)
             for lo, hi in low_parts:
                 nc.vector.scalar_tensor_tensor(
                     out=planes[u][:, e, lo:hi],
-                    in0=low_sides[u, 0][:, e, lo:hi],
+                    in0=low_sides[u, e][:, 0, lo:hi],
                     scalar=g_low[:, u, e : e + 1],
-                    in1=low_sides[u, 1][:, e, lo:hi],
+                    in1=low_sides[u, e][:, 1, lo:hi],
                     op0=ALU.mult,
                     op1=ALU.min,
                 )
@@ -248,8 +247,8 @@ def tile_list_join_sketch_cardinality_kernel(
         round_low(nc.vector.tensor_copy, rounded, 1, 0)
         quantize_w1(rounded, 0, 1, 0)
         sigmoid(0, 0)
-        fetch_low(0, 0, 0)
-        fetch_low(0, 0, 1, "w1_raw0_256")
+        fetch_low(0, 0, 0, "w1_raw0_256")
+        fetch_low(0, 0, 1)
         rounded = rounded_tile("w1_bf011")
         round_low(nc.scalar.copy, rounded, 1, 1)
         quantize_w1(rounded, 0, 1, 1)

@@ -34,11 +34,19 @@ def tile_list_join_sketch_cardinality_kernel(
 ):
     nc = tc.nc
     with ExitStack() as ctx:
+        windows = ctx.enter_context(tc.tile_pool(name="windows", bufs=1))
         keep = ctx.enter_context(tc.tile_pool(name="keep", bufs=1))
+        picks = ctx.enter_context(tc.tile_pool(name="picks", bufs=1))
         psum = ctx.enter_context(tc.psum_pool(name="psum", bufs=1))
 
         def tile(shape, dtype, name, tag=None):
-            return keep.tile(shape, dtype, name=name, tag=tag or name, align_bytes=64)
+            tag = tag or name
+            pool = keep
+            if tag.startswith(("tab_", "h0", "h1", "w1_raw1_256", "w1_raw0_512", "w1_raw1_512")):
+                pool = windows
+            if tag.startswith(("v_", "low_sides", "high_side", "w1_raw0_256", "w1_plane10")):
+                pool = picks
+            return pool.tile(shape, dtype, name=name, tag=tag, align_bytes=64)
 
         offs_sb = keep.tile([P, S // LIST_ROWS], U16, name="offs_sb")
         pos_sb = [keep.tile([P, J // LIST_ROWS], U16, name="pos%d_sb" % side) for side in range(2)]

@@ -25,6 +25,7 @@ LIST_ROWS = 16
 CHUNKS = ((0, 384), (384, 128))
 N_MX = 128
 EARLY = 768
+SLOT = 4 * T
 
 FLOPS = 2 * K * H * S + 2 * H * N * J
 
@@ -34,78 +35,72 @@ def tile_list_join_sketch_cardinality_kernel(
 ):
     nc = tc.nc
     with ExitStack() as ctx:
-        windows = ctx.enter_context(tc.tile_pool(name="windows", bufs=1))
         keep = ctx.enter_context(tc.tile_pool(name="keep", bufs=1))
-        picks = ctx.enter_context(tc.tile_pool(name="picks", bufs=1))
+        shared = ctx.enter_context(tc.tile_pool(name="shared", bufs=1))
         psum = ctx.enter_context(tc.psum_pool(name="psum", bufs=1))
 
-        def tile(shape, dtype, name, tag=None):
-            tag = tag or name
-            pool = keep
-            if tag.startswith(("tab_", "h0", "h1", "w1_raw1_256", "w1_raw0_512", "w1_raw1_512")):
-                pool = windows
-            if tag.startswith(("v_", "low_sides", "high_side", "w1_raw0_256", "w1_plane10")):
-                pool = picks
-            return pool.tile(shape, dtype, name=name, tag=tag, align_bytes=64)
+        def tile(shape, dtype, name, tag=None, at=None):
+            if at is not None:
+                return shared.tile(shape, dtype, name=name, offset=at, align_bytes=64)
+            return keep.tile(shape, dtype, name=name, tag=tag or name, align_bytes=64)
 
         offs_sb = keep.tile([P, S // LIST_ROWS], U16, name="offs_sb")
         pos_sb = [keep.tile([P, J // LIST_ROWS], U16, name="pos%d_sb" % side) for side in range(2)]
         tab_w = [tile([P, T], I32, "tab_w%d" % a) for a in range(2)]
-        tab_s = tile([P, T // 4], I32, "tab_s")
-        w2_w = tile([P, 2, 2 * N], U8, "w2_w")
-        w2_s = tile([P, 2, N], U8, "w2_s")
+        tab_s = tile([P, T // 4], I32, "tab_s", at=2 * SLOT + 3 * S)
         g_low = tile([P, 2, 2], F32, "g_low")
         g_high = tile([P, PACK], F32, "g_high")
-        b2_sb = tile([P, N // P], F32, "b2_sb")
+        planes_s = [tile([P, S], U8, "planes_s0")]
 
-        nc.vector.memset(tab_s[:], 0)
-        nc.gpsimd.memset(w2_s[:].bitcast(I32), 0)
+        nc.vector.memset(tab_s[32:64, :], 0)
+        nc.vector.memset(tab_s[64:P, :], 0)
+        nc.gpsimd.memset(planes_s[0][:].bitcast(I32), 0)
 
-        def load_w1(a, c0, width):
-            raw = tile([P, PACK, width], F32, "w1_raw%d_%d" % (a, c0))
+        def load_w1(a, c0, width, at=None):
+            raw = tile([P, PACK, width], F32, "w1_raw%d_%d" % (a, c0), at=at)
             rows = w1[a * PASS : (a + 1) * PASS, c0 : c0 + width]
             nc.sync.dma_start(out=raw[:], in_=rows.rearrange("(p j) c -> p j c", j=PACK))
             return raw
 
         nc.sync.dma_start(offs_sb[:], offs)
-        nc.sync.dma_start(out=g_low[:], in_=g[0:PASS].rearrange("(u p e) -> p u e", u=2, e=2))
-        for q in range(4):
-            nc.sync.dma_start(
-                out=tab_s[32 * q : 32 * q + 8, :], in_=tab_scales[:, 4 * q : 4 * q + 4, :].bitcast(I32)
-            )
+        nc.scalar.dma_start(out=g_low[:], in_=g[0:PASS].rearrange("(u p e) -> p u e", u=2, e=2))
+        nc.scalar.dma_start(out=g_high[:], in_=g[PASS:H].rearrange("(p t) -> p t", t=PACK))
+        nc.sync.dma_start(out=tab_s[0:32, :], in_=tab_scales.rearrange("a q c -> (a q) c").bitcast(I32))
         words = [tab_words[a].rearrange("p n t -> p (n t)").bitcast(I32) for a in range(2)]
         nc.sync.dma_start(out=tab_w[0][:], in_=words[0])
-        low_raw = {(0, 0): load_w1(0, 0, QUARTER)}
-        nc.sync.dma_start(out=g_high[:], in_=g[PASS:H].rearrange("(p t) -> p t", t=PACK))
+        low_raw = {(0, 0): load_w1(0, 0, QUARTER, at=4 * SLOT)}
         nc.sync.dma_start(out=tab_w[1][:], in_=words[1])
         low_raw[0, 1] = load_w1(1, 0, QUARTER)
-        nc.sync.dma_start(pos_sb[0][:], pos1)
-        nc.sync.dma_start(pos_sb[1][:], pos2)
-        low_raw.update({(1, a): load_w1(a, QUARTER, QUARTER) for a in range(2)})
-        high_raw = [load_w1(a, PASS, PASS) for a in range(2)]
-        nc.sync.dma_start(out=w2_w[:].bitcast(I32), in_=w2_words.rearrange("a p c -> p a c").bitcast(I32))
-        for q in range(4):
-            nc.sync.dma_start(
-                out=w2_s[32 * q : 32 * q + 4, :, :].bitcast(I32),
-                in_=w2_scales[:, 4 * q : 4 * q + 4, :].rearrange("a q c -> q a c").bitcast(I32),
-            )
-        with nc.allow_non_contiguous_dma(reason="one bias value a partition"):
-            nc.sync.dma_start(out=b2_sb[:], in_=b2.rearrange("(t p) -> p t", p=P))
 
-        warm = tile([P, 1], F32, "warm")
-        nc.scalar.activation(warm[:], g_low[:, 0, 0:1], ACT.Sigmoid)
+        warm = tile([P, 2], F32, "warm")
+        nc.vector.memset(warm[:, 0:1], 0.0)
+        nc.scalar.activation(warm[:, 1:2], warm[:, 0:1], ACT.Sigmoid)
 
         widest = max(n for j0, n in CHUNKS)
         g_wide = {}
         g_rows = [g_low[:].rearrange("p u e -> p (u e)"), g_high[:]]
 
-        def spread_g(b, width, tag=None):
-            g_wide[b] = tile([P, PACK, width], F32, "g_wide%d" % b, tag)
+        def spread_g(b, width, at=None):
+            g_wide[b] = tile([P, PACK, width], F32, "g_wide%d" % b, at=at)
             nc.scalar.activation(g_wide[b][:], g_rows[b].unsqueeze(2).to_broadcast([P, PACK, width]), ACT.Copy)
 
-        v_w = {}
+        spread_g(0, J // 2)
         v_s = tile([P, S], U8, "v_s")
         nc.vector.tensor_copy(v_s[:], tab_s[:].bitcast(U8).indirect(offs_sb[:]))
+
+        def carry_scales(queue, a):
+            for q in range(4):
+                rows = slice(16 * a + 4 * q, 16 * a + 4 * q + 4)
+                queue.dma_start(out=planes_s[a][32 * q : 32 * q + 4, :].bitcast(I32), in_=v_s[rows, :].bitcast(I32))
+
+        carry_scales(nc.scalar, 0)
+        planes_s.append(tile([P, S], U8, "planes_s1", at=2 * SLOT + 4 * S))
+        nc.vector.memset(planes_s[1][:].bitcast(I32), 0)
+        carry_scales(nc.sync, 1)
+        nc.sync.dma_start(pos_sb[0][:], pos1)
+        nc.sync.dma_start(pos_sb[1][:], pos2)
+
+        v_w = {}
 
         def gather_words(a, lo, hi, tag=None):
             picked = tile([P, hi - lo], U32, "v_w%d_%d" % (a, lo), tag)
@@ -169,19 +164,19 @@ def tile_list_join_sketch_cardinality_kernel(
                             lhsT=w1_w[b, a, t].bitcast(FP8X4),
                             lhsT_scale=w1_s[b, a, t],
                             rhs=picked[:, first - lo : last - lo].bitcast(FP8X4),
-                            rhs_scale=v_s[4 * a : P, first:last],
+                            rhs_scale=planes_s[a][:, first:last],
                             start=(a == 0),
                             stop=(a == 1 and last == c1),
                         )
 
-        def sigmoid(b, t, tag=None):
-            h[b, t] = tile([P, S], F32, "h%d%d" % (b, t), tag)
+        def sigmoid(b, t, at=None):
+            h[b, t] = tile([P, S], F32, "h%d%d" % (b, t), at=at)
             for c0, c1 in spans(b, t):
                 nc.scalar.activation(h[b, t][:, c0:c1], acc[t, c0][:], ACT.Sigmoid)
 
         def fetch(dst, side, b, t, j0, lo, hi):
             entries = pos_sb[side][:, (j0 + lo) // LIST_ROWS : (j0 + hi) // LIST_ROWS]
-            nc.vector.tensor_tensor(dst, h[b, t][:].indirect(entries), g_wide[b][:, t, lo:hi], ALU.mult)
+            nc.vector.tensor_tensor(dst, h[b, t][:].indirect(entries), g_wide[b][:, t, 0 : hi - lo], ALU.mult)
 
         z_w = [tile([P, J], U32, "z_w%d" % b) for b in range(2)]
         z_s = [tile([P, J], U8, "z_s%d" % b) for b in range(2)]
@@ -198,7 +193,7 @@ def tile_list_join_sketch_cardinality_kernel(
             nc.tensor.matmul_mx(
                 out=y[:, jj : jj + N_MX],
                 lhsT=w2_w[:, b, 2 * nt * P : 2 * (nt + 1) * P].bitcast(FP4X4),
-                lhsT_scale=w2_s[:, b, nt * P : (nt + 1) * P],
+                lhsT_scale=planes_s[0][:, b * N + nt * P : b * N + (nt + 1) * P],
                 rhs=z_w[b][:, cols].bitcast(FP8X4),
                 rhs_scale=z_s[b][:, cols],
                 start=(b == 0 and jj == 0),
@@ -211,9 +206,9 @@ def tile_list_join_sketch_cardinality_kernel(
 
         low_parts = ((0, J // 2), (J // 2, J))
 
-        def fetch_low(u, e, side, tag=None):
+        def fetch_low(u, e, side, at=None):
             if side == 0:
-                low_sides[u, e] = tile([P, 2, J], F32, "low_sides%d%d" % (u, e), tag)
+                low_sides[u, e] = tile([P, 2, J], F32, "low_sides%d%d" % (u, e), at=at)
                 nc.vector.tensor_copy(low_sides[u, e][:, 0, :], h[0, 2 * u + e][:].indirect(pos_sb[0][:]))
                 return
             if e == 0:
@@ -237,43 +232,49 @@ def tile_list_join_sketch_cardinality_kernel(
                     in_=planes[u][x:P:2].rearrange("p e j -> p (e j)").bitcast(I32),
                 )
 
-        spread_g(0, J)
         gather_words(0, 0, S)
+        low_raw.update({(1, a): load_w1(a, QUARTER, QUARTER, at=a * SLOT // 2) for a in range(2)})
         rounded = rounded_tile("w1_bf000")
         round_low(nc.scalar.copy, rounded, 0, 0)
+        spread_g(1, widest, 4 * SLOT)
         quantize_w1(rounded, 0, 0, 0)
         for t in (0, 1):
             first_product(0, 0, t)
-        spread_g(1, widest)
         gather_words(1, 0, EARLY)
         prepare_plane(1, 0)
         gather_words(1, EARLY, S, "w1_plane10")
         first_product(0, 1, 0)
         prepare_plane(1, 1)
         first_product(0, 1, 1)
+        high_raw = [load_w1(a, PASS, PASS, at=(a + 1) * SLOT + a * 5 * S) for a in range(2)]
         rounded = rounded_tile("w1_bf010")
         round_low(nc.vector.tensor_copy, rounded, 1, 0)
         quantize_w1(rounded, 0, 1, 0)
+        w2_w = tile([P, 2, 2 * N], U8, "w2_w")
+        nc.sync.dma_start(out=w2_w[:].bitcast(I32), in_=w2_words.rearrange("a p c -> p a c").bitcast(I32))
         sigmoid(0, 0)
-        fetch_low(0, 0, 0, "w1_raw0_256")
+        fetch_low(0, 0, 0, 0)
         fetch_low(0, 0, 1)
         rounded = rounded_tile("w1_bf011")
         round_low(nc.scalar.copy, rounded, 1, 1)
         quantize_w1(rounded, 0, 1, 1)
+        b2_sb = tile([P, N // P], F32, "b2_sb")
+        with nc.allow_non_contiguous_dma(reason="one bias value a partition"):
+            nc.sync.dma_start(out=b2_sb[:], in_=b2.rearrange("(t p) -> p t", p=P))
         for a in range(2):
             for t in (2, 3):
                 first_product(0, a, t)
-        sigmoid(0, 1, "w1_raw1_256")
+        sigmoid(0, 1, SLOT // 2)
         fetch_low(0, 1, 0)
         fetch_low(0, 1, 1)
         overlap_low(0)
 
         prepare_high(0)
-        sigmoid(0, 2, "w1_raw0_512")
+        sigmoid(0, 2, SLOT)
         fetch_low(1, 0, 0)
         fetch_low(1, 0, 1)
         prepare_high(1)
-        sigmoid(0, 3, "w1_raw1_512")
+        sigmoid(0, 3, 2 * SLOT + 5 * S)
         fetch_low(1, 1, 0)
         fetch_low(1, 1, 1)
         overlap_low(1)
@@ -282,6 +283,11 @@ def tile_list_join_sketch_cardinality_kernel(
             first_product(1, 0, t)
             first_product(1, 1, t)
             sigmoid(1, t)
+        for q in range(4):
+            nc.sync.dma_start(
+                out=planes_s[0][32 * q : 32 * q + 4, :].bitcast(I32).rearrange("q (a c) -> q a c", a=2),
+                in_=w2_scales[:, 4 * q : 4 * q + 4, :].rearrange("a q c -> q a c").bitcast(I32),
+            )
 
         z_low = tile([P, J, PACK], BF16, "z_low", "w1_w110")
         nc.scalar.copy(z_low[:], halves[:].rearrange("p x (e j) -> p j (x e)", e=2))

@@ -68,9 +68,8 @@ def tile_list_join_sketch_cardinality_kernel(
         nc.sync.dma_start(out=tab_s[0:32, :], in_=tab_scales.rearrange("a q c -> (a q) c").bitcast(I32))
         words = [tab_words[a].rearrange("p n t -> p (n t)").bitcast(I32) for a in range(2)]
         nc.sync.dma_start(out=tab_w[0][:], in_=words[0])
-        low_raw = {(0, 0): load_w1(0, 0, QUARTER, at=4 * SLOT)}
+        low_raw = {(0, 0): load_w1(0, 0, QUARTER)}
         nc.sync.dma_start(out=tab_w[1][:], in_=words[1])
-        low_raw[0, 1] = load_w1(1, 0, QUARTER)
 
         warm = tile([P, 2], F32, "warm")
         nc.vector.memset(warm[:, 0:1], 0.0)
@@ -85,6 +84,7 @@ def tile_list_join_sketch_cardinality_kernel(
             nc.scalar.activation(g_wide[b][:], g_rows[b].unsqueeze(2).to_broadcast([P, PACK, width]), ACT.Copy)
 
         spread_g(0, J // 2)
+        spread_g(1, widest)
         v_s = tile([P, S], U8, "v_s")
         nc.vector.tensor_copy(v_s[:], tab_s[:].bitcast(U8).indirect(offs_sb[:]))
 
@@ -93,12 +93,16 @@ def tile_list_join_sketch_cardinality_kernel(
                 rows = slice(16 * a + 4 * q, 16 * a + 4 * q + 4)
                 queue.dma_start(out=planes_s[a][32 * q : 32 * q + 4, :].bitcast(I32), in_=v_s[rows, :].bitcast(I32))
 
-        carry_scales(nc.scalar, 0)
+        carry_scales(nc.sync, 0)
+        low_raw[0, 1] = load_w1(1, 0, QUARTER)
         planes_s.append(tile([P, S], U8, "planes_s1", at=2 * SLOT + 4 * S))
         nc.vector.memset(planes_s[1][:].bitcast(I32), 0)
         carry_scales(nc.sync, 1)
+        low_raw[1, 0] = load_w1(0, QUARTER, QUARTER, at=0)
         nc.sync.dma_start(pos_sb[0][:], pos1)
         nc.sync.dma_start(pos_sb[1][:], pos2)
+        low_raw[1, 1] = load_w1(1, QUARTER, QUARTER, at=SLOT // 2)
+        high_raw = [load_w1(a, PASS, PASS, at=SLOT + a * 3 * SLOT) for a in range(2)]
 
         v_w = {}
 
@@ -233,10 +237,8 @@ def tile_list_join_sketch_cardinality_kernel(
                 )
 
         gather_words(0, 0, S)
-        low_raw.update({(1, a): load_w1(a, QUARTER, QUARTER, at=a * SLOT // 2) for a in range(2)})
         rounded = rounded_tile("w1_bf000")
         round_low(nc.scalar.copy, rounded, 0, 0)
-        spread_g(1, widest, 4 * SLOT)
         quantize_w1(rounded, 0, 0, 0)
         for t in (0, 1):
             first_product(0, 0, t)
@@ -246,7 +248,6 @@ def tile_list_join_sketch_cardinality_kernel(
         first_product(0, 1, 0)
         prepare_plane(1, 1)
         first_product(0, 1, 1)
-        high_raw = [load_w1(a, PASS, PASS, at=(a + 1) * SLOT + a * 5 * S) for a in range(2)]
         rounded = rounded_tile("w1_bf010")
         round_low(nc.vector.tensor_copy, rounded, 1, 0)
         quantize_w1(rounded, 0, 1, 0)
@@ -274,7 +275,7 @@ def tile_list_join_sketch_cardinality_kernel(
         fetch_low(1, 0, 0)
         fetch_low(1, 0, 1)
         prepare_high(1)
-        sigmoid(0, 3, 2 * SLOT + 5 * S)
+        sigmoid(0, 3, 4 * SLOT)
         fetch_low(1, 1, 0)
         fetch_low(1, 1, 1)
         overlap_low(1)

@@ -1,6 +1,7 @@
 from contextlib import ExitStack
 
 import concourse.mybir as mybir
+from concourse.masks import make_identity
 
 K, H, N, T, S, J = 1024, 1024, 512, 2048, 1024, 512
 
@@ -26,6 +27,8 @@ CHUNKS = ((0, 384), (384, 128))
 N_MX = 128
 EARLY = 768
 SLOT = 4 * T
+PARK = 96
+DIRECT = 256
 
 FLOPS = 2 * K * H * S + 2 * H * N * J
 
@@ -47,14 +50,17 @@ def tile_list_join_sketch_cardinality_kernel(
         offs_sb = keep.tile([P, S // LIST_ROWS], U16, name="offs_sb")
         pos_sb = [keep.tile([P, J // LIST_ROWS], U16, name="pos%d_sb" % side) for side in range(2)]
         tab_w = [tile([P, T], I32, "tab_w%d" % a) for a in range(2)]
-        tab_s = tile([P, T // 4], I32, "tab_s", at=2 * SLOT + 3 * S)
+        tab_s = tile([P, T // 4], I32, "tab_s")
         g_low = tile([P, 2, 2], F32, "g_low")
         g_high = tile([P, PACK], F32, "g_high")
-        planes_s = [tile([P, S], U8, "planes_s0")]
+        both_planes = tile([P, 2 * S], U8, "both_planes")
+        planes_s = [both_planes[:, a * S : (a + 1) * S] for a in range(2)]
 
-        nc.vector.memset(tab_s[32:64, :], 0)
-        nc.vector.memset(tab_s[64:P, :], 0)
-        nc.gpsimd.memset(planes_s[0][:].bitcast(I32), 0)
+        nc.vector.memset(tab_s[0:PARK, :], 0)
+        nc.vector.memset(both_planes[:].bitcast(I32), 0)
+
+        identity = tile([P, P], F32, "identity")
+        make_identity(nc, identity[:])
 
         def load_w1(a, c0, width, at=None):
             raw = tile([P, PACK, width], F32, "w1_raw%d_%d" % (a, c0), at=at)
@@ -65,10 +71,10 @@ def tile_list_join_sketch_cardinality_kernel(
         nc.sync.dma_start(offs_sb[:], offs)
         nc.scalar.dma_start(out=g_low[:], in_=g[0:PASS].rearrange("(u p e) -> p u e", u=2, e=2))
         nc.scalar.dma_start(out=g_high[:], in_=g[PASS:H].rearrange("(p t) -> p t", t=PACK))
-        nc.sync.dma_start(out=tab_s[0:32, :], in_=tab_scales.rearrange("a q c -> (a q) c").bitcast(I32))
+        nc.sync.dma_start(out=tab_s[PARK:P, :], in_=tab_scales.rearrange("a q c -> (a q) c").bitcast(I32))
         words = [tab_words[a].rearrange("p n t -> p (n t)").bitcast(I32) for a in range(2)]
         nc.sync.dma_start(out=tab_w[0][:], in_=words[0])
-        low_raw = {(0, 0): load_w1(0, 0, QUARTER)}
+        low_raw = {(0, 0): load_w1(0, 0, QUARTER, at=3 * SLOT)}
         nc.sync.dma_start(out=tab_w[1][:], in_=words[1])
 
         warm = tile([P, 2], F32, "warm")
@@ -90,19 +96,17 @@ def tile_list_join_sketch_cardinality_kernel(
 
         def carry_scales(queue, a):
             for q in range(4):
-                rows = slice(16 * a + 4 * q, 16 * a + 4 * q + 4)
+                rows = slice(PARK + 16 * a + 4 * q, PARK + 16 * a + 4 * q + 4)
                 queue.dma_start(out=planes_s[a][32 * q : 32 * q + 4, :].bitcast(I32), in_=v_s[rows, :].bitcast(I32))
 
         carry_scales(nc.sync, 0)
         low_raw[0, 1] = load_w1(1, 0, QUARTER)
-        planes_s.append(tile([P, S], U8, "planes_s1", at=2 * SLOT + 4 * S))
-        nc.vector.memset(planes_s[1][:].bitcast(I32), 0)
         carry_scales(nc.sync, 1)
         low_raw[1, 0] = load_w1(0, QUARTER, QUARTER, at=0)
         nc.sync.dma_start(pos_sb[0][:], pos1)
         nc.sync.dma_start(pos_sb[1][:], pos2)
         low_raw[1, 1] = load_w1(1, QUARTER, QUARTER, at=SLOT // 2)
-        high_raw = [load_w1(a, PASS, PASS, at=SLOT + a * 3 * SLOT) for a in range(2)]
+        high_raw = [load_w1(a, PASS, PASS, at=(a + 1) * SLOT) for a in range(2)]
 
         v_w = {}
 
@@ -150,7 +154,7 @@ def tile_list_join_sketch_cardinality_kernel(
 
         h = {}
         acc = {}
-        banks = (((0, 1, 6), (2, 3), (4, 5), (6, 7)), ((0, 1), (2, 3), (4, 5), (6, 7)))
+        banks = (((0, 1, 4), (2, 3), (0, 1), (2, 3)), ((0, 1), (2, 3), (0, 1), (2, 3)))
 
         def spans(b, t):
             edges = (0, BANK, EARLY, S) if len(banks[b][t]) == 3 else (0, BANK, S)
@@ -206,28 +210,39 @@ def tile_list_join_sketch_cardinality_kernel(
 
         low_sides = {}
         planes = {}
-        halves = tile([P, 2, 2 * J], BF16, "halves")
+        halves = tile([P, 2, 2 * DIRECT], BF16, "halves")
+        turned = range(DIRECT, J, P)
+        differences, negatives = {}, {}
 
-        low_parts = ((0, J // 2), (J // 2, J))
-
-        def fetch_low(u, e, side, at=None):
-            if side == 0:
-                low_sides[u, e] = tile([P, 2, J], F32, "low_sides%d%d" % (u, e), at=at)
-                nc.vector.tensor_copy(low_sides[u, e][:, 0, :], h[0, 2 * u + e][:].indirect(pos_sb[0][:]))
-                return
+        def fetch_low(u, e, at=None):
+            t = 2 * u + e
+            sides = tile([P, 2, J], F32, "low_sides%d%d" % (u, e), at=at)
             if e == 0:
-                planes[u] = tile([P, 2, J], BF16, "planes%d" % u)
-            for lo, hi in low_parts:
-                fetch(low_sides[u, e][:, 1, lo:hi], 1, 0, 2 * u + e, 0, lo, hi)
-            for lo, hi in low_parts:
-                nc.vector.scalar_tensor_tensor(
-                    out=planes[u][:, e, lo:hi],
-                    in0=low_sides[u, e][:, 0, lo:hi],
-                    scalar=g_low[:, u, e : e + 1],
-                    in1=low_sides[u, e][:, 1, lo:hi],
-                    op0=ALU.mult,
-                    op1=ALU.min,
-                )
+                planes[u] = tile([P, 2, DIRECT], BF16, "planes%d" % u)
+            nc.vector.tensor_copy(sides[:, 0, 0:DIRECT], h[0, t][:].indirect(pos_sb[0][:, 0 : DIRECT // LIST_ROWS]))
+            fetch(sides[:, 1, 0:DIRECT], 1, 0, t, 0, 0, DIRECT)
+            fetch(sides[:, 0, DIRECT:J], 0, 0, t, 0, DIRECT, J)
+            nc.vector.scalar_tensor_tensor(
+                out=planes[u][:, e, :],
+                in0=sides[:, 0, 0:DIRECT],
+                scalar=g_low[:, u, e : e + 1],
+                in1=sides[:, 1, 0:DIRECT],
+                op0=ALU.mult,
+                op1=ALU.min,
+            )
+            entries = pos_sb[1][:, DIRECT // LIST_ROWS : J // LIST_ROWS]
+            nc.vector.tensor_tensor(sides[:, 1, DIRECT:J], h[0, t][:].indirect(entries), minus_g[:, t, :], ALU.mult)
+            cols = slice(e * QUARTER + u * P, e * QUARTER + (u + 1) * P)
+            for n, j0 in enumerate(turned):
+                if t == 0:
+                    differences[j0] = psum.tile([P, BANK], F32, name="bank%d" % (4 + 2 * n))
+                    negatives[j0] = psum.tile([P, BANK], F32, name="bank%d" % (5 + 2 * n))
+                add_turned(differences[j0][:, cols], sides[:, 0, j0 : j0 + P], sides[:, 1, j0 : j0 + P])
+                nc.tensor.transpose(negatives[j0][:, cols], sides[:, 1, j0 : j0 + P], identity[:])
+
+        def add_turned(dst, first, second):
+            nc.tensor.matmul(dst, first, identity[:], start=True, stop=False, is_transpose=True)
+            nc.tensor.matmul(dst, second, identity[:], start=False, stop=True, is_transpose=True)
 
         def overlap_low(u):
             for x in range(2):
@@ -236,9 +251,26 @@ def tile_list_join_sketch_cardinality_kernel(
                     in_=planes[u][x:P:2].rearrange("p e j -> p (e j)").bitcast(I32),
                 )
 
+        def overlap_turned(n, j0):
+            terms = [tile([P, PACK, P], F32, "term%d_%d" % (k, j0)) for k in range(2)]
+            dealt = [term[:].rearrange("j (x e) p -> j x e p", x=2) for term in terms]
+            banked = [bank[j0][:].rearrange("j (e p x) -> j x e p", e=2, x=2) for bank in (differences, negatives)]
+            nc.scalar.activation(dealt[0], banked[0], ACT.Relu, scale=-1.0)
+            nc.scalar.copy(dealt[1], banked[1])
+            back = psum.tile([P, PACK, P], F32, name="bank%d" % n)
+            for t in range(PACK):
+                add_turned(back[:, t, :], terms[0][:, t, :], terms[1][:, t, :])
+            z_bf = tile([P, P, PACK], BF16, "z_turned%d" % j0)
+            nc.scalar.activation(z_bf[:], back[:].rearrange("p t j -> p j t"), ACT.Copy, scale=-1.0)
+            quantize_z(z_bf, 0, j0, 0, P)
+
         gather_words(0, 0, S)
         rounded = rounded_tile("w1_bf000")
         round_low(nc.scalar.copy, rounded, 0, 0)
+        minus_g = tile([P, PACK, J - DIRECT], F32, "minus_g", at=3 * SLOT)
+        nc.scalar.activation(
+            minus_g[:], g_rows[0].unsqueeze(2).to_broadcast([P, PACK, J - DIRECT]), ACT.Copy, scale=-1.0
+        )
         quantize_w1(rounded, 0, 0, 0)
         for t in (0, 1):
             first_product(0, 0, t)
@@ -254,8 +286,7 @@ def tile_list_join_sketch_cardinality_kernel(
         w2_w = tile([P, 2, 2 * N], U8, "w2_w")
         nc.sync.dma_start(out=w2_w[:].bitcast(I32), in_=w2_words.rearrange("a p c -> p a c").bitcast(I32))
         sigmoid(0, 0)
-        fetch_low(0, 0, 0, 0)
-        fetch_low(0, 0, 1)
+        fetch_low(0, 0, 0)
         rounded = rounded_tile("w1_bf011")
         round_low(nc.scalar.copy, rounded, 1, 1)
         quantize_w1(rounded, 0, 1, 1)
@@ -263,21 +294,19 @@ def tile_list_join_sketch_cardinality_kernel(
         with nc.allow_non_contiguous_dma(reason="one bias value a partition"):
             nc.sync.dma_start(out=b2_sb[:], in_=b2.rearrange("(t p) -> p t", p=P))
         for a in range(2):
-            for t in (2, 3):
-                first_product(0, a, t)
+            first_product(0, a, 2)
         sigmoid(0, 1, SLOT // 2)
-        fetch_low(0, 1, 0)
-        fetch_low(0, 1, 1)
+        for a in range(2):
+            first_product(0, a, 3)
+        fetch_low(0, 1)
         overlap_low(0)
 
         prepare_high(0)
         sigmoid(0, 2, SLOT)
-        fetch_low(1, 0, 0)
-        fetch_low(1, 0, 1)
+        fetch_low(1, 0)
         prepare_high(1)
-        sigmoid(0, 3, 4 * SLOT)
-        fetch_low(1, 1, 0)
-        fetch_low(1, 1, 1)
+        sigmoid(0, 3, 2 * SLOT)
+        fetch_low(1, 1)
         overlap_low(1)
         high_sides = [tile([P, PACK * widest], F32, "high_side%d" % side) for side in range(2)]
         for t in range(PACK):
@@ -290,15 +319,17 @@ def tile_list_join_sketch_cardinality_kernel(
                 in_=w2_scales[:, 4 * q : 4 * q + 4, :].rearrange("a q c -> q a c").bitcast(I32),
             )
 
-        z_low = tile([P, J, PACK], BF16, "z_low", "w1_w110")
+        z_low = tile([P, DIRECT, PACK], BF16, "z_low", "w1_w110")
         nc.scalar.copy(z_low[:], halves[:].rearrange("p x (e j) -> p j (x e)", e=2))
-        quantize_z(z_low, 0, 0, 0, J)
+        quantize_z(z_low, 0, 0, 0, DIRECT)
+        for n, j0 in enumerate(turned):
+            overlap_turned(n, j0)
 
         out_rows = out.rearrange("(t p) j -> p t j", p=P)
         for c, (j0, n) in enumerate(CHUNKS):
             parts = ((0, 256), (256, n)) if n > 256 else ((0, n // 2), (n // 2, n))
             pair = [side[:, 0 : PACK * n].rearrange("p (t j) -> p t j", t=PACK) for side in high_sides]
-            y = [psum.tile([P, n], F32, name="bank%d" % (4 * c + nt)) for nt in range(N // P)]
+            y = [psum.tile([P, n], F32, name="bank%d" % (4 - 4 * c + nt)) for nt in range(N // P)]
             for nt in range(N // P):
                 for jj in range(0, n, N_MX):
                     second_product(y[nt], 0, nt, j0, jj)

@@ -29,6 +29,7 @@ EARLY = 768
 SLOT = 4 * T
 PARK = 96
 DIRECT = 256
+SUM_BANKS = ((6, 7, 4, 5), (2, 3, 0, 1))
 
 FLOPS = 2 * K * H * S + 2 * H * N * J
 
@@ -74,7 +75,7 @@ def tile_list_join_sketch_cardinality_kernel(
         nc.sync.dma_start(out=tab_s[PARK:P, :], in_=tab_scales.rearrange("a q c -> (a q) c").bitcast(I32))
         words = [tab_words[a].rearrange("p n t -> p (n t)").bitcast(I32) for a in range(2)]
         nc.sync.dma_start(out=tab_w[0][:], in_=words[0])
-        low_raw = {(0, 0): load_w1(0, 0, QUARTER, at=3 * SLOT)}
+        low_raw = {(0, 0): load_w1(0, 0, QUARTER, at=4 * SLOT)}
         nc.sync.dma_start(out=tab_w[1][:], in_=words[1])
 
         warm = tile([P, 2], F32, "warm")
@@ -119,8 +120,8 @@ def tile_list_join_sketch_cardinality_kernel(
         w1_w, w1_s = {}, {}
 
         def round_low(copy, rounded, u, a):
-            dst = rounded.rearrange("p (e m j) -> p m j e", e=2, j=PACK)
-            copy(dst, low_raw[u, a][:].rearrange("p j (m e) -> p m j e", e=2))
+            dst = rounded.rearrange("p (e m i j) -> p m j i e", e=2, i=2, j=PACK)
+            copy(dst, low_raw[u, a][:].rearrange("p j (m i e) -> p m j i e", i=2, e=2))
 
         def prepare_plane(a, e):
             rounded = tile([P, PASS], BF16, "w1_plane%d%d" % (a, e))
@@ -135,7 +136,7 @@ def tile_list_join_sketch_cardinality_kernel(
             rounded = tile([P, PACK * PASS], BF16, "w1_bf1%d" % a)
             dst = rounded[:].rearrange("p (t m j) -> p m j t", t=PACK, j=PACK)
             nc.scalar.copy(dst, high_raw[a][:].rearrange("p j (m t) -> p m j t", t=PACK))
-            quantize_w1(rounded[:], 1, 0, a, ((0, PACK),))
+            quantize_w1(rounded[:], 1, 0, a, ((0, 1), (1, PACK)) if a else ((0, PACK),))
 
         def quantize_w1(rounded, b, u, a, parts=((0, 2),)):
             for e0, e1 in parts:
@@ -154,7 +155,7 @@ def tile_list_join_sketch_cardinality_kernel(
 
         h = {}
         acc = {}
-        banks = (((0, 1, 4), (2, 3), (0, 1), (2, 3)), ((0, 1), (2, 3), (0, 1), (2, 3)))
+        banks = (((0, 1, 4), (2, 3), (4, 5), (0, 1)), ((2, 3), (4, 5), (0, 1), (2, 3)))
 
         def spans(b, t):
             edges = (0, BANK, EARLY, S) if len(banks[b][t]) == 3 else (0, BANK, S)
@@ -212,7 +213,7 @@ def tile_list_join_sketch_cardinality_kernel(
         planes = {}
         halves = tile([P, 2, 2 * DIRECT], BF16, "halves")
         turned = range(DIRECT, J, P)
-        differences, negatives = {}, {}
+        banked = {}
 
         def fetch_low(u, e, at=None):
             t = 2 * u + e
@@ -232,13 +233,14 @@ def tile_list_join_sketch_cardinality_kernel(
             )
             entries = pos_sb[1][:, DIRECT // LIST_ROWS : J // LIST_ROWS]
             nc.vector.tensor_tensor(sides[:, 1, DIRECT:J], h[0, t][:].indirect(entries), minus_g[:, t, :], ALU.mult)
-            cols = slice(e * QUARTER + u * P, e * QUARTER + (u + 1) * P)
+            low_sides[u, e] = sides
+
+        def turn(u, e):
+            banked[u, e] = psum.tile([P, 2, 2, P], F32, name="bank%d" % (6 - 2 * u + e))
             for n, j0 in enumerate(turned):
-                if t == 0:
-                    differences[j0] = psum.tile([P, BANK], F32, name="bank%d" % (4 + 2 * n))
-                    negatives[j0] = psum.tile([P, BANK], F32, name="bank%d" % (5 + 2 * n))
-                add_turned(differences[j0][:, cols], sides[:, 0, j0 : j0 + P], sides[:, 1, j0 : j0 + P])
-                nc.tensor.transpose(negatives[j0][:, cols], sides[:, 1, j0 : j0 + P], identity[:])
+                left, right = (low_sides[u, e][:, side, j0 : j0 + P] for side in range(2))
+                add_turned(banked[u, e][:, 0, n, :], left, right)
+                nc.tensor.transpose(banked[u, e][:, 1, n, :], right, identity[:])
 
         def add_turned(dst, first, second):
             nc.tensor.matmul(dst, first, identity[:], start=True, stop=False, is_transpose=True)
@@ -251,15 +253,16 @@ def tile_list_join_sketch_cardinality_kernel(
                     in_=planes[u][x:P:2].rearrange("p e j -> p (e j)").bitcast(I32),
                 )
 
-        def overlap_turned(n, j0):
-            terms = [tile([P, PACK, P], F32, "term%d_%d" % (k, j0)) for k in range(2)]
-            dealt = [term[:].rearrange("j (x e) p -> j x e p", x=2) for term in terms]
-            banked = [bank[j0][:].rearrange("j (e p x) -> j x e p", e=2, x=2) for bank in (differences, negatives)]
-            nc.scalar.activation(dealt[0], banked[0], ACT.Relu, scale=-1.0)
-            nc.scalar.copy(dealt[1], banked[1])
+        def split_turned(terms, u, e):
+            dealt = terms[:].rearrange("j k n (x e) (u m) -> j u e k n x m", x=2, u=2)[:, u, e]
+            source = banked[u, e][:].rearrange("j k n (m x) -> j k n x m", x=2)
+            nc.scalar.activation(dealt[:, 0], source[:, 0], ACT.Relu, scale=-1.0)
+            nc.scalar.copy(dealt[:, 1], source[:, 1])
+
+        def overlap_turned(terms, n, j0):
             back = psum.tile([P, PACK, P], F32, name="bank%d" % n)
             for t in range(PACK):
-                add_turned(back[:, t, :], terms[0][:, t, :], terms[1][:, t, :])
+                add_turned(back[:, t, :], terms[:, 0, n, t, :], terms[:, 1, n, t, :])
             z_bf = tile([P, P, PACK], BF16, "z_turned%d" % j0)
             nc.scalar.activation(z_bf[:], back[:].rearrange("p t j -> p j t"), ACT.Copy, scale=-1.0)
             quantize_z(z_bf, 0, j0, 0, P)
@@ -267,7 +270,7 @@ def tile_list_join_sketch_cardinality_kernel(
         gather_words(0, 0, S)
         rounded = rounded_tile("w1_bf000")
         round_low(nc.scalar.copy, rounded, 0, 0)
-        minus_g = tile([P, PACK, J - DIRECT], F32, "minus_g", at=3 * SLOT)
+        minus_g = tile([P, PACK, J - DIRECT], F32, "minus_g", at=4 * SLOT)
         nc.scalar.activation(
             minus_g[:], g_rows[0].unsqueeze(2).to_broadcast([P, PACK, J - DIRECT]), ACT.Copy, scale=-1.0
         )
@@ -287,6 +290,7 @@ def tile_list_join_sketch_cardinality_kernel(
         nc.sync.dma_start(out=w2_w[:].bitcast(I32), in_=w2_words.rearrange("a p c -> p a c").bitcast(I32))
         sigmoid(0, 0)
         fetch_low(0, 0, 0)
+        turn(0, 0)
         rounded = rounded_tile("w1_bf011")
         round_low(nc.scalar.copy, rounded, 1, 1)
         quantize_w1(rounded, 0, 1, 1)
@@ -299,6 +303,7 @@ def tile_list_join_sketch_cardinality_kernel(
         for a in range(2):
             first_product(0, a, 3)
         fetch_low(0, 1)
+        turn(0, 1)
         overlap_low(0)
 
         prepare_high(0)
@@ -306,6 +311,9 @@ def tile_list_join_sketch_cardinality_kernel(
         fetch_low(1, 0)
         prepare_high(1)
         sigmoid(0, 3, 2 * SLOT)
+        terms = tile([P, 2, 2, PACK, P], F32, "terms", at=2 * SLOT + SLOT // 2)
+        for e in range(2):
+            split_turned(terms, 0, e)
         fetch_low(1, 1)
         overlap_low(1)
         high_sides = [tile([P, PACK * widest], F32, "high_side%d" % side) for side in range(2)]
@@ -319,17 +327,20 @@ def tile_list_join_sketch_cardinality_kernel(
                 in_=w2_scales[:, 4 * q : 4 * q + 4, :].rearrange("a q c -> q a c").bitcast(I32),
             )
 
-        z_low = tile([P, DIRECT, PACK], BF16, "z_low", "w1_w110")
+        for e in range(2):
+            turn(1, e)
+            split_turned(terms, 1, e)
+        z_low = tile([P, DIRECT, PACK], BF16, "z_low", "w1_w111")
         nc.scalar.copy(z_low[:], halves[:].rearrange("p x (e j) -> p j (x e)", e=2))
         quantize_z(z_low, 0, 0, 0, DIRECT)
         for n, j0 in enumerate(turned):
-            overlap_turned(n, j0)
+            overlap_turned(terms, n, j0)
 
         out_rows = out.rearrange("(t p) j -> p t j", p=P)
         for c, (j0, n) in enumerate(CHUNKS):
             parts = ((0, 256), (256, n)) if n > 256 else ((0, n // 2), (n // 2, n))
             pair = [side[:, 0 : PACK * n].rearrange("p (t j) -> p t j", t=PACK) for side in high_sides]
-            y = [psum.tile([P, n], F32, name="bank%d" % (4 - 4 * c + nt)) for nt in range(N // P)]
+            y = [psum.tile([P, n], F32, name="bank%d" % SUM_BANKS[c][nt]) for nt in range(N // P)]
             for nt in range(N // P):
                 for jj in range(0, n, N_MX):
                     second_product(y[nt], 0, nt, j0, jj)

@@ -28,8 +28,10 @@ N_MX = 128
 EARLY = 768
 SLOT = 4 * T
 PARK = 96
-DIRECT = 256
-SUM_BANKS = ((6, 7, 4, 5), (2, 3, 0, 1))
+DIRECT = 128
+TURN_BANKS = ((5, 6, 7), (3, 0, 1))
+BACK_BANKS = (4, 5, 6)
+SUM_BANKS = ((3, 0, 1, 7), (2, 4, 5, 6))
 
 FLOPS = 2 * K * H * S + 2 * H * N * J
 
@@ -75,7 +77,7 @@ def tile_list_join_sketch_cardinality_kernel(
         nc.sync.dma_start(out=tab_s[PARK:P, :], in_=tab_scales.rearrange("a q c -> (a q) c").bitcast(I32))
         words = [tab_words[a].rearrange("p n t -> p (n t)").bitcast(I32) for a in range(2)]
         nc.sync.dma_start(out=tab_w[0][:], in_=words[0])
-        low_raw = {(0, 0): load_w1(0, 0, QUARTER, at=4 * SLOT)}
+        low_raw = {(0, 0): load_w1(0, 0, QUARTER, at=5 * SLOT)}
         nc.sync.dma_start(out=tab_w[1][:], in_=words[1])
 
         warm = tile([P, 2], F32, "warm")
@@ -102,11 +104,11 @@ def tile_list_join_sketch_cardinality_kernel(
 
         carry_scales(nc.sync, 0)
         low_raw[0, 1] = load_w1(1, 0, QUARTER)
+        low_raw[1, 0] = load_w1(0, QUARTER, QUARTER)
         carry_scales(nc.sync, 1)
-        low_raw[1, 0] = load_w1(0, QUARTER, QUARTER, at=0)
+        low_raw[1, 1] = load_w1(1, QUARTER, QUARTER, at=0)
         nc.sync.dma_start(pos_sb[0][:], pos1)
         nc.sync.dma_start(pos_sb[1][:], pos2)
-        low_raw[1, 1] = load_w1(1, QUARTER, QUARTER, at=SLOT // 2)
         high_raw = [load_w1(a, PASS, PASS, at=(a + 1) * SLOT) for a in range(2)]
 
         v_w = {}
@@ -123,14 +125,17 @@ def tile_list_join_sketch_cardinality_kernel(
             dst = rounded.rearrange("p (e m i j) -> p m j i e", e=2, i=2, j=PACK)
             copy(dst, low_raw[u, a][:].rearrange("p j (m i e) -> p m j i e", i=2, e=2))
 
-        def prepare_plane(a, e):
-            rounded = tile([P, PASS], BF16, "w1_plane%d%d" % (a, e))
+        def round_plane(copy, u, a, e):
+            rounded = tile([P, PASS], BF16, "w1_plane%d%d" % (a, 2 * u + e))
             dst = rounded[:].rearrange("p (m i j) -> p m j i", i=2, j=PACK)
-            nc.scalar.copy(dst, low_raw[0, a][:].rearrange("p j (m i e) -> p e m j i", i=2, e=2)[:, e])
-            words = tile([P, P], U32, "w1_w0%d%d" % (a, e))
-            scales = tile([P, P], U8, "w1_s0%d%d" % (a, e))
+            copy(dst, low_raw[u, a][:].rearrange("p j (m i e) -> p e m j i", i=2, e=2)[:, e])
+            return rounded
+
+        def quantize_plane(rounded, a, t):
+            words = tile([P, P], U32, "w1_w0%d%d" % (a, t))
+            scales = tile([P, P], U8, "w1_s0%d%d" % (a, t))
             nc.vector.quantize_mx(out=words[:].bitcast(FP8X4), scales=scales[:], in_=rounded[:])
-            w1_w[0, a, e], w1_s[0, a, e] = words[:], scales[:]
+            w1_w[0, a, t], w1_s[0, a, t] = words[:], scales[:]
 
         def prepare_high(a):
             rounded = tile([P, PACK * PASS], BF16, "w1_bf1%d" % a)
@@ -155,7 +160,7 @@ def tile_list_join_sketch_cardinality_kernel(
 
         h = {}
         acc = {}
-        banks = (((0, 1, 4), (2, 3), (4, 5), (0, 1)), ((2, 3), (4, 5), (0, 1), (2, 3)))
+        banks = (((0, 1, 4), (2, 3), (0, 1), (4, 2)), ((3, 0), (1, 4), (5, 6), (7, 2)))
 
         def spans(b, t):
             edges = (0, BANK, EARLY, S) if len(banks[b][t]) == 3 else (0, BANK, S)
@@ -220,27 +225,23 @@ def tile_list_join_sketch_cardinality_kernel(
             sides = tile([P, 2, J], F32, "low_sides%d%d" % (u, e), at=at)
             if e == 0:
                 planes[u] = tile([P, 2, DIRECT], BF16, "planes%d" % u)
-            nc.vector.tensor_copy(sides[:, 0, 0:DIRECT], h[0, t][:].indirect(pos_sb[0][:, 0 : DIRECT // LIST_ROWS]))
+            fetch(sides[:, 0, 0 : J // 2], 0, 0, t, 0, 0, J // 2)
             fetch(sides[:, 1, 0:DIRECT], 1, 0, t, 0, 0, DIRECT)
-            fetch(sides[:, 0, DIRECT:J], 0, 0, t, 0, DIRECT, J)
-            nc.vector.scalar_tensor_tensor(
-                out=planes[u][:, e, :],
-                in0=sides[:, 0, 0:DIRECT],
-                scalar=g_low[:, u, e : e + 1],
-                in1=sides[:, 1, 0:DIRECT],
-                op0=ALU.mult,
-                op1=ALU.min,
-            )
+            fetch(sides[:, 0, J // 2 : J], 0, 0, t, 0, J // 2, J)
+            nc.vector.tensor_tensor(planes[u][:, e, :], sides[:, 0, 0:DIRECT], sides[:, 1, 0:DIRECT], ALU.min)
             entries = pos_sb[1][:, DIRECT // LIST_ROWS : J // LIST_ROWS]
             nc.vector.tensor_tensor(sides[:, 1, DIRECT:J], h[0, t][:].indirect(entries), minus_g[:, t, :], ALU.mult)
             low_sides[u, e] = sides
 
         def turn(u, e):
-            banked[u, e] = psum.tile([P, 2, 2, P], F32, name="bank%d" % (6 - 2 * u + e))
+            banked[u, e] = psum.tile([P, 2, 2, P], F32, name="bank%d" % TURN_BANKS[u][e])
+            if e == 0:
+                banked[u, 2] = psum.tile([P, 2, 2, P], F32, name="bank%d" % TURN_BANKS[u][2])
             for n, j0 in enumerate(turned):
+                place = banked[u, e][:, :, n, :] if n < 2 else banked[u, 2][:, :, e, :]
                 left, right = (low_sides[u, e][:, side, j0 : j0 + P] for side in range(2))
-                add_turned(banked[u, e][:, 0, n, :], left, right)
-                nc.tensor.transpose(banked[u, e][:, 1, n, :], right, identity[:])
+                add_turned(place[:, 0, :], left, right)
+                nc.tensor.transpose(place[:, 1, :], right, identity[:])
 
         def add_turned(dst, first, second):
             nc.tensor.matmul(dst, first, identity[:], start=True, stop=False, is_transpose=True)
@@ -254,13 +255,16 @@ def tile_list_join_sketch_cardinality_kernel(
                 )
 
         def split_turned(terms, u, e):
-            dealt = terms[:].rearrange("j k n (x e) (u m) -> j u e k n x m", x=2, u=2)[:, u, e]
+            if e < 2:
+                dealt = terms[:, :, 0:2].rearrange("j k n (x e) (u m) -> j u e k n x m", x=2, u=2)[:, u, e]
+            else:
+                dealt = terms[:, :, 2].rearrange("j k (x e) (u m) -> j u k e x m", x=2, u=2)[:, u]
             source = banked[u, e][:].rearrange("j k n (m x) -> j k n x m", x=2)
             nc.scalar.activation(dealt[:, 0], source[:, 0], ACT.Relu, scale=-1.0)
             nc.scalar.copy(dealt[:, 1], source[:, 1])
 
         def overlap_turned(terms, n, j0):
-            back = psum.tile([P, PACK, P], F32, name="bank%d" % n)
+            back = psum.tile([P, PACK, P], F32, name="bank%d" % BACK_BANKS[n])
             for t in range(PACK):
                 add_turned(back[:, t, :], terms[:, 0, n, t, :], terms[:, 1, n, t, :])
             z_bf = tile([P, P, PACK], BF16, "z_turned%d" % j0)
@@ -270,7 +274,7 @@ def tile_list_join_sketch_cardinality_kernel(
         gather_words(0, 0, S)
         rounded = rounded_tile("w1_bf000")
         round_low(nc.scalar.copy, rounded, 0, 0)
-        minus_g = tile([P, PACK, J - DIRECT], F32, "minus_g", at=4 * SLOT)
+        minus_g = tile([P, PACK, J - DIRECT], F32, "minus_g", at=5 * SLOT)
         nc.scalar.activation(
             minus_g[:], g_rows[0].unsqueeze(2).to_broadcast([P, PACK, J - DIRECT]), ACT.Copy, scale=-1.0
         )
@@ -278,28 +282,28 @@ def tile_list_join_sketch_cardinality_kernel(
         for t in (0, 1):
             first_product(0, 0, t)
         gather_words(1, 0, EARLY)
-        prepare_plane(1, 0)
+        quantize_plane(round_plane(nc.scalar.copy, 0, 1, 0), 1, 0)
         gather_words(1, EARLY, S, "w1_plane10")
         first_product(0, 1, 0)
-        prepare_plane(1, 1)
+        quantize_plane(round_plane(nc.scalar.copy, 0, 1, 1), 1, 1)
         first_product(0, 1, 1)
-        rounded = rounded_tile("w1_bf010")
-        round_low(nc.vector.tensor_copy, rounded, 1, 0)
-        quantize_w1(rounded, 0, 1, 0)
+        third = [round_plane(copy, 1, 0, e) for e, copy in enumerate((nc.vector.tensor_copy, nc.scalar.copy))]
+        for e in (1, 0):
+            quantize_plane(third[e], 0, 2 + e)
+        fourth = [round_plane(nc.vector.tensor_copy, 1, 1, e) for e in range(2)]
+        for e in range(2):
+            quantize_plane(fourth[e], 1, 2 + e)
         w2_w = tile([P, 2, 2 * N], U8, "w2_w")
         nc.sync.dma_start(out=w2_w[:].bitcast(I32), in_=w2_words.rearrange("a p c -> p a c").bitcast(I32))
         sigmoid(0, 0)
         fetch_low(0, 0, 0)
         turn(0, 0)
-        rounded = rounded_tile("w1_bf011")
-        round_low(nc.scalar.copy, rounded, 1, 1)
-        quantize_w1(rounded, 0, 1, 1)
         b2_sb = tile([P, N // P], F32, "b2_sb")
         with nc.allow_non_contiguous_dma(reason="one bias value a partition"):
             nc.sync.dma_start(out=b2_sb[:], in_=b2.rearrange("(t p) -> p t", p=P))
         for a in range(2):
             first_product(0, a, 2)
-        sigmoid(0, 1, SLOT // 2)
+        sigmoid(0, 1)
         for a in range(2):
             first_product(0, a, 3)
         fetch_low(0, 1)
@@ -311,8 +315,8 @@ def tile_list_join_sketch_cardinality_kernel(
         fetch_low(1, 0)
         prepare_high(1)
         sigmoid(0, 3, 2 * SLOT)
-        terms = tile([P, 2, 2, PACK, P], F32, "terms", at=2 * SLOT + SLOT // 2)
-        for e in range(2):
+        terms = tile([P, 2, 3, PACK, P], F32, "terms", at=2 * SLOT + SLOT // 2)
+        for e in range(3):
             split_turned(terms, 0, e)
         fetch_low(1, 1)
         overlap_low(1)
@@ -320,21 +324,26 @@ def tile_list_join_sketch_cardinality_kernel(
         for t in range(PACK):
             first_product(1, 0, t)
             first_product(1, 1, t)
-            sigmoid(1, t)
+            if t < 2:
+                sigmoid(1, t)
+        for e in range(2):
+            turn(1, e)
+        for e in range(2):
+            split_turned(terms, 1, e)
+            sigmoid(1, 2 + e)
+        split_turned(terms, 1, 2)
         for q in range(4):
             nc.sync.dma_start(
                 out=planes_s[0][32 * q : 32 * q + 4, :].bitcast(I32).rearrange("q (a c) -> q a c", a=2),
                 in_=w2_scales[:, 4 * q : 4 * q + 4, :].rearrange("a q c -> q a c").bitcast(I32),
             )
 
-        for e in range(2):
-            turn(1, e)
-            split_turned(terms, 1, e)
+        overlap_turned(terms, 0, turned[0])
         z_low = tile([P, DIRECT, PACK], BF16, "z_low", "w1_w111")
         nc.scalar.copy(z_low[:], halves[:].rearrange("p x (e j) -> p j (x e)", e=2))
         quantize_z(z_low, 0, 0, 0, DIRECT)
-        for n, j0 in enumerate(turned):
-            overlap_turned(terms, n, j0)
+        for n in (1, 2):
+            overlap_turned(terms, n, turned[n])
 
         out_rows = out.rearrange("(t p) j -> p t j", p=P)
         for c, (j0, n) in enumerate(CHUNKS):

@@ -29,9 +29,9 @@ EARLY = 768
 SLOT = 4 * T
 PARK = 96
 DIRECT = 128
-TURN_BANKS = ((5, 6, 7), (3, 0, 1))
-BACK_BANKS = (4, 5, 6)
-SUM_BANKS = ((3, 0, 1, 7), (2, 4, 5, 6))
+TURN_BANKS = ((5, 6, 7), (4, 0, 1))
+BACK_BANKS = (2, 5, 6)
+SUM_BANKS = ((4, 0, 1, 7), (3, 2, 5, 6))
 
 FLOPS = 2 * K * H * S + 2 * H * N * J
 
@@ -160,7 +160,7 @@ def tile_list_join_sketch_cardinality_kernel(
 
         h = {}
         acc = {}
-        banks = (((0, 1, 4), (2, 3), (0, 1), (4, 2)), ((3, 0), (1, 4), (5, 6), (7, 2)))
+        banks = (((0, 1), (2, 3), (0, 1), (2, 3)), ((4, 0), (1, 2), (5, 6), (7, 3)))
 
         def spans(b, t):
             edges = (0, BANK, EARLY, S) if len(banks[b][t]) == 3 else (0, BANK, S)
@@ -202,16 +202,16 @@ def tile_list_join_sketch_cardinality_kernel(
                 in_=z_bf[:, lo:hi, :].rearrange("p j t -> p (j t)"),
             )
 
-        def second_product(y, b, nt, j0, jj):
-            cols = slice(j0 + jj, j0 + jj + N_MX)
+        def second_product(y, b, nt, j0, lo, hi):
+            cols = slice(j0 + lo, j0 + hi)
             nc.tensor.matmul_mx(
-                out=y[:, jj : jj + N_MX],
+                out=y[:, lo:hi],
                 lhsT=w2_w[:, b, 2 * nt * P : 2 * (nt + 1) * P].bitcast(FP4X4),
                 lhsT_scale=planes_s[0][:, b * N + nt * P : b * N + (nt + 1) * P],
                 rhs=z_w[b][:, cols].bitcast(FP8X4),
                 rhs_scale=z_s[b][:, cols],
-                start=(b == 0 and jj == 0),
-                stop=(b == 1 and jj + N_MX == y.shape[1]),
+                start=(b == 0 and lo == 0),
+                stop=(b == 1 and hi == y.shape[1]),
             )
 
         low_sides = {}
@@ -281,9 +281,8 @@ def tile_list_join_sketch_cardinality_kernel(
         quantize_w1(rounded, 0, 0, 0)
         for t in (0, 1):
             first_product(0, 0, t)
-        gather_words(1, 0, EARLY)
+        gather_words(1, 0, S)
         quantize_plane(round_plane(nc.scalar.copy, 0, 1, 0), 1, 0)
-        gather_words(1, EARLY, S, "w1_plane10")
         first_product(0, 1, 0)
         quantize_plane(round_plane(nc.scalar.copy, 0, 1, 1), 1, 1)
         first_product(0, 1, 1)
@@ -348,11 +347,12 @@ def tile_list_join_sketch_cardinality_kernel(
         out_rows = out.rearrange("(t p) j -> p t j", p=P)
         for c, (j0, n) in enumerate(CHUNKS):
             parts = ((0, 256), (256, n)) if n > 256 else ((0, n // 2), (n // 2, n))
+            passes = parts if n > 256 else ((0, n),)
             pair = [side[:, 0 : PACK * n].rearrange("p (t j) -> p t j", t=PACK) for side in high_sides]
             y = [psum.tile([P, n], F32, name="bank%d" % SUM_BANKS[c][nt]) for nt in range(N // P)]
             for nt in range(N // P):
-                for jj in range(0, n, N_MX):
-                    second_product(y[nt], 0, nt, j0, jj)
+                for lo, hi in passes:
+                    second_product(y[nt], 0, nt, j0, lo, hi)
             for t in range(PACK):
                 for side in range(2):
                     for lo, hi in parts if c == 1 and t == PACK - 1 and side == 1 else ((0, n),):
@@ -367,7 +367,7 @@ def tile_list_join_sketch_cardinality_kernel(
                 quantize_z(z_bf, 1, j0, lo, hi)
             res = tile([P, N // P, n], F32, "res%d" % c)
             for nt in range(N // P):
-                for jj in range(0, n, N_MX):
-                    second_product(y[nt], 1, nt, j0, jj)
+                for lo, hi in passes:
+                    second_product(y[nt], 1, nt, j0, lo, hi)
                 nc.scalar.activation(res[:, nt, :], y[nt][:], ACT.Exp, bias=b2_sb[:, nt : nt + 1])
                 nc.sync.dma_start(out=out_rows[:, nt, j0 : j0 + n], in_=res[:, nt, :])

@@ -104,9 +104,9 @@ def tile_list_join_sketch_cardinality_kernel(
 
         carry_scales(nc.sync, 0)
         low_raw[0, 1] = load_w1(1, 0, QUARTER)
-        low_raw[1, 0] = load_w1(0, QUARTER, QUARTER)
+        low_raw[1, 0] = load_w1(0, QUARTER, QUARTER, at=0)
         carry_scales(nc.sync, 1)
-        low_raw[1, 1] = load_w1(1, QUARTER, QUARTER, at=0)
+        low_raw[1, 1] = load_w1(1, QUARTER, QUARTER)
         nc.sync.dma_start(pos_sb[0][:], pos1)
         nc.sync.dma_start(pos_sb[1][:], pos2)
         high_raw = [load_w1(a, PASS, PASS, at=(a + 1) * SLOT) for a in range(2)]
@@ -125,8 +125,8 @@ def tile_list_join_sketch_cardinality_kernel(
             dst = rounded.rearrange("p (e m i j) -> p m j i e", e=2, i=2, j=PACK)
             copy(dst, low_raw[u, a][:].rearrange("p j (m i e) -> p m j i e", i=2, e=2))
 
-        def round_plane(copy, u, a, e):
-            rounded = tile([P, PASS], BF16, "w1_plane%d%d" % (a, 2 * u + e))
+        def round_plane(copy, u, a, e, tag=None):
+            rounded = tile([P, PASS], BF16, "w1_plane%d%d" % (a, 2 * u + e), tag)
             dst = rounded[:].rearrange("p (m i j) -> p m j i", i=2, j=PACK)
             copy(dst, low_raw[u, a][:].rearrange("p j (m i e) -> p e m j i", i=2, e=2)[:, e])
             return rounded
@@ -289,13 +289,12 @@ def tile_list_join_sketch_cardinality_kernel(
         third = [round_plane(copy, 1, 0, e) for e, copy in enumerate((nc.vector.tensor_copy, nc.scalar.copy))]
         for e in (1, 0):
             quantize_plane(third[e], 0, 2 + e)
-        fourth = [round_plane(nc.vector.tensor_copy, 1, 1, e) for e in range(2)]
-        for e in range(2):
-            quantize_plane(fourth[e], 1, 2 + e)
+        quantize_plane(round_plane(nc.vector.tensor_copy, 1, 1, 0), 1, 2)
         w2_w = tile([P, 2, 2 * N], U8, "w2_w")
         nc.sync.dma_start(out=w2_w[:].bitcast(I32), in_=w2_words.rearrange("a p c -> p a c").bitcast(I32))
         sigmoid(0, 0)
         fetch_low(0, 0, 0)
+        quantize_plane(round_plane(nc.scalar.copy, 1, 1, 1, "w1_w010"), 1, 3)
         turn(0, 0)
         b2_sb = tile([P, N // P], F32, "b2_sb")
         with nc.allow_non_contiguous_dma(reason="one bias value a partition"):

@@ -17,21 +17,19 @@ ACT = mybir.ActivationFunctionType
 ALU = mybir.AluOpType
 
 P = 128
-HALF = P // 2
 PACK = 4
 PASS = P * PACK
-QUARTER = PASS // 2
 BANK = 512
 LIST_ROWS = 16
-CHUNKS = ((0, 384), (384, 128))
-N_MX = 128
-EARLY = 768
-SLOT = 4 * T
-PARK = 96
-DIRECT = 128
-TURN_BANKS = ((5, 6, 7), (4, 0, 1))
-BACK_BANKS = (2, 5, 6)
-SUM_BANKS = ((4, 0, 1, 7), (3, 2, 5, 6))
+PARK = 64
+LOW_RUN = 512
+FIRST, LAST = 384, 128
+KIB = 1024
+LOW_PIECES = ((0, 0, 1), (1, 0, 2), (0, 1, 2), (0, 2, 4), (1, 2, 4))
+RAW_LOW = 2 * KIB
+RAW_HIGH = 8 * KIB
+HIGH_AT = 9 * RAW_LOW
+TERMS_AT = HIGH_AT + RAW_HIGH + RAW_HIGH // 2
 
 FLOPS = 2 * K * H * S + 2 * H * N * J
 
@@ -45,328 +43,344 @@ def tile_list_join_sketch_cardinality_kernel(
         shared = ctx.enter_context(tc.tile_pool(name="shared", bufs=1))
         psum = ctx.enter_context(tc.psum_pool(name="psum", bufs=1))
 
-        def tile(shape, dtype, name, tag=None, at=None):
+        def tile(shape, dtype, name, at=None):
             if at is not None:
                 return shared.tile(shape, dtype, name=name, offset=at, align_bytes=64)
-            return keep.tile(shape, dtype, name=name, tag=tag or name, align_bytes=64)
+            return keep.tile(shape, dtype, name=name, align_bytes=64)
+
+        def bank(shape, number):
+            return psum.tile(shape, F32, name="bank%d" % number)
 
         offs_sb = keep.tile([P, S // LIST_ROWS], U16, name="offs_sb")
         pos_sb = [keep.tile([P, J // LIST_ROWS], U16, name="pos%d_sb" % side) for side in range(2)]
         tab_w = [tile([P, T], I32, "tab_w%d" % a) for a in range(2)]
         tab_s = tile([P, T // 4], I32, "tab_s")
-        g_low = tile([P, 2, 2], F32, "g_low")
+        g_low = tile([P, PACK], F32, "g_low")
         g_high = tile([P, PACK], F32, "g_high")
-        both_planes = tile([P, 2 * S], U8, "both_planes")
-        planes_s = [both_planes[:, a * S : (a + 1) * S] for a in range(2)]
 
         nc.vector.memset(tab_s[0:PARK, :], 0)
-        nc.vector.memset(both_planes[:].bitcast(I32), 0)
+        nc.vector.memset(tab_s[PARK + 32 : P, :], 0)
 
         identity = tile([P, P], F32, "identity")
         make_identity(nc, identity[:])
 
-        def load_w1(a, c0, width, at=None):
-            raw = tile([P, PACK, width], F32, "w1_raw%d_%d" % (a, c0), at=at)
+        def load_w1(a, c0, width, at):
+            raw = tile([P, PACK, width], F32, "w1_raw%d_%d" % (a, c0), at)
             rows = w1[a * PASS : (a + 1) * PASS, c0 : c0 + width]
             nc.sync.dma_start(out=raw[:], in_=rows.rearrange("(p j) c -> p j c", j=PACK))
             return raw
 
+        low_raw = {}
+        low_at = [RAW_LOW * sum(t1 - t0 for a, t0, t1 in LOW_PIECES[:n]) for n in range(len(LOW_PIECES))]
+
+        def load_low(n):
+            a, t0, t1 = LOW_PIECES[n]
+            raw = load_w1(a, t0 * P, (t1 - t0) * P, low_at[n])
+            low_raw[n] = raw
+
         nc.sync.dma_start(offs_sb[:], offs)
-        nc.scalar.dma_start(out=g_low[:], in_=g[0:PASS].rearrange("(u p e) -> p u e", u=2, e=2))
         nc.scalar.dma_start(out=g_high[:], in_=g[PASS:H].rearrange("(p t) -> p t", t=PACK))
-        nc.sync.dma_start(out=tab_s[PARK:P, :], in_=tab_scales.rearrange("a q c -> (a q) c").bitcast(I32))
+        with nc.allow_non_contiguous_dma(reason="one factor a partition and tile"):
+            nc.scalar.dma_start(out=g_low[:], in_=g[0:PASS].rearrange("(t p) -> p t", p=P))
+        nc.sync.dma_start(out=tab_s[PARK : PARK + 32, :], in_=tab_scales.bitcast(I32).rearrange("a q c -> q a c"))
         words = [tab_words[a].rearrange("p n t -> p (n t)").bitcast(I32) for a in range(2)]
         nc.sync.dma_start(out=tab_w[0][:], in_=words[0])
-        low_raw = {(0, 0): load_w1(0, 0, QUARTER, at=5 * SLOT)}
+        nc.sync.dma_start(pos_sb[0][:], pos1)
+        nc.sync.dma_start(pos_sb[1][:], pos2)
+        load_low(0)
         nc.sync.dma_start(out=tab_w[1][:], in_=words[1])
+        load_low(1)
 
         warm = tile([P, 2], F32, "warm")
         nc.vector.memset(warm[:, 0:1], 0.0)
         nc.scalar.activation(warm[:, 1:2], warm[:, 0:1], ACT.Sigmoid)
 
-        widest = max(n for j0, n in CHUNKS)
-        g_wide = {}
-        g_rows = [g_low[:].rearrange("p u e -> p (u e)"), g_high[:]]
+        def spread(rows, width, sign, name):
+            wide = tile([P, PACK, width], F32, name)
+            nc.scalar.activation(wide[:], rows[:].unsqueeze(2).to_broadcast([P, PACK, width]), ACT.Copy, scale=sign)
+            return wide
 
-        def spread_g(b, width, at=None):
-            g_wide[b] = tile([P, PACK, width], F32, "g_wide%d" % b, at=at)
-            nc.scalar.activation(g_wide[b][:], g_rows[b].unsqueeze(2).to_broadcast([P, PACK, width]), ACT.Copy)
+        high_factor = spread(g_high, FIRST, 1.0, "high_factor")
+        minus_low = tile([P, PACK, LOW_RUN], F32, "minus_low")
+        nc.gpsimd.tensor_scalar(
+            minus_low[:], g_low[:].unsqueeze(2).to_broadcast([P, PACK, LOW_RUN]), -1.0, 0.0, ALU.mult, ALU.add
+        )
+        low_factor = [spread(g_low, LOW_RUN, 1.0, "plus_low"), minus_low]
 
-        spread_g(0, J // 2)
-        spread_g(1, widest)
         v_s = tile([P, S], U8, "v_s")
         nc.vector.tensor_copy(v_s[:], tab_s[:].bitcast(U8).indirect(offs_sb[:]))
+        planes = tile([P, S], U8, "planes")
+        for r in range(4):
+            nc.sync.dma_start(
+                out=planes[r:P:4, :].bitcast(I32), in_=v_s[PARK + 2 * r : PARK + 2 * r + 32, :].bitcast(I32)
+            )
+        for n in range(2, len(LOW_PIECES)):
+            load_low(n)
+        high_raw = [load_w1(a, PASS, PASS, HIGH_AT + a * RAW_HIGH) for a in range(2)]
+        w2_w = tile([P, 2, 2 * N], U8, "w2_w")
+        nc.sync.dma_start(out=w2_w[:].bitcast(I32), in_=w2_words.rearrange("a p c -> p a c").bitcast(I32))
+        b2_sb = tile([P, N // P], F32, "b2_sb")
+        with nc.allow_non_contiguous_dma(reason="one bias value a partition"):
+            nc.sync.dma_start(out=b2_sb[:], in_=b2.rearrange("(t p) -> p t", p=P))
 
-        def carry_scales(queue, a):
-            for q in range(4):
-                rows = slice(PARK + 16 * a + 4 * q, PARK + 16 * a + 4 * q + 4)
-                queue.dma_start(out=planes_s[a][32 * q : 32 * q + 4, :].bitcast(I32), in_=v_s[rows, :].bitcast(I32))
+        v_w = {0: [], 1: []}
 
-        carry_scales(nc.sync, 0)
-        low_raw[0, 1] = load_w1(1, 0, QUARTER)
-        low_raw[1, 0] = load_w1(0, QUARTER, QUARTER, at=0)
-        carry_scales(nc.sync, 1)
-        low_raw[1, 1] = load_w1(1, QUARTER, QUARTER)
-        nc.sync.dma_start(pos_sb[0][:], pos1)
-        nc.sync.dma_start(pos_sb[1][:], pos2)
-        high_raw = [load_w1(a, PASS, PASS, at=(a + 1) * SLOT) for a in range(2)]
-
-        v_w = {}
-
-        def gather_words(a, lo, hi, tag=None):
-            picked = tile([P, hi - lo], U32, "v_w%d_%d" % (a, lo), tag)
+        def gather_words(a, lo, hi, at=None):
+            picked = tile([P, hi - lo], U32, "v_w%d_%d" % (a, lo), at)
             entries = offs_sb[:, lo // LIST_ROWS : hi // LIST_ROWS]
             nc.vector.tensor_copy(picked[:], tab_w[a][:].bitcast(U32).indirect(entries))
-            v_w.setdefault(a, []).append((lo, hi, picked))
+            v_w[a].append((lo, hi, picked))
 
         w1_w, w1_s = {}, {}
+        rounded = {}
 
-        def round_low(copy, rounded, u, a):
-            dst = rounded.rearrange("p (e m i j) -> p m j i e", e=2, i=2, j=PACK)
-            copy(dst, low_raw[u, a][:].rearrange("p j (m i e) -> p m j i e", i=2, e=2))
+        def round_low(copy, n, t, count=1):
+            a, t0, t1 = LOW_PIECES[n]
+            rounded[t, a] = tile([P, count * PASS], BF16, "w1_bf%d%d" % (t, a))
+            dst = rounded[t, a][:].rearrange("p (c i j) -> p c j i", i=4, j=PACK)
+            columns = low_raw[n][:, :, (t - t0) * P : (t - t0 + count) * P]
+            copy(dst, columns.rearrange("p j (c i) -> p c j i", i=4))
 
-        def round_plane(copy, u, a, e, tag=None):
-            rounded = tile([P, PASS], BF16, "w1_plane%d%d" % (a, 2 * u + e), tag)
-            dst = rounded[:].rearrange("p (m i j) -> p m j i", i=2, j=PACK)
-            copy(dst, low_raw[u, a][:].rearrange("p j (m i e) -> p e m j i", i=2, e=2)[:, e])
-            return rounded
-
-        def quantize_plane(rounded, a, t):
-            words = tile([P, P], U32, "w1_w0%d%d" % (a, t))
-            scales = tile([P, P], U8, "w1_s0%d%d" % (a, t))
-            nc.vector.quantize_mx(out=words[:].bitcast(FP8X4), scales=scales[:], in_=rounded[:])
-            w1_w[0, a, t], w1_s[0, a, t] = words[:], scales[:]
-
-        def prepare_high(a):
-            rounded = tile([P, PACK * PASS], BF16, "w1_bf1%d" % a)
-            dst = rounded[:].rearrange("p (t m j) -> p m j t", t=PACK, j=PACK)
+        def round_high(a):
+            whole = tile([P, PACK * PASS], BF16, "w1_bf_high%d" % a)
+            dst = whole[:].rearrange("p (t m j) -> p m j t", t=PACK, j=PACK)
             nc.scalar.copy(dst, high_raw[a][:].rearrange("p j (m t) -> p m j t", t=PACK))
-            quantize_w1(rounded[:], 1, 0, a, ((0, 1), (1, PACK)) if a else ((0, PACK),))
+            return whole
 
-        def quantize_w1(rounded, b, u, a, parts=((0, 2),)):
-            for e0, e1 in parts:
-                width = (e1 - e0) * P
-                words = tile([P, width], U32, "w1_w%d%d%d" % (b, a, 2 * u + e0))
-                scales = tile([P, width], U8, "w1_s%d%d%d" % (b, a, 2 * u + e0))
-                nc.vector.quantize_mx(
-                    out=words[:].bitcast(FP8X4), scales=scales[:], in_=rounded[:, e0 * PASS : e1 * PASS]
-                )
-                for e in range(e0, e1):
-                    cols = slice((e - e0) * P, (e - e0 + 1) * P)
-                    w1_w[b, a, 2 * u + e], w1_s[b, a, 2 * u + e] = words[:, cols], scales[:, cols]
+        def quantize_w1(source, a, t0, count):
+            words = tile([P, count * P], U32, "w1_w%d%d" % (a, t0))
+            scales = tile([P, count * P], U8, "w1_s%d%d" % (a, t0))
+            nc.vector.quantize_mx(out=words[:].bitcast(FP8X4), scales=scales[:], in_=source)
+            for e in range(count):
+                cols = slice(e * P, (e + 1) * P)
+                w1_w[t0 + e, a], w1_s[t0 + e, a] = words[:, cols], scales[:, cols]
 
-        def rounded_tile(name, tag=None):
-            return tile([P, 2 * PASS], BF16, name, tag)[:]
+        def quantize_low(t, a, count=1):
+            quantize_w1(rounded[t, a][:], a, t, count)
 
         h = {}
         acc = {}
-        banks = (((0, 1), (2, 3), (0, 1), (2, 3)), ((4, 0), (1, 2), (5, 6), (7, 3)))
+        sum_banks = ((0, 1, 6), (2, 3), (4, 5), (6, 7), (4, 5), (6, 7), (0, 1), (2, 3))
+        opening = (0, 1, 0, 0, 0, 0, 0, 0)
 
-        def spans(b, t):
-            edges = (0, BANK, EARLY, S) if len(banks[b][t]) == 3 else (0, BANK, S)
+        def spans(t):
+            edges = (0, BANK, 768, S) if len(sum_banks[t]) == 3 else (0, BANK, S)
             return list(zip(edges, edges[1:]))
 
-        def first_product(b, a, t):
-            for (c0, c1), bank in zip(spans(b, t), banks[b][t]):
-                if a == 0:
-                    acc[t, c0] = psum.tile([P, c1 - c0], F32, name="bank%d" % bank)
+        def first_product(t, a):
+            for (c0, c1), number in zip(spans(t), sum_banks[t]):
+                if a == opening[t]:
+                    acc[t, c0] = bank([P, c1 - c0], number)
                 for lo, hi, picked in v_w[a]:
                     first, last = max(lo, c0), min(hi, c1)
                     if first < last:
                         nc.tensor.matmul_mx(
                             out=acc[t, c0][:, first - c0 : last - c0],
-                            lhsT=w1_w[b, a, t].bitcast(FP8X4),
-                            lhsT_scale=w1_s[b, a, t],
+                            lhsT=w1_w[t, a].bitcast(FP8X4),
+                            lhsT_scale=w1_s[t, a],
                             rhs=picked[:, first - lo : last - lo].bitcast(FP8X4),
-                            rhs_scale=planes_s[a][:, first:last],
-                            start=(a == 0),
-                            stop=(a == 1 and last == c1),
+                            rhs_scale=planes[4 * a : P, first:last],
+                            start=(a == opening[t] and first == c0),
+                            stop=(a != opening[t] and last == c1),
                         )
 
-        def sigmoid(b, t, at=None):
-            h[b, t] = tile([P, S], F32, "h%d%d" % (b, t), at=at)
-            for c0, c1 in spans(b, t):
-                nc.scalar.activation(h[b, t][:, c0:c1], acc[t, c0][:], ACT.Sigmoid)
+        def sigmoid(t, at=None):
+            h[t] = tile([P, S], F32, "h%d" % t, at)
+            for c0, c1 in spans(t):
+                nc.scalar.activation(h[t][:, c0:c1], acc[t, c0][:], ACT.Sigmoid)
 
-        def fetch(dst, side, b, t, j0, lo, hi):
-            entries = pos_sb[side][:, (j0 + lo) // LIST_ROWS : (j0 + hi) // LIST_ROWS]
-            nc.vector.tensor_tensor(dst, h[b, t][:].indirect(entries), g_wide[b][:, t, 0 : hi - lo], ALU.mult)
-
-        z_w = [tile([P, J], U32, "z_w%d" % b) for b in range(2)]
-        z_s = [tile([P, J], U8, "z_s%d" % b) for b in range(2)]
-
-        def quantize_z(z_bf, b, j0, lo, hi):
-            nc.vector.quantize_mx(
-                out=z_w[b][:, j0 + lo : j0 + hi].bitcast(FP8X4),
-                scales=z_s[b][:, j0 + lo : j0 + hi],
-                in_=z_bf[:, lo:hi, :].rearrange("p j t -> p (j t)"),
-            )
-
-        def second_product(y, b, nt, j0, lo, hi):
-            cols = slice(j0 + lo, j0 + hi)
-            nc.tensor.matmul_mx(
-                out=y[:, lo:hi],
-                lhsT=w2_w[:, b, 2 * nt * P : 2 * (nt + 1) * P].bitcast(FP4X4),
-                lhsT_scale=planes_s[0][:, b * N + nt * P : b * N + (nt + 1) * P],
-                rhs=z_w[b][:, cols].bitcast(FP8X4),
-                rhs_scale=z_s[b][:, cols],
-                start=(b == 0 and lo == 0),
-                stop=(b == 1 and hi == y.shape[1]),
-            )
+        def fetch(dst, side, t, lo, hi, factor):
+            entries = pos_sb[side][:, lo // LIST_ROWS : hi // LIST_ROWS]
+            nc.vector.tensor_tensor(dst, h[t][:].indirect(entries), factor[:, t % PACK, 0 : hi - lo], ALU.mult)
 
         low_sides = {}
-        planes = {}
-        halves = tile([P, 2, 2 * DIRECT], BF16, "halves")
-        turned = range(DIRECT, J, P)
-        banked = {}
 
-        def fetch_low(u, e, at=None):
-            t = 2 * u + e
-            sides = tile([P, 2, J], F32, "low_sides%d%d" % (u, e), at=at)
-            if e == 0:
-                planes[u] = tile([P, 2, DIRECT], BF16, "planes%d" % u)
-            fetch(sides[:, 0, 0 : J // 2], 0, 0, t, 0, 0, J // 2)
-            fetch(sides[:, 1, 0:DIRECT], 1, 0, t, 0, 0, DIRECT)
-            fetch(sides[:, 0, J // 2 : J], 0, 0, t, 0, J // 2, J)
-            nc.vector.tensor_tensor(planes[u][:, e, :], sides[:, 0, 0:DIRECT], sides[:, 1, 0:DIRECT], ALU.min)
-            entries = pos_sb[1][:, DIRECT // LIST_ROWS : J // LIST_ROWS]
-            nc.vector.tensor_tensor(sides[:, 1, DIRECT:J], h[0, t][:].indirect(entries), minus_g[:, t, :], ALU.mult)
-            low_sides[u, e] = sides
+        def fetch_low(t, side, dst):
+            low_sides[t, side] = dst
+            for lo in range(0, J, LOW_RUN):
+                fetch(dst[:, lo : lo + LOW_RUN], side, t, lo, lo + LOW_RUN, low_factor[side])
 
-        def turn(u, e):
-            banked[u, e] = psum.tile([P, 2, 2, P], F32, name="bank%d" % TURN_BANKS[u][e])
-            if e == 0:
-                banked[u, 2] = psum.tile([P, 2, 2, P], F32, name="bank%d" % TURN_BANKS[u][2])
-            for n, j0 in enumerate(turned):
-                place = banked[u, e][:, :, n, :] if n < 2 else banked[u, 2][:, :, e, :]
-                left, right = (low_sides[u, e][:, side, j0 : j0 + P] for side in range(2))
-                add_turned(place[:, 0, :], left, right)
-                nc.tensor.transpose(place[:, 1, :], right, identity[:])
+        def fetch_both(t, at=None):
+            sides = tile([P, 2, J], F32, "low_sides%d" % t, at)
+            for side in range(2):
+                fetch_low(t, side, sides[:, side, :])
 
         def add_turned(dst, first, second):
             nc.tensor.matmul(dst, first, identity[:], start=True, stop=False, is_transpose=True)
             nc.tensor.matmul(dst, second, identity[:], start=False, stop=True, is_transpose=True)
 
-        def overlap_low(u):
-            for x in range(2):
-                nc.sync.dma_start(
-                    out=halves[u * HALF : (u + 1) * HALF, x, :].bitcast(I32),
-                    in_=planes[u][x:P:2].rearrange("p e j -> p (e j)").bitcast(I32),
-                )
+        turned = {}
 
-        def split_turned(terms, u, e):
-            if e < 2:
-                dealt = terms[:, :, 0:2].rearrange("j k n (x e) (u m) -> j u e k n x m", x=2, u=2)[:, u, e]
-            else:
-                dealt = terms[:, :, 2].rearrange("j k (x e) (u m) -> j u k e x m", x=2, u=2)[:, u]
-            source = banked[u, e][:].rearrange("j k n (m x) -> j k n x m", x=2)
-            nc.scalar.activation(dealt[:, 0], source[:, 0], ACT.Relu, scale=-1.0)
-            nc.scalar.copy(dealt[:, 1], source[:, 1])
+        def turn(t):
+            first = 2 * t
+            turned[t] = [bank([P, PACK, P], first + k) for k in range(2)]
+            for n in range(PACK):
+                left, right = (low_sides[t, side][:, n * P : (n + 1) * P] for side in range(2))
+                add_turned(turned[t][0][:, n, :], left, right)
+                nc.tensor.transpose(turned[t][1][:, n, :], right, identity[:])
 
-        def overlap_turned(terms, n, j0):
-            back = psum.tile([P, PACK, P], F32, name="bank%d" % BACK_BANKS[n])
-            for t in range(PACK):
-                add_turned(back[:, t, :], terms[:, 0, n, t, :], terms[:, 1, n, t, :])
-            z_bf = tile([P, P, PACK], BF16, "z_turned%d" % j0)
-            nc.scalar.activation(z_bf[:], back[:].rearrange("p t j -> p j t"), ACT.Copy, scale=-1.0)
-            quantize_z(z_bf, 0, j0, 0, P)
+        terms = tile([P, 2, PACK, PACK, P], F32, "terms", TERMS_AT)
+
+        def split(t, n0=0, n1=PACK):
+            dealt = terms[:, :, n0:n1, :, 32 * t : 32 * (t + 1)]
+            source = [turned[t][k][:, n0:n1, :].rearrange("j n (m i) -> j n i m", i=PACK) for k in range(2)]
+            nc.scalar.activation(dealt[:, 0], source[0], ACT.Relu, scale=-1.0)
+            nc.scalar.copy(dealt[:, 1], source[1])
+
+        z_w = [tile([P, J], U32, "z_w%d" % b) for b in range(2)]
+        z_s = [tile([P, J], U8, "z_s%d" % b) for b in range(2)]
+
+        def quantize_z(source, b, lo, hi):
+            nc.vector.quantize_mx(
+                out=z_w[b][:, lo:hi].bitcast(FP8X4), scales=z_s[b][:, lo:hi], in_=source.rearrange("p j t -> p (j t)")
+            )
+
+        def turn_back(n, number, dst):
+            back = bank([P, PACK, P], number)
+            for i in range(PACK):
+                add_turned(back[:, i, :], terms[:, 0, n, i, :], terms[:, 1, n, i, :])
+            nc.scalar.activation(dst, back[:].rearrange("p i j -> p j i"), ACT.Copy, scale=-1.0)
+
+        def second_product(y, b, nt, j0, lo, hi, opening_half):
+            nc.tensor.matmul_mx(
+                out=y[:, lo - j0 : hi - j0],
+                lhsT=w2_w[:, b, 2 * nt * P : 2 * (nt + 1) * P].bitcast(FP4X4),
+                lhsT_scale=planes[:, b * N + nt * P : b * N + (nt + 1) * P],
+                rhs=z_w[b][:, lo:hi].bitcast(FP8X4),
+                rhs_scale=z_s[b][:, lo:hi],
+                start=(b == opening_half and lo == j0),
+                stop=(b != opening_half and hi - j0 == y.shape[1]),
+            )
 
         gather_words(0, 0, S)
-        rounded = rounded_tile("w1_bf000")
-        round_low(nc.scalar.copy, rounded, 0, 0)
-        minus_g = tile([P, PACK, J - DIRECT], F32, "minus_g", at=5 * SLOT)
-        nc.scalar.activation(
-            minus_g[:], g_rows[0].unsqueeze(2).to_broadcast([P, PACK, J - DIRECT]), ACT.Copy, scale=-1.0
-        )
-        quantize_w1(rounded, 0, 0, 0)
-        for t in (0, 1):
-            first_product(0, 0, t)
-        gather_words(1, 0, S)
-        quantize_plane(round_plane(nc.scalar.copy, 0, 1, 0), 1, 0)
-        first_product(0, 1, 0)
-        quantize_plane(round_plane(nc.scalar.copy, 0, 1, 1), 1, 1)
-        first_product(0, 1, 1)
-        third = [round_plane(copy, 1, 0, e) for e, copy in enumerate((nc.vector.tensor_copy, nc.scalar.copy))]
-        for e in (1, 0):
-            quantize_plane(third[e], 0, 2 + e)
-        quantize_plane(round_plane(nc.vector.tensor_copy, 1, 1, 0), 1, 2)
-        w2_w = tile([P, 2, 2 * N], U8, "w2_w")
-        nc.sync.dma_start(out=w2_w[:].bitcast(I32), in_=w2_words.rearrange("a p c -> p a c").bitcast(I32))
-        sigmoid(0, 0)
-        fetch_low(0, 0, 0)
-        quantize_plane(round_plane(nc.scalar.copy, 1, 1, 1, "w1_w010"), 1, 3)
-        turn(0, 0)
-        b2_sb = tile([P, N // P], F32, "b2_sb")
-        with nc.allow_non_contiguous_dma(reason="one bias value a partition"):
-            nc.sync.dma_start(out=b2_sb[:], in_=b2.rearrange("(t p) -> p t", p=P))
-        for a in range(2):
-            first_product(0, a, 2)
-        sigmoid(0, 1)
-        for a in range(2):
-            first_product(0, a, 3)
-        fetch_low(0, 1)
-        turn(0, 1)
-        overlap_low(0)
+        round_low(nc.scalar.copy, 0, 0)
+        quantize_low(0, 0)
+        first_product(0, 0)
+        gather_words(1, 0, 768)
+        round_low(nc.scalar.copy, 1, 0)
+        round_low(nc.scalar.copy, 1, 1)
+        quantize_low(0, 1)
+        quantize_low(1, 1)
+        gather_words(1, 768, S, low_at[1])
+        first_product(0, 1)
+        first_product(1, 1)
+        round_low(nc.scalar.copy, 2, 1)
+        round_low(nc.vector.tensor_copy, 3, 2, 2)
+        quantize_low(1, 0)
+        first_product(1, 0)
+        quantize_low(2, 0, 2)
+        first_product(2, 0)
+        sigmoid(0)
+        first_product(3, 0)
+        fetch_low(0, 0, tile([P, J], F32, "low_left0", low_at[3])[:])
+        round_low(nc.scalar.copy, 4, 2, 2)
+        quantize_low(2, 1, 2)
+        first_product(2, 1)
+        first_product(3, 1)
+        fetch_low(0, 1, tile([P, J], F32, "low_right0", low_at[4])[:])
+        turn(0)
+        sigmoid(1, low_at[4] + RAW_LOW)
+        fetch_both(1)
+        turn(1)
+        sigmoid(2)
+        fetch_low(2, 0, tile([P, J], F32, "low_left2")[:])
+        whole = round_high(0)
+        quantize_w1(whole[:], 0, PACK, PACK)
+        fetch_low(2, 1, tile([P, J], F32, "low_right2", HIGH_AT + RAW_HIGH // 2)[:])
+        sigmoid(3, HIGH_AT)
+        for t in (4, 5):
+            first_product(t, 0)
+        fetch_low(3, 0, tile([P, J], F32, "low_left3")[:])
+        whole = round_high(1)
+        quantize_w1(whole[:, 0:PASS], 1, PACK, 1)
+        first_product(4, 1)
+        right = tile([P, J], F32, "low_right3", HIGH_AT + RAW_HIGH)
+        low_sides[3, 1] = right[:]
+        fetch(right[:, 0 : J // 2], 1, 3, 0, J // 2, low_factor[1])
+        quantize_w1(whole[:, PASS : PACK * PASS], 1, PACK + 1, PACK - 1)
+        first_product(5, 1)
+        fetch(right[:, J // 2 : J], 1, 3, J // 2, J, low_factor[1])
+        split(0)
 
-        prepare_high(0)
-        sigmoid(0, 2, SLOT)
-        fetch_low(1, 0)
-        prepare_high(1)
-        sigmoid(0, 3, 2 * SLOT)
-        terms = tile([P, 2, 3, PACK, P], F32, "terms", at=2 * SLOT + SLOT // 2)
-        for e in range(3):
-            split_turned(terms, 0, e)
-        fetch_low(1, 1)
-        overlap_low(1)
-        high_sides = [tile([P, PACK * widest], F32, "high_side%d" % side) for side in range(2)]
-        for t in range(PACK):
-            first_product(1, 0, t)
-            first_product(1, 1, t)
-            if t < 2:
-                sigmoid(1, t)
-        for e in range(2):
-            turn(1, e)
-        for e in range(2):
-            split_turned(terms, 1, e)
-            sigmoid(1, 2 + e)
-        split_turned(terms, 1, 2)
+        first_pair = [tile([P, PACK, FIRST], F32, "first_side%d" % side) for side in range(2)]
+
+        def fetch_high(t):
+            for side in range(2):
+                fetch(first_pair[side][:, t, :], side, PACK + t, 0, FIRST, high_factor)
+
+        for a in range(2):
+            first_product(6, a)
+        sigmoid(4)
+        fetch_high(0)
+        turn(2)
+        sigmoid(5)
+        fetch_high(1)
+        split(1)
+        for a in range(2):
+            first_product(7, a)
+        turn(3)
+        sigmoid(6)
+        fetch_high(2)
+        sigmoid(7)
+        fetch_high(3)
+        for n0 in (0, 2):
+            for t in (2, 3):
+                split(t, n0, n0 + 2)
         for q in range(4):
             nc.sync.dma_start(
-                out=planes_s[0][32 * q : 32 * q + 4, :].bitcast(I32).rearrange("q (a c) -> q a c", a=2),
+                out=planes[32 * q : 32 * q + 4, :].bitcast(I32).rearrange("q (a c) -> q a c", a=2),
                 in_=w2_scales[:, 4 * q : 4 * q + 4, :].rearrange("a q c -> q a c").bitcast(I32),
             )
 
-        overlap_turned(terms, 0, turned[0])
-        z_low = tile([P, DIRECT, PACK], BF16, "z_low", "w1_w111")
-        nc.scalar.copy(z_low[:], halves[:].rearrange("p x (e j) -> p j (x e)", e=2))
-        quantize_z(z_low, 0, 0, 0, DIRECT)
-        for n in (1, 2):
-            overlap_turned(terms, n, turned[n])
+        z_low = [tile([P, width, PACK], BF16, "z_low%d" % n) for n, width in enumerate((2 * P, P, P))]
+        turn_back(0, 0, z_low[0][:, 0:P, :])
+        turn_back(1, 1, z_low[0][:, P : 2 * P, :])
+        turn_back(2, 2, z_low[1][:])
+        turn_back(3, 3, z_low[2][:])
+
+        def overlap(pair, lo, hi, dst):
+            left, right = (side[:, :, lo:hi].rearrange("p t (c i) -> p c t i", i=4) for side in pair)
+            nc.vector.tensor_tensor(dst.rearrange("p (c i) t -> p c t i", i=4), left, right, ALU.min)
 
         out_rows = out.rearrange("(t p) j -> p t j", p=P)
-        for c, (j0, n) in enumerate(CHUNKS):
-            parts = ((0, 256), (256, n)) if n > 256 else ((0, n // 2), (n // 2, n))
-            passes = parts if n > 256 else ((0, n),)
-            pair = [side[:, 0 : PACK * n].rearrange("p (t j) -> p t j", t=PACK) for side in high_sides]
-            y = [psum.tile([P, n], F32, name="bank%d" % SUM_BANKS[c][nt]) for nt in range(N // P)]
+
+        def finish(y, j0, parts, b):
+            width = parts[-1][1] - j0
+            res = tile([P, N // P, width], F32, "res%d" % j0)
             for nt in range(N // P):
-                for lo, hi in passes:
-                    second_product(y[nt], 0, nt, j0, lo, hi)
-            for t in range(PACK):
-                for side in range(2):
-                    for lo, hi in parts if c == 1 and t == PACK - 1 and side == 1 else ((0, n),):
-                        fetch(pair[side][:, t, lo:hi], side, 1, t, j0, lo, hi)
-            z_bf = tile([P, n, PACK], BF16, "z_bf%d" % c, "halves" if c == 0 else None)
-            for lo, hi in parts:
-                left, right = (side[:, :, lo:hi].rearrange("p t (c i) -> p c t i", i=4) for side in pair)
-                nc.vector.tensor_tensor(
-                    z_bf[:, lo:hi, :].rearrange("p (c i) t -> p c t i", i=4), left, right, ALU.min
-                )
-            for lo, hi in parts:
-                quantize_z(z_bf, 1, j0, lo, hi)
-            res = tile([P, N // P, n], F32, "res%d" % c)
-            for nt in range(N // P):
-                for lo, hi in passes:
-                    second_product(y[nt], 1, nt, j0, lo, hi)
+                for lo, hi in parts:
+                    second_product(y[nt], b, nt, j0, lo, hi, 1 - b)
                 nc.scalar.activation(res[:, nt, :], y[nt][:], ACT.Exp, bias=b2_sb[:, nt : nt + 1])
-                nc.sync.dma_start(out=out_rows[:, nt, j0 : j0 + n], in_=res[:, nt, :])
+                nc.sync.dma_start(out=out_rows[:, nt, j0 : j0 + width], in_=res[:, nt, :])
+
+        parts = ((0, 256), (256, FIRST))
+        z_first = tile([P, FIRST, PACK], BF16, "z_first")
+        for lo, hi in parts:
+            overlap(first_pair, lo, hi, z_first[:, lo:hi, :])
+        for lo, hi in parts:
+            quantize_z(z_first[:, lo:hi, :], 1, lo, hi)
+        y_first = [bank([P, FIRST], number) for number in (4, 5, 6, 7)]
+        y_last = [bank([P, LAST], number) for number in (0, 1, 2, 3)]
+        for nt in range(N // P):
+            for lo, hi in parts:
+                second_product(y_first[nt], 1, nt, 0, lo, hi, 1)
+        for part, (lo, hi) in zip(z_low, parts):
+            quantize_z(part[:], 0, lo, hi)
+        finish(y_first, 0, parts, 0)
+        quantize_z(z_low[2][:], 0, FIRST, J)
+        for nt in range(N // P):
+            second_product(y_last[nt], 0, nt, FIRST, FIRST, J, 0)
+
+        halves = ((0, LAST // 2), (LAST // 2, LAST))
+        last_sides = tile([P, 2, PACK, LAST], F32, "last_sides", TERMS_AT)
+        last_pair = [last_sides[:, side] for side in range(2)]
+        for t in range(PACK):
+            fetch(last_pair[0][:, t, :], 0, PACK + t, FIRST, J, high_factor)
+            for lo, hi in halves if t == PACK - 1 else ((0, LAST),):
+                fetch(last_pair[1][:, t, lo:hi], 1, PACK + t, FIRST + lo, FIRST + hi, high_factor)
+        z_last = tile([P, LAST, PACK], BF16, "z_last")
+        for lo, hi in halves:
+            overlap(last_pair, lo, hi, z_last[:, lo:hi, :])
+        for lo, hi in halves:
+            quantize_z(z_last[:, lo:hi, :], 1, FIRST + lo, FIRST + hi)
+        finish(y_last, FIRST, ((FIRST, J),), 1)

@@ -25,11 +25,12 @@ PARK = 64
 LOW_RUN = 512
 FIRST, LAST = 384, 128
 KIB = 1024
-LOW_PIECES = ((0, 0, 1), (1, 0, 2), (0, 1, 2), (0, 2, 4), (1, 2, 4))
+LOW_PIECES = ((0, 0, 1), (1, 0, 1), (1, 1, 3), (0, 1, 3), (0, 3, 4), (1, 3, 4))
 RAW_LOW = 2 * KIB
 RAW_HIGH = 8 * KIB
 HIGH_AT = 9 * RAW_LOW
-TERMS_AT = HIGH_AT + RAW_HIGH + RAW_HIGH // 2
+TERMS_AT = HIGH_AT + 2 * RAW_HIGH
+LATE_AT = TERMS_AT + 17 * KIB
 
 FLOPS = 2 * K * H * S + 2 * H * N * J
 
@@ -134,42 +135,43 @@ def tile_list_join_sketch_cardinality_kernel(
         w1_w, w1_s = {}, {}
         rounded = {}
 
-        def round_low(copy, n, t, count=1):
+        def round_low(copy, n, t, count=1, into=None, at=None):
             a, t0, t1 = LOW_PIECES[n]
-            rounded[t, a] = tile([P, count * PASS], BF16, "w1_bf%d%d" % (t, a))
-            dst = rounded[t, a][:].rearrange("p (c i j) -> p c j i", i=4, j=PACK)
+            rounded[t, a] = tile([P, count * PASS], BF16, "w1_bf%d%d" % (t, a), at)[:] if into is None else into
+            dst = rounded[t, a].rearrange("p (c i j) -> p c j i", i=4, j=PACK)
             columns = low_raw[n][:, :, (t - t0) * P : (t - t0 + count) * P]
             copy(dst, columns.rearrange("p j (c i) -> p c j i", i=4))
 
-        def round_high(a):
-            whole = tile([P, PACK * PASS], BF16, "w1_bf_high%d" % a)
-            dst = whole[:].rearrange("p (t m j) -> p m j t", t=PACK, j=PACK)
-            nc.scalar.copy(dst, high_raw[a][:].rearrange("p j (m t) -> p m j t", t=PACK))
-            return whole
+        high_rounded = [tile([P, PACK * PASS], BF16, "w1_bf_high%d" % a) for a in range(2)]
 
-        def quantize_w1(source, a, t0, count):
-            words = tile([P, count * P], U32, "w1_w%d%d" % (a, t0))
-            scales = tile([P, count * P], U8, "w1_s%d%d" % (a, t0))
+        def round_high(a, lo=0, hi=P):
+            dst = high_rounded[a][:].rearrange("p (t m j) -> p m j t", t=PACK, j=PACK)
+            nc.scalar.copy(dst[:, lo:hi], high_raw[a][:].rearrange("p j (m t) -> p m j t", t=PACK)[:, lo:hi])
+
+        def quantize_w1(source, keys):
+            words = tile([P, len(keys) * P], U32, "w1_w%d%d" % keys[0])
+            scales = tile([P, len(keys) * P], U8, "w1_s%d%d" % keys[0])
             nc.vector.quantize_mx(out=words[:].bitcast(FP8X4), scales=scales[:], in_=source)
-            for e in range(count):
+            for e, key in enumerate(keys):
                 cols = slice(e * P, (e + 1) * P)
-                w1_w[t0 + e, a], w1_s[t0 + e, a] = words[:, cols], scales[:, cols]
+                w1_w[key], w1_s[key] = words[:, cols], scales[:, cols]
 
-        def quantize_low(t, a, count=1):
-            quantize_w1(rounded[t, a][:], a, t, count)
+        def quantize_low(t, a):
+            quantize_w1(rounded[t, a], [(t, a)])
 
         h = {}
         acc = {}
-        sum_banks = ((0, 1, 6), (2, 3), (4, 5), (6, 7), (4, 5), (6, 7), (0, 1), (2, 3))
+        sum_banks = ((0, 1, 6), (2, 3), (4, 5), (6, 7), (4, 5), (6, 7), (2, 3), (6, 7))
         opening = (0, 1, 0, 0, 0, 0, 0, 0)
 
         def spans(t):
             edges = (0, BANK, 768, S) if len(sum_banks[t]) == 3 else (0, BANK, S)
             return list(zip(edges, edges[1:]))
 
-        def first_product(t, a):
-            for (c0, c1), number in zip(spans(t), sum_banks[t]):
-                if a == opening[t]:
+        def first_product(t, a, chosen=slice(None), opens=None):
+            opens = a == opening[t] if opens is None else opens
+            for (c0, c1), number in list(zip(spans(t), sum_banks[t]))[chosen]:
+                if opens:
                     acc[t, c0] = bank([P, c1 - c0], number)
                 for lo, hi, picked in v_w[a]:
                     first, last = max(lo, c0), min(hi, c1)
@@ -180,8 +182,8 @@ def tile_list_join_sketch_cardinality_kernel(
                             lhsT_scale=w1_s[t, a],
                             rhs=picked[:, first - lo : last - lo].bitcast(FP8X4),
                             rhs_scale=planes[4 * a : P, first:last],
-                            start=(a == opening[t] and first == c0),
-                            stop=(a != opening[t] and last == c1),
+                            start=(opens and first == c0),
+                            stop=(not opens and last == c1),
                         )
 
         def sigmoid(t, at=None):
@@ -193,17 +195,13 @@ def tile_list_join_sketch_cardinality_kernel(
             entries = pos_sb[side][:, lo // LIST_ROWS : hi // LIST_ROWS]
             nc.vector.tensor_tensor(dst, h[t][:].indirect(entries), factor[:, t % PACK, 0 : hi - lo], ALU.mult)
 
-        low_sides = {}
+        low_runs = {}
 
-        def fetch_low(t, side, dst):
-            low_sides[t, side] = dst
-            for lo in range(0, J, LOW_RUN):
-                fetch(dst[:, lo : lo + LOW_RUN], side, t, lo, lo + LOW_RUN, low_factor[side])
-
-        def fetch_both(t, at=None):
-            sides = tile([P, 2, J], F32, "low_sides%d" % t, at)
-            for side in range(2):
-                fetch_low(t, side, sides[:, side, :])
+        def fetch_low(t, side, lo=0, hi=J, at=None):
+            run = tile([P, hi - lo], F32, "low_run%d%d_%d" % (t, side, lo), at)
+            fetch(run[:], side, t, lo, hi, low_factor[side])
+            for n in range(lo // P, hi // P):
+                low_runs[t, side, n] = run[:, n * P - lo : (n + 1) * P - lo]
 
         def add_turned(dst, first, second):
             nc.tensor.matmul(dst, first, identity[:], start=True, stop=False, is_transpose=True)
@@ -212,10 +210,10 @@ def tile_list_join_sketch_cardinality_kernel(
         turned = {}
 
         def turn(t):
-            first = 2 * t
+            first = (2, 0, 0, 6)[t]
             turned[t] = [bank([P, PACK, P], first + k) for k in range(2)]
             for n in range(PACK):
-                left, right = (low_sides[t, side][:, n * P : (n + 1) * P] for side in range(2))
+                left, right = (low_runs[t, side, n] for side in range(2))
                 add_turned(turned[t][0][:, n, :], left, right)
                 nc.tensor.transpose(turned[t][1][:, n, :], right, identity[:])
 
@@ -255,88 +253,95 @@ def tile_list_join_sketch_cardinality_kernel(
         gather_words(0, 0, S)
         round_low(nc.scalar.copy, 0, 0)
         quantize_low(0, 0)
-        first_product(0, 0)
-        gather_words(1, 0, 768)
+        gather_words(1, 0, BANK)
         round_low(nc.scalar.copy, 1, 0)
-        round_low(nc.scalar.copy, 1, 1)
         quantize_low(0, 1)
-        quantize_low(1, 1)
-        gather_words(1, 768, S, low_at[1])
-        first_product(0, 1)
+        gather_words(1, BANK, 768, low_at[1])
+        gather_words(1, 768, S, low_at[1] + KIB)
+        for a, n, opens in ((0, 0, True), (0, 2, True), (1, 0, False), (0, 1, True), (1, 1, False), (1, 2, False)):
+            first_product(0, a, slice(n, n + 1), opens)
+        middle = tile([P, 2 * PASS], BF16, "w1_bf_middle")
+        round_low(nc.scalar.copy, 2, 1, 2, into=middle[:])
+        quantize_w1(middle[:], [(1, 1), (2, 1)])
         first_product(1, 1)
-        round_low(nc.scalar.copy, 2, 1)
-        round_low(nc.vector.tensor_copy, 3, 2, 2)
+        round_low(nc.vector.tensor_copy, 3, 1, at=LATE_AT + KIB)
+        round_low(nc.vector.tensor_copy, 3, 2)
         quantize_low(1, 0)
         first_product(1, 0)
-        quantize_low(2, 0, 2)
-        first_product(2, 0)
-        sigmoid(0)
-        first_product(3, 0)
-        fetch_low(0, 0, tile([P, J], F32, "low_left0", low_at[3])[:])
-        round_low(nc.scalar.copy, 4, 2, 2)
-        quantize_low(2, 1, 2)
-        first_product(2, 1)
-        first_product(3, 1)
-        fetch_low(0, 1, tile([P, J], F32, "low_right0", low_at[4])[:])
+        quantize_low(2, 0)
+        for a in range(2):
+            first_product(2, a)
+        sigmoid(0, low_at[2])
+        fetch_low(0, 0, at=LATE_AT - KIB // 2)
+        fetch_low(0, 1, at=LATE_AT + KIB + KIB // 2)
+        sigmoid(1)
+        fourth = tile([P, 2 * PASS], BF16, "w1_bf_fourth")
+        for a in range(2):
+            round_low(nc.scalar.copy, 4 + a, 3, into=fourth[:, a * PASS : (a + 1) * PASS])
+        quantize_w1(fourth[:], [(3, 0), (3, 1)])
+        for a in range(2):
+            first_product(3, a)
         turn(0)
-        sigmoid(1, low_at[4] + RAW_LOW)
-        fetch_both(1)
+        fetch_low(1, 0, at=low_at[5] - KIB)
+        fetch_low(1, 1, at=low_at[5] + KIB)
         turn(1)
         sigmoid(2)
-        fetch_low(2, 0, tile([P, J], F32, "low_left2")[:])
-        whole = round_high(0)
-        quantize_w1(whole[:], 0, PACK, PACK)
-        fetch_low(2, 1, tile([P, J], F32, "low_right2", HIGH_AT + RAW_HIGH // 2)[:])
-        sigmoid(3, HIGH_AT)
+        fetch_low(2, 0)
+        round_high(0)
+        quantize_w1(high_rounded[0][:], [(PACK + t, 0) for t in range(PACK)])
+        fetch_low(2, 1, at=HIGH_AT)
+        sigmoid(3)
         for t in (4, 5):
             first_product(t, 0)
-        fetch_low(3, 0, tile([P, J], F32, "low_left3")[:])
-        whole = round_high(1)
-        quantize_w1(whole[:, 0:PASS], 1, PACK, 1)
+        fetch_low(3, 1, 0, J // 2)
+        round_high(1)
+        whole = high_rounded[1]
+        quantize_w1(whole[:, 0:PASS], [(PACK, 1)])
         first_product(4, 1)
-        right = tile([P, J], F32, "low_right3", HIGH_AT + RAW_HIGH)
-        low_sides[3, 1] = right[:]
-        fetch(right[:, 0 : J // 2], 1, 3, 0, J // 2, low_factor[1])
-        quantize_w1(whole[:, PASS : PACK * PASS], 1, PACK + 1, PACK - 1)
+        fetch_low(3, 1, J // 2, J, HIGH_AT + RAW_HIGH)
+        quantize_w1(whole[:, PASS : PACK * PASS], [(PACK + t, 1) for t in range(1, PACK)])
         first_product(5, 1)
-        fetch(right[:, J // 2 : J], 1, 3, J // 2, J, low_factor[1])
+        fetch_low(3, 0, at=HIGH_AT + RAW_HIGH + KIB)
         split(0)
 
         first_pair = [tile([P, PACK, FIRST], F32, "first_side%d" % side) for side in range(2)]
 
+        last_left = tile([P, PACK, LAST], F32, "last_left")
+
         def fetch_high(t):
-            for side in range(2):
-                fetch(first_pair[side][:, t, :], side, PACK + t, 0, FIRST, high_factor)
+            fetch(first_pair[0][:, t, :], 0, PACK + t, 0, FIRST, high_factor)
+            fetch(last_left[:, t, :], 0, PACK + t, FIRST, J, high_factor)
+            fetch(first_pair[1][:, t, :], 1, PACK + t, 0, FIRST, high_factor)
 
         for a in range(2):
             first_product(6, a)
         sigmoid(4)
         fetch_high(0)
-        turn(2)
         sigmoid(5)
         fetch_high(1)
+        turn(3)
         split(1)
+        turn(2)
+        split(3)
         for a in range(2):
             first_product(7, a)
-        turn(3)
         sigmoid(6)
         fetch_high(2)
+        split(2, 0, 2)
         sigmoid(7)
         fetch_high(3)
-        for n0 in (0, 2):
-            for t in (2, 3):
-                split(t, n0, n0 + 2)
+        split(2, 2, PACK)
         for q in range(4):
             nc.sync.dma_start(
                 out=planes[32 * q : 32 * q + 4, :].bitcast(I32).rearrange("q (a c) -> q a c", a=2),
                 in_=w2_scales[:, 4 * q : 4 * q + 4, :].rearrange("a q c -> q a c").bitcast(I32),
             )
 
-        z_low = [tile([P, width, PACK], BF16, "z_low%d" % n) for n, width in enumerate((2 * P, P, P))]
-        turn_back(0, 0, z_low[0][:, 0:P, :])
-        turn_back(1, 1, z_low[0][:, P : 2 * P, :])
-        turn_back(2, 2, z_low[1][:])
-        turn_back(3, 3, z_low[2][:])
+        z_low = [tile([P, width, PACK], BF16, "z_low%d" % n) for n, width in enumerate((FIRST, LAST))]
+        turn_back(0, 4, z_low[0][:, 0:P, :])
+        turn_back(1, 5, z_low[0][:, P : 2 * P, :])
+        turn_back(2, 2, z_low[0][:, 2 * P : FIRST, :])
+        turn_back(3, 3, z_low[1][:])
 
         def overlap(pair, lo, hi, dst):
             left, right = (side[:, :, lo:hi].rearrange("p t (c i) -> p c t i", i=4) for side in pair)
@@ -351,31 +356,29 @@ def tile_list_join_sketch_cardinality_kernel(
                 for lo, hi in parts:
                     second_product(y[nt], b, nt, j0, lo, hi, 1 - b)
                 nc.scalar.activation(res[:, nt, :], y[nt][:], ACT.Exp, bias=b2_sb[:, nt : nt + 1])
-                nc.sync.dma_start(out=out_rows[:, nt, j0 : j0 + width], in_=res[:, nt, :])
+                queue = nc.scalar if j0 + width == J and nt == N // P - 1 else nc.sync
+                queue.dma_start(out=out_rows[:, nt, j0 : j0 + width], in_=res[:, nt, :])
 
         parts = ((0, 256), (256, FIRST))
-        z_first = tile([P, FIRST, PACK], BF16, "z_first")
+        y_first = [bank([P, FIRST], number) for number in (0, 1, 6, 7)]
+        quantize_z(z_low[0][:], 0, 0, FIRST)
+        for nt in range(N // P):
+            for lo, hi in parts:
+                second_product(y_first[nt], 0, nt, 0, lo, hi, 0)
+        z_first = tile([P, FIRST, PACK], BF16, "z_first", TERMS_AT + 4 * KIB)
         for lo, hi in parts:
             overlap(first_pair, lo, hi, z_first[:, lo:hi, :])
         for lo, hi in parts:
             quantize_z(z_first[:, lo:hi, :], 1, lo, hi)
-        y_first = [bank([P, FIRST], number) for number in (4, 5, 6, 7)]
-        y_last = [bank([P, LAST], number) for number in (0, 1, 2, 3)]
-        for nt in range(N // P):
-            for lo, hi in parts:
-                second_product(y_first[nt], 1, nt, 0, lo, hi, 1)
-        for part, (lo, hi) in zip(z_low, parts):
-            quantize_z(part[:], 0, lo, hi)
-        finish(y_first, 0, parts, 0)
-        quantize_z(z_low[2][:], 0, FIRST, J)
+        y_last = [bank([P, LAST], number) for number in (4, 5, 2, 3)]
+        finish(y_first, 0, parts, 1)
+        quantize_z(z_low[1][:], 0, FIRST, J)
         for nt in range(N // P):
             second_product(y_last[nt], 0, nt, FIRST, FIRST, J, 0)
 
         halves = ((0, LAST // 2), (LAST // 2, LAST))
-        last_sides = tile([P, 2, PACK, LAST], F32, "last_sides", TERMS_AT)
-        last_pair = [last_sides[:, side] for side in range(2)]
+        last_pair = [last_left, tile([P, PACK, LAST], F32, "last_right", TERMS_AT)]
         for t in range(PACK):
-            fetch(last_pair[0][:, t, :], 0, PACK + t, FIRST, J, high_factor)
             for lo, hi in halves if t == PACK - 1 else ((0, LAST),):
                 fetch(last_pair[1][:, t, lo:hi], 1, PACK + t, FIRST + lo, FIRST + hi, high_factor)
         z_last = tile([P, LAST, PACK], BF16, "z_last")

@@ -356,8 +356,7 @@ def tile_list_join_sketch_cardinality_kernel(
                 for lo, hi in parts:
                     second_product(y[nt], b, nt, j0, lo, hi, 1 - b)
                 nc.scalar.activation(res[:, nt, :], y[nt][:], ACT.Exp, bias=b2_sb[:, nt : nt + 1])
-                queue = nc.scalar if j0 + width == J and nt == N // P - 1 else nc.sync
-                queue.dma_start(out=out_rows[:, nt, j0 : j0 + width], in_=res[:, nt, :])
+                nc.sync.dma_start(out=out_rows[:, nt, j0 : j0 + width], in_=res[:, nt, :])
 
         parts = ((0, 256), (256, FIRST))
         y_first = [bank([P, FIRST], number) for number in (0, 1, 6, 7)]

from contextlib import ExitStack

import concourse.mybir as mybir
from concourse.masks import make_identity

K, H, N, T, S, J = 1024, 1024, 512, 2048, 1024, 512

F32 = mybir.dt.float32
BF16 = mybir.dt.bfloat16
I32 = mybir.dt.int32
U32 = mybir.dt.uint32
U16 = mybir.dt.uint16
U8 = mybir.dt.uint8
FP8X4 = mybir.dt.float8_e4m3fn_x4
FP4X4 = mybir.dt.float4_e2m1fn_x4
ACT = mybir.ActivationFunctionType
ALU = mybir.AluOpType

P = 128
PACK = 4
PASS = P * PACK
BANK = 512
LIST_ROWS = 16
PARK = 64
LOW_RUN = 512
FIRST, LAST = 384, 128
KIB = 1024
LOW_PIECES = ((0, 0, 1), (1, 0, 1), (1, 1, 3), (0, 1, 3), (0, 3, 4), (1, 3, 4))
RAW_LOW = 2 * KIB
RAW_HIGH = 8 * KIB
HIGH_AT = 9 * RAW_LOW
TERMS_AT = HIGH_AT + 2 * RAW_HIGH
LATE_AT = TERMS_AT + 17 * KIB

FLOPS = 2 * K * H * S + 2 * H * N * J


def tile_list_join_sketch_cardinality_kernel(
    tc, tab_words, tab_scales, w1, g, w2_words, w2_scales, b2, offs, pos1, pos2, out
):
    nc = tc.nc
    with ExitStack() as ctx:
        keep = ctx.enter_context(tc.tile_pool(name="keep", bufs=1))
        shared = ctx.enter_context(tc.tile_pool(name="shared", bufs=1))
        psum = ctx.enter_context(tc.psum_pool(name="psum", bufs=1))

        def tile(shape, dtype, name, at=None):
            if at is not None:
                return shared.tile(shape, dtype, name=name, offset=at, align_bytes=64)
            return keep.tile(shape, dtype, name=name, align_bytes=64)

        def bank(shape, number):
            return psum.tile(shape, F32, name="bank%d" % number)

        offs_sb = keep.tile([P, S // LIST_ROWS], U16, name="offs_sb")
        pos_sb = [keep.tile([P, J // LIST_ROWS], U16, name="pos%d_sb" % side) for side in range(2)]
        tab_w = [tile([P, T], I32, "tab_w%d" % a) for a in range(2)]
        tab_s = tile([P, T // 4], I32, "tab_s")
        g_low = tile([P, PACK], F32, "g_low")
        g_high = tile([P, PACK], F32, "g_high")

        nc.vector.memset(tab_s[0:PARK, :], 0)
        nc.vector.memset(tab_s[PARK + 32 : P, :], 0)

        identity = tile([P, P], F32, "identity")
        make_identity(nc, identity[:])

        def load_w1(a, c0, width, at):
            raw = tile([P, PACK, width], F32, "w1_raw%d_%d" % (a, c0), at)
            rows = w1[a * PASS : (a + 1) * PASS, c0 : c0 + width]
            nc.sync.dma_start(out=raw[:], in_=rows.rearrange("(p j) c -> p j c", j=PACK))
            return raw

        low_raw = {}
        low_at = [RAW_LOW * sum(t1 - t0 for a, t0, t1 in LOW_PIECES[:n]) for n in range(len(LOW_PIECES))]

        def load_low(n):
            a, t0, t1 = LOW_PIECES[n]
            raw = load_w1(a, t0 * P, (t1 - t0) * P, low_at[n])
            low_raw[n] = raw

        nc.sync.dma_start(offs_sb[:], offs)
        nc.scalar.dma_start(out=g_high[:], in_=g[PASS:H].rearrange("(p t) -> p t", t=PACK))
        with nc.allow_non_contiguous_dma(reason="one factor a partition and tile"):
            nc.scalar.dma_start(out=g_low[:], in_=g[0:PASS].rearrange("(t p) -> p t", p=P))
        nc.sync.dma_start(out=tab_s[PARK : PARK + 32, :], in_=tab_scales.bitcast(I32).rearrange("a q c -> q a c"))
        words = [tab_words[a].rearrange("p n t -> p (n t)").bitcast(I32) for a in range(2)]
        nc.sync.dma_start(out=tab_w[0][:], in_=words[0])
        nc.sync.dma_start(pos_sb[0][:], pos1)
        nc.sync.dma_start(pos_sb[1][:], pos2)
        load_low(0)
        nc.sync.dma_start(out=tab_w[1][:], in_=words[1])
        load_low(1)

        warm = tile([P, 2], F32, "warm")
        nc.vector.memset(warm[:, 0:1], 0.0)
        nc.scalar.activation(warm[:, 1:2], warm[:, 0:1], ACT.Sigmoid)

        def spread(rows, width, sign, name):
            wide = tile([P, PACK, width], F32, name)
            nc.scalar.activation(wide[:], rows[:].unsqueeze(2).to_broadcast([P, PACK, width]), ACT.Copy, scale=sign)
            return wide

        high_factor = spread(g_high, FIRST, 1.0, "high_factor")
        minus_low = tile([P, PACK, LOW_RUN], F32, "minus_low")
        nc.gpsimd.tensor_scalar(
            minus_low[:], g_low[:].unsqueeze(2).to_broadcast([P, PACK, LOW_RUN]), -1.0, 0.0, ALU.mult, ALU.add
        )
        low_factor = [spread(g_low, LOW_RUN, 1.0, "plus_low"), minus_low]

        v_s = tile([P, S], U8, "v_s")
        nc.vector.tensor_copy(v_s[:], tab_s[:].bitcast(U8).indirect(offs_sb[:]))
        planes = tile([P, S], U8, "planes")
        for r in range(4):
            nc.sync.dma_start(
                out=planes[r:P:4, :].bitcast(I32), in_=v_s[PARK + 2 * r : PARK + 2 * r + 32, :].bitcast(I32)
            )
        for n in range(2, len(LOW_PIECES)):
            load_low(n)
        high_raw = [load_w1(a, PASS, PASS, HIGH_AT + a * RAW_HIGH) for a in range(2)]
        w2_w = tile([P, 2, 2 * N], U8, "w2_w")
        nc.sync.dma_start(out=w2_w[:].bitcast(I32), in_=w2_words.rearrange("a p c -> p a c").bitcast(I32))
        b2_sb = tile([P, N // P], F32, "b2_sb")
        with nc.allow_non_contiguous_dma(reason="one bias value a partition"):
            nc.sync.dma_start(out=b2_sb[:], in_=b2.rearrange("(t p) -> p t", p=P))

        v_w = {0: [], 1: []}

        def gather_words(a, lo, hi, at=None):
            picked = tile([P, hi - lo], U32, "v_w%d_%d" % (a, lo), at)
            entries = offs_sb[:, lo // LIST_ROWS : hi // LIST_ROWS]
            nc.vector.tensor_copy(picked[:], tab_w[a][:].bitcast(U32).indirect(entries))
            v_w[a].append((lo, hi, picked))

        w1_w, w1_s = {}, {}
        rounded = {}

        def round_low(copy, n, t, count=1, into=None, at=None):
            a, t0, t1 = LOW_PIECES[n]
            rounded[t, a] = tile([P, count * PASS], BF16, "w1_bf%d%d" % (t, a), at)[:] if into is None else into
            dst = rounded[t, a].rearrange("p (c i j) -> p c j i", i=4, j=PACK)
            columns = low_raw[n][:, :, (t - t0) * P : (t - t0 + count) * P]
            copy(dst, columns.rearrange("p j (c i) -> p c j i", i=4))

        high_rounded = [tile([P, PACK * PASS], BF16, "w1_bf_high%d" % a) for a in range(2)]

        def round_high(a, lo=0, hi=P):
            dst = high_rounded[a][:].rearrange("p (t m j) -> p m j t", t=PACK, j=PACK)
            nc.scalar.copy(dst[:, lo:hi], high_raw[a][:].rearrange("p j (m t) -> p m j t", t=PACK)[:, lo:hi])

        def quantize_w1(source, keys):
            words = tile([P, len(keys) * P], U32, "w1_w%d%d" % keys[0])
            scales = tile([P, len(keys) * P], U8, "w1_s%d%d" % keys[0])
            nc.vector.quantize_mx(out=words[:].bitcast(FP8X4), scales=scales[:], in_=source)
            for e, key in enumerate(keys):
                cols = slice(e * P, (e + 1) * P)
                w1_w[key], w1_s[key] = words[:, cols], scales[:, cols]

        def quantize_low(t, a):
            quantize_w1(rounded[t, a], [(t, a)])

        h = {}
        acc = {}
        sum_banks = ((0, 1, 6), (2, 3), (4, 5), (6, 7), (4, 5), (6, 7), (2, 3), (6, 7))
        opening = (0, 1, 0, 0, 0, 0, 0, 0)

        def spans(t):
            edges = (0, BANK, 768, S) if len(sum_banks[t]) == 3 else (0, BANK, S)
            return list(zip(edges, edges[1:]))

        def first_product(t, a, chosen=slice(None), opens=None):
            opens = a == opening[t] if opens is None else opens
            for (c0, c1), number in list(zip(spans(t), sum_banks[t]))[chosen]:
                if opens:
                    acc[t, c0] = bank([P, c1 - c0], number)
                for lo, hi, picked in v_w[a]:
                    first, last = max(lo, c0), min(hi, c1)
                    if first < last:
                        nc.tensor.matmul_mx(
                            out=acc[t, c0][:, first - c0 : last - c0],
                            lhsT=w1_w[t, a].bitcast(FP8X4),
                            lhsT_scale=w1_s[t, a],
                            rhs=picked[:, first - lo : last - lo].bitcast(FP8X4),
                            rhs_scale=planes[4 * a : P, first:last],
                            start=(opens and first == c0),
                            stop=(not opens and last == c1),
                        )

        def sigmoid(t, at=None):
            h[t] = tile([P, S], F32, "h%d" % t, at)
            for c0, c1 in spans(t):
                nc.scalar.activation(h[t][:, c0:c1], acc[t, c0][:], ACT.Sigmoid)

        def fetch(dst, side, t, lo, hi, factor):
            entries = pos_sb[side][:, lo // LIST_ROWS : hi // LIST_ROWS]
            nc.vector.tensor_tensor(dst, h[t][:].indirect(entries), factor[:, t % PACK, 0 : hi - lo], ALU.mult)

        low_runs = {}

        def fetch_low(t, side, lo=0, hi=J, at=None):
            run = tile([P, hi - lo], F32, "low_run%d%d_%d" % (t, side, lo), at)
            fetch(run[:], side, t, lo, hi, low_factor[side])
            for n in range(lo // P, hi // P):
                low_runs[t, side, n] = run[:, n * P - lo : (n + 1) * P - lo]

        def add_turned(dst, first, second):
            nc.tensor.matmul(dst, first, identity[:], start=True, stop=False, is_transpose=True)
            nc.tensor.matmul(dst, second, identity[:], start=False, stop=True, is_transpose=True)

        turned = {}

        def turn(t):
            first = (2, 0, 0, 6)[t]
            turned[t] = [bank([P, PACK, P], first + k) for k in range(2)]
            for n in range(PACK):
                left, right = (low_runs[t, side, n] for side in range(2))
                add_turned(turned[t][0][:, n, :], left, right)
                nc.tensor.transpose(turned[t][1][:, n, :], right, identity[:])

        terms = tile([P, 2, PACK, PACK, P], F32, "terms", TERMS_AT)

        def split(t, n0=0, n1=PACK):
            dealt = terms[:, :, n0:n1, :, 32 * t : 32 * (t + 1)]
            source = [turned[t][k][:, n0:n1, :].rearrange("j n (m i) -> j n i m", i=PACK) for k in range(2)]
            nc.scalar.activation(dealt[:, 0], source[0], ACT.Relu, scale=-1.0)
            nc.scalar.copy(dealt[:, 1], source[1])

        z_w = [tile([P, J], U32, "z_w%d" % b) for b in range(2)]
        z_s = [tile([P, J], U8, "z_s%d" % b) for b in range(2)]

        def quantize_z(source, b, lo, hi):
            nc.vector.quantize_mx(
                out=z_w[b][:, lo:hi].bitcast(FP8X4), scales=z_s[b][:, lo:hi], in_=source.rearrange("p j t -> p (j t)")
            )

        def turn_back(n, number, dst):
            back = bank([P, PACK, P], number)
            for i in range(PACK):
                add_turned(back[:, i, :], terms[:, 0, n, i, :], terms[:, 1, n, i, :])
            nc.scalar.activation(dst, back[:].rearrange("p i j -> p j i"), ACT.Copy, scale=-1.0)

        def second_product(y, b, nt, j0, lo, hi, opening_half):
            nc.tensor.matmul_mx(
                out=y[:, lo - j0 : hi - j0],
                lhsT=w2_w[:, b, 2 * nt * P : 2 * (nt + 1) * P].bitcast(FP4X4),
                lhsT_scale=planes[:, b * N + nt * P : b * N + (nt + 1) * P],
                rhs=z_w[b][:, lo:hi].bitcast(FP8X4),
                rhs_scale=z_s[b][:, lo:hi],
                start=(b == opening_half and lo == j0),
                stop=(b != opening_half and hi - j0 == y.shape[1]),
            )

        gather_words(0, 0, S)
        round_low(nc.scalar.copy, 0, 0)
        quantize_low(0, 0)
        gather_words(1, 0, BANK)
        round_low(nc.scalar.copy, 1, 0)
        quantize_low(0, 1)
        gather_words(1, BANK, 768, low_at[1])
        gather_words(1, 768, S, low_at[1] + KIB)
        for a, n, opens in ((0, 0, True), (0, 2, True), (1, 0, False), (0, 1, True), (1, 1, False), (1, 2, False)):
            first_product(0, a, slice(n, n + 1), opens)
        middle = tile([P, 2 * PASS], BF16, "w1_bf_middle")
        round_low(nc.scalar.copy, 2, 1, 2, into=middle[:])
        quantize_w1(middle[:], [(1, 1), (2, 1)])
        first_product(1, 1)
        round_low(nc.vector.tensor_copy, 3, 1, at=LATE_AT + KIB)
        round_low(nc.vector.tensor_copy, 3, 2)
        quantize_low(1, 0)
        first_product(1, 0)
        quantize_low(2, 0)
        for a in range(2):
            first_product(2, a)
        sigmoid(0, low_at[2])
        fetch_low(0, 0, at=LATE_AT - KIB // 2)
        fetch_low(0, 1, at=LATE_AT + KIB + KIB // 2)
        sigmoid(1)
        fourth = tile([P, 2 * PASS], BF16, "w1_bf_fourth")
        for a in range(2):
            round_low(nc.scalar.copy, 4 + a, 3, into=fourth[:, a * PASS : (a + 1) * PASS])
        quantize_w1(fourth[:], [(3, 0), (3, 1)])
        for a in range(2):
            first_product(3, a)
        turn(0)
        fetch_low(1, 0, at=low_at[5] - KIB)
        fetch_low(1, 1, at=low_at[5] + KIB)
        turn(1)
        sigmoid(2)
        fetch_low(2, 0)
        round_high(0)
        quantize_w1(high_rounded[0][:], [(PACK + t, 0) for t in range(PACK)])
        fetch_low(2, 1, at=HIGH_AT)
        sigmoid(3)
        for t in (4, 5):
            first_product(t, 0)
        fetch_low(3, 1, 0, J // 2)
        round_high(1)
        whole = high_rounded[1]
        quantize_w1(whole[:, 0:PASS], [(PACK, 1)])
        first_product(4, 1)
        fetch_low(3, 1, J // 2, J, HIGH_AT + RAW_HIGH)
        quantize_w1(whole[:, PASS : PACK * PASS], [(PACK + t, 1) for t in range(1, PACK)])
        first_product(5, 1)
        fetch_low(3, 0, at=HIGH_AT + RAW_HIGH + KIB)
        split(0)

        first_pair = [tile([P, PACK, FIRST], F32, "first_side%d" % side) for side in range(2)]

        last_left = tile([P, PACK, LAST], F32, "last_left")

        def fetch_high(t):
            fetch(first_pair[0][:, t, :], 0, PACK + t, 0, FIRST, high_factor)
            fetch(last_left[:, t, :], 0, PACK + t, FIRST, J, high_factor)
            fetch(first_pair[1][:, t, :], 1, PACK + t, 0, FIRST, high_factor)

        for a in range(2):
            first_product(6, a)
        sigmoid(4)
        fetch_high(0)
        sigmoid(5)
        fetch_high(1)
        turn(3)
        split(1)
        turn(2)
        split(3)
        for a in range(2):
            first_product(7, a)
        sigmoid(6)
        fetch_high(2)
        split(2, 0, 2)
        sigmoid(7)
        fetch_high(3)
        split(2, 2, PACK)
        for q in range(4):
            nc.sync.dma_start(
                out=planes[32 * q : 32 * q + 4, :].bitcast(I32).rearrange("q (a c) -> q a c", a=2),
                in_=w2_scales[:, 4 * q : 4 * q + 4, :].rearrange("a q c -> q a c").bitcast(I32),
            )

        z_low = [tile([P, width, PACK], BF16, "z_low%d" % n) for n, width in enumerate((FIRST, LAST))]
        turn_back(0, 4, z_low[0][:, 0:P, :])
        turn_back(1, 5, z_low[0][:, P : 2 * P, :])
        turn_back(2, 2, z_low[0][:, 2 * P : FIRST, :])
        turn_back(3, 3, z_low[1][:])

        def overlap(pair, lo, hi, dst):
            left, right = (side[:, :, lo:hi].rearrange("p t (c i) -> p c t i", i=4) for side in pair)
            nc.vector.tensor_tensor(dst.rearrange("p (c i) t -> p c t i", i=4), left, right, ALU.min)

        out_rows = out.rearrange("(t p) j -> p t j", p=P)

        def finish(y, j0, parts, b):
            width = parts[-1][1] - j0
            res = tile([P, N // P, width], F32, "res%d" % j0)
            for nt in range(N // P):
                for lo, hi in parts:
                    second_product(y[nt], b, nt, j0, lo, hi, 1 - b)
                nc.scalar.activation(res[:, nt, :], y[nt][:], ACT.Exp, bias=b2_sb[:, nt : nt + 1])
                nc.sync.dma_start(out=out_rows[:, nt, j0 : j0 + width], in_=res[:, nt, :])

        parts = ((0, 256), (256, FIRST))
        y_first = [bank([P, FIRST], number) for number in (0, 1, 6, 7)]
        quantize_z(z_low[0][:], 0, 0, FIRST)
        for nt in range(N // P):
            for lo, hi in parts:
                second_product(y_first[nt], 0, nt, 0, lo, hi, 0)
        z_first = tile([P, FIRST, PACK], BF16, "z_first", TERMS_AT + 4 * KIB)
        for lo, hi in parts:
            overlap(first_pair, lo, hi, z_first[:, lo:hi, :])
        for lo, hi in parts:
            quantize_z(z_first[:, lo:hi, :], 1, lo, hi)
        y_last = [bank([P, LAST], number) for number in (4, 5, 2, 3)]
        finish(y_first, 0, parts, 1)
        quantize_z(z_low[1][:], 0, FIRST, J)
        for nt in range(N // P):
            second_product(y_last[nt], 0, nt, FIRST, FIRST, J, 0)

        halves = ((0, LAST // 2), (LAST // 2, LAST))
        last_pair = [last_left, tile([P, PACK, LAST], F32, "last_right", TERMS_AT)]
        for t in range(PACK):
            for lo, hi in halves if t == PACK - 1 else ((0, LAST),):
                fetch(last_pair[1][:, t, lo:hi], 1, PACK + t, FIRST + lo, FIRST + hi, high_factor)
        z_last = tile([P, LAST, PACK], BF16, "z_last")
        for lo, hi in halves:
            overlap(last_pair, lo, hi, z_last[:, lo:hi, :])
        for lo, hi in halves:
            quantize_z(z_last[:, lo:hi, :], 1, FIRST + lo, FIRST + hi)
        finish(y_last, FIRST, ((FIRST, J),), 1)
